import numpy as np
import ml_dtypes


def mxq(x, axis, fmt="e4m3"):
    dtype, down = {"e4m3": (ml_dtypes.float8_e4m3fn, 7), "e5m2": (ml_dtypes.float8_e5m2, 14)}[fmt]
    v = np.moveaxis(np.asarray(x, np.float32).astype(ml_dtypes.bfloat16).astype(np.float64), axis, -1)
    blocks = v.reshape(v.shape[:-1] + (-1, 32))
    amax = np.abs(blocks).max(-1, keepdims=True)
    byte = np.maximum(np.where(amax > 0, np.frexp(amax)[1] - 1 + 127, 0) - down, 1)
    scale = np.exp2(byte - 127.0)
    codes = (blocks / scale).astype(np.float32).astype(dtype).astype(np.float64)
    return np.moveaxis((codes * scale).reshape(v.shape), -1, axis)


WIDE = False


def mx_kscale(k):
    if not WIDE:
        return np.ones(k)
    levels = np.array([10, -10, 5, -5, 0])
    if k % 512:
        return np.exp2(np.random.permutation(np.resize(levels, k // 32))).repeat(32)
    a = np.empty((k // 512, 16))
    for p in range(k // 512):
        a[p, :8] = np.random.permutation(np.resize(levels, 8))
        for g in range(8):
            far = levels[np.abs(levels - a[p, g]) >= 10]
            a[p, g + 8] = far[np.random.randint(len(far))]
    return np.exp2(a.ravel()).repeat(32)


def f64(x):
    return np.asarray(x).astype(np.float64)


def striped(idx):
    return np.tile(idx.reshape(-1, 16).T, (8, 1)).astype(np.uint16)


def unstriped(offs):
    return offs[:16].T.reshape(-1).astype(np.int64)


E2M1 = np.array([0.0, 0.5, 1.0, 1.5, 2.0, 3.0, 4.0, 6.0, -0.0, -0.5, -1.0, -1.5, -2.0, -3.0, -4.0, -6.0])


def pack_fp4(w):
    k, n = w.shape
    w = f64(np.asarray(w, np.float32).astype(ml_dtypes.bfloat16)).reshape(k // 32, 32, n)
    amax = np.abs(w).max(1)
    mant, ex = np.frexp(amax / 6.0)
    byte = np.clip(np.where(amax > 0, np.where(mant > 0.5, ex, ex - 1) + 127, 1), 1, 254)
    scaled = (w * np.exp2(127.0 - byte)[:, None, :]).reshape(k, n).astype(np.float32)
    c = np.ascontiguousarray(scaled.reshape(k // 512, 128, 4, n).transpose(0, 1, 3, 2)).astype(ml_dtypes.float4_e2m1fn).view(np.uint8) & 0xF
    words = (c[..., 0::2] | (c[..., 1::2] << 4)).reshape(k // 512, 128, 2 * n)
    return np.ascontiguousarray(words), np.ascontiguousarray(byte.astype(np.uint8).reshape(k // 512, 16, n))


def unpack_fp4(words, scales):
    g, _, n = scales.shape
    words = np.ascontiguousarray(words).reshape(g, 128, n, 2)
    nib = np.empty((g, 128, n, 4), np.uint8)
    nib[..., 0::2] = words & 0xF
    nib[..., 1::2] = words >> 4
    vals = E2M1[nib] * np.repeat(np.exp2(scales.astype(np.float64) - 127.0), 8, axis=1)[..., None]
    return vals.transpose(0, 1, 3, 2).reshape(g * 512, n)


def gelu(v):
    return 0.5 * v * (1.0 + np.tanh(np.sqrt(2.0 / np.pi) * (v + 0.044715 * v**3)))

def planes(y):
    n, m = y.shape
    v = y.astype(np.float32).astype(ml_dtypes.bfloat16).astype(np.float64).reshape(n // 32, 32, m)
    top = np.abs(v).max(1)
    byte = np.clip(np.where(top > 0, np.frexp(top)[1] - 1 + 127 - 7, 1), 1, 254)
    codes = (v * np.exp2(127.0 - byte)[:, None, :]).reshape(n, m).astype(np.float32).astype(ml_dtypes.float8_e4m3fn).view(np.uint8)
    words = codes.reshape(n // 512, 128, 4, m).transpose(0, 1, 3, 2)
    return np.ascontiguousarray(words), np.ascontiguousarray(byte.astype(np.uint8).reshape(n // 512, 16, m))


K, T, D, H = 1024, 512, 4, 512
P = 2 ** 7


def setup_inputs():
    n = np.random.standard_normal
    s = mx_kscale(K)[:, None]
    u = mx_kscale(H)
    packed_xT = pack_fp4(n((K, T)) * s)
    return {
        "x_words": packed_xT[0],
        "x_scales": packed_xT[1],
        "w1": (n((K, H)) / np.sqrt(K) / s * u).astype(np.float32),
        "w2": (n((H, H)) / np.sqrt(H) / u[:, None]).astype(np.float32),
        "gate": (np.tile(np.random.uniform(0.2, 1.0, (D, 1, T)) / np.sqrt(D), (1, P, 1))).astype(np.float32),
        "pos1": striped(np.random.permutation(T)),
        "pos2": striped(np.random.permutation(T)),
        "pos3": striped(np.random.permutation(T)),
        "pos4": striped(np.random.permutation(T)),
    }


def reference(x_words, x_scales, w1, w2, gate, pos1, pos2, pos3, pos4):
    xq = unpack_fp4(x_words, x_scales)
    h = gelu(mxq(f64(w1), 0, "e4m3").T @ xq)
    z = h - (h[:, unstriped(pos1)] * f64(gate)[0, :1] + h[:, unstriped(pos2)] * f64(gate)[1, :1] + h[:, unstriped(pos3)] * f64(gate)[2, :1] + h[:, unstriped(pos4)] * f64(gate)[3, :1])
    out_0 = mxq(f64(w2), 0, "e4m3").T @ mxq(z, 0, "e4m3")
    return (out_0,) + planes(out_0)

@@ -1,0 +1,255 @@
+from contextlib import ExitStack
+
+import concourse.mybir as mybir
+from concourse.masks import make_identity
+
+K, T, D, H = 1024, 512, 4, 512
+P = 128
+PACK = 4
+PASSES = K // (P * PACK)
+TILES = H // P
+SPARE = 16
+
+FLOPS = 2 * K * H * T + 2 * H * H * T
+
+F32 = mybir.dt.float32
+BF16 = mybir.dt.bfloat16
+I32 = mybir.dt.int32
+U32 = mybir.dt.uint32
+U16 = mybir.dt.uint16
+U8 = mybir.dt.uint8
+FP8X4 = mybir.dt.float8_e4m3fn_x4
+FP4X4 = mybir.dt.float4_e2m1fn_x4
+ACT = mybir.ActivationFunctionType
+ALU = mybir.AluOpType
+
+CHUNKS = ((0, 256), (256, 128), (384, 128))
+
+
+def tile_picked_wlapl_gelu_lo_kernel(tc, x_words, x_scales, w1, w2, gate, pos1, pos2, pos3, pos4, out_0, out_1, out_2):
+    nc = tc.nc
+    with ExitStack() as ctx:
+        keep = ctx.enter_context(tc.tile_pool(name="keep", bufs=1))
+        psum = ctx.enter_context(tc.psum_pool(name="psum", bufs=1))
+
+        def sb(name, shape, dtype, tag=None):
+            return keep.tile(shape, dtype, name=name, tag=tag or name, align_bytes=64)
+
+        lists = [keep.tile([P, T // 16], U16, name="list%d" % d) for d in range(D)]
+        x_sc = sb("x_sc", [P, PASSES * T], U8)
+        nc.vector.memset(x_sc[:].bitcast(I32), 0)
+        warm = sb("warm", [P, 1], F32)
+        warm_out = sb("warm_out", [P, 1], F32)
+        nc.vector.memset(warm[:], 0.0)
+
+        w1_raw = [[sb("w1_raw%d_%d" % (t, g), [P, PACK, P], F32) for g in range(PASSES)] for t in range(TILES)]
+
+        def load_w1(t):
+            for g in range(PASSES):
+                rows = w1[g * P * PACK : (g + 1) * P * PACK, t * P : (t + 1) * P]
+                nc.sync.dma_start(out=w1_raw[t][g][:], in_=rows.rearrange("(p j) c -> p j c", j=PACK))
+
+        gate_raw = [sb("gate_raw%d" % d, [P, T], F32) for d in range(D)]
+        pos = (pos1, pos2, pos3, pos4)
+
+        def load_gate(d):
+            nc.sync.dma_start(out=gate_raw[d][:], in_=gate[d])
+
+        def load_list(d):
+            nc.sync.dma_start(out=lists[d][:], in_=pos[d])
+
+        load_w1(0)
+        x_w = sb("x_w", [P, PASSES, 2 * T], U8)
+        nc.sync.dma_start(out=x_w[:].bitcast(I32), in_=x_words.bitcast(I32).rearrange("g p c -> p g c"))
+        x_sc_rows = x_sc[:].bitcast(I32).rearrange("p (g c) -> p g c", g=PASSES)
+        for q in range(4):
+            nc.scalar.dma_start(
+                out=x_sc_rows[32 * q : 32 * q + 4],
+                in_=x_scales.bitcast(I32)[:, 4 * q : 4 * q + 4, :].rearrange("g r c -> r g c"),
+            )
+        nc.scalar.activation(out=warm_out[:], in_=warm[:], func=ACT.Gelu_apprx_tanh)
+        load_gate(0)
+        load_w1(1)
+        load_list(0)
+        for d in range(1, D):
+            load_gate(d)
+            load_list(d)
+        load_w1(2)
+        load_w1(3)
+        w2_raw = sb("w2_raw", [P, PACK, H], F32)
+        nc.sync.dma_start(out=w2_raw[:], in_=w2.rearrange("(p j) m -> p j m", j=PACK))
+
+        ident = sb("ident", [P, P], F32)
+        make_identity(nc, ident[:])
+
+        h = [sb("h%d" % t, [P, T + (SPARE if t == 0 else 0)], F32) for t in range(TILES)]
+        nc.gpsimd.memset(h[0][:, T:], 0.0)
+
+        w1_bf = [sb("w1_bf%d" % t, [P, PASSES * P * PACK], BF16) for t in range(TILES)]
+        w1_codes = [sb("w1_codes%d" % t, [P, PASSES * P], U32) for t in range(TILES)]
+        w1_sc = [sb("w1_sc%d" % t, [P, PASSES * P], U8) for t in range(TILES)]
+
+        def round_w1(t, copy):
+            for g in range(PASSES):
+                copy(
+                    out=w1_bf[t][:, g * P * PACK : (g + 1) * P * PACK].rearrange("p (c i j) -> p c j i", i=4, j=PACK),
+                    in_=w1_raw[t][g][:].rearrange("p j (c i) -> p c j i", i=4),
+                )
+
+        def first_layer(t):
+            width = P if t == 0 else PASSES * P
+            for c in range(0, PASSES * P, width):
+                nc.vector.quantize_mx(
+                    out=w1_codes[t][:, c : c + width].bitcast(FP8X4),
+                    scales=w1_sc[t][:, c : c + width],
+                    in_=w1_bf[t][:, c * PACK : (c + width) * PACK],
+                )
+            u = psum.tile([P, T], F32, name="u%d" % t, tag="work", bufs=4)
+            for g in range(PASSES):
+                nc.tensor.matmul_mx(
+                    out=u[:],
+                    lhsT=w1_codes[t][:, g * P : (g + 1) * P].bitcast(FP8X4),
+                    lhsT_scale=w1_sc[t][:, g * P : (g + 1) * P],
+                    rhs=x_w[:, g, :].bitcast(FP4X4),
+                    rhs_scale=x_sc[:, g * T : (g + 1) * T],
+                    start=(g == 0),
+                    stop=(g == PASSES - 1),
+                )
+            nc.scalar.activation(out=h[t][:, :T], in_=u[:], func=ACT.Gelu_apprx_tanh)
+
+        neg_gate = [sb("neg_gate%d" % d, [P, T], F32) for d in range(D)]
+
+        def negate_on_vector(d):
+            nc.vector.tensor_scalar(out=neg_gate[d][:], in0=gate_raw[d][:], scalar1=-1.0, scalar2=None, op0=ALU.mult)
+
+        def negate_on_scalar(d):
+            nc.scalar.activation(out=neg_gate[d][:], in_=gate_raw[d][:], func=ACT.Copy, scale=-1.0)
+
+        zT = [sb("zT%d" % c, [P, n // P, 2, 2 * P], BF16) for c, (v0, n) in enumerate(CHUNKS)]
+
+        sums = [psum.tile([P, H], F32, name="sum%d" % b) for b in range(T // P)]
+
+        def transpose_add(t, b, part, start, stop):
+            nc.tensor.matmul(sums[b][:, t * P : (t + 1) * P], lhsT=part, rhs=ident[:], start=start, stop=stop, is_transpose=True)
+
+        def stage(jobs, after=None):
+            t, v0, n, ds = jobs[0]
+            terms = sb("terms%d_%d_%d" % (t, v0, ds[0]), [P, sum(n * len(ds) for t, v0, n, ds in jobs)], F32, tag=after)
+            at = 0
+            for t, v0, n, ds in jobs:
+                neighbours(t, v0, n, ds, terms[:, at : at + n * len(ds)])
+                at = at + n * len(ds)
+            return terms
+
+        def neighbours(t, v0, n, ds, terms):
+            blocks = range(v0 // P, (v0 + n) // P)
+            for s, d in enumerate(ds):
+                term = terms[:, s * n : (s + 1) * n]
+                nc.vector.tensor_tensor(
+                    out=term,
+                    in0=h[t][:].indirect(lists[d][:, v0 // 16 : (v0 + n) // 16]),
+                    in1=neg_gate[d][:, v0 : v0 + n],
+                    op=ALU.mult,
+                )
+                for b in blocks:
+                    if d == 0:
+                        transpose_add(t, b, h[t][:, b * P : (b + 1) * P], True, False)
+                    transpose_add(t, b, term[:, b * P - v0 : (b + 1) * P - v0], False, d == D - 1)
+            if ds[-1] == D - 1:
+                for b in blocks:
+                    c = max(b - 1, 0)
+                    nc.scalar.copy(
+                        out=zT[c][:, b - CHUNKS[c][0] // P, :, 64 * t : 64 * (t + 1)].rearrange("p u (q e) -> p u q e", e=2),
+                        in_=sums[b][:, t * P : (t + 1) * P].rearrange("p (q u e) -> p u q e", u=2, e=2),
+                    )
+
+        w2_bf = sb("w2_bf", [P, TILES, P, PACK], BF16)
+        w2_codes = sb("w2_codes", [P, H], U32)
+        w2_sc = sb("w2_sc", [P, H], U8)
+
+        def prepare_w2():
+            nc.scalar.copy(
+                out=w2_bf[:].rearrange("p t m j -> p m j t"),
+                in_=w2_raw[:].rearrange("p j (m t) -> p m j t", t=TILES),
+            )
+            nc.vector.quantize_mx(out=w2_codes[:].bitcast(FP8X4), scales=w2_sc[:], in_=w2_bf[:].rearrange("p t m j -> p (t m j)"))
+
+        y_codes = sb("y_codes", [P, T], U32)
+        y_sc = sb("y_sc", [P, T], U8)
+        out_rows = out_0.rearrange("(p t) v -> p t v", t=TILES)
+        out_words = out_1[0].rearrange("p v r -> p (v r)").bitcast(I32)
+
+        def second_layer(c):
+            v0, n = CHUNKS[c]
+            last = c == len(CHUNKS) - 1
+            words = zT[c][:].bitcast(F32)
+            back = psum.tile([P, 2, 2, P], F32, name="back%d" % c, tag="work", bufs=4)
+            for b in range(n // P):
+                for u in range(2):
+                    nc.tensor.transpose(back[:, b, u, :], words[:, b, u, :], ident[:])
+            z_bf = sb("z_bf%d" % c, [P, n * PACK], BF16)
+            nc.scalar.copy(
+                out=z_bf[:].bitcast(F32).rearrange("p (b v u) -> p b v u", v=P, u=2),
+                in_=back[:, : n // P].rearrange("p b u v -> p b v u"),
+            )
+            z_codes = sb("z_codes%d" % c, [P, n], U32)
+            z_sc = sb("z_sc%d" % c, [P, n], U8)
+            nc.vector.quantize_mx(out=z_codes[:].bitcast(FP8X4), scales=z_sc[:], in_=z_bf[:])
+            y = sb("y%d" % c, [P, TILES, n], F32)
+            for half in range(2):
+                acc = psum.tile([P, 2, 256], F32, name="acc%d_%d" % (c, half), tag="work", bufs=4)
+                for s in range(2):
+                    t = 2 * half + s
+                    nc.tensor.matmul_mx(
+                        out=acc[:, s, :n],
+                        lhsT=w2_codes[:, t * P : (t + 1) * P].bitcast(FP8X4),
+                        lhsT_scale=w2_sc[:, t * P : (t + 1) * P],
+                        rhs=z_codes[:].bitcast(FP8X4),
+                        rhs_scale=z_sc[:],
+                        start=True,
+                        stop=True,
+                    )
+                copy = nc.vector.tensor_copy if last and half == 1 else nc.scalar.copy
+                copy(out=y[:, 2 * half : 2 * half + 2, :], in_=acc[:, :, :n])
+            nc.sync.dma_start(out=out_rows[:, :, v0 : v0 + n], in_=y[:])
+            y_bf = sb("y_bf%d" % c, [P, n * PACK], BF16)
+            copy = nc.vector.tensor_copy if c > 0 else nc.scalar.copy
+            copy(
+                out=y_bf[:].rearrange("p (c i t) -> p c t i", i=4, t=TILES),
+                in_=y[:].rearrange("p t (c i) -> p c t i", i=4),
+            )
+            nc.vector.quantize_mx(out=y_codes[:, v0 : v0 + n].bitcast(FP8X4), scales=y_sc[:, v0 : v0 + n], in_=y_bf[:])
+            nc.sync.dma_start(out=out_words[:, v0 : v0 + n], in_=y_codes[:, v0 : v0 + n].bitcast(I32))
+
+        round_w1(0, nc.vector.tensor_copy)
+        first_layer(0)
+        negate_on_vector(0)
+        negate_on_vector(1)
+        round_w1(1, nc.scalar.copy)
+        first_layer(1)
+        negate_on_scalar(2)
+        negate_on_scalar(3)
+        every = (0, 1, 2, 3)
+        stage([(0, 0, T, (0, 1))])
+        stage([(0, 0, T, (2, 3))], after="w1_bf1")
+        round_w1(2, nc.scalar.copy)
+        first_layer(2)
+        round_w1(3, nc.scalar.copy)
+        first_layer(3)
+        stage([(1, 0, 384, (0,))])
+        stage([(1, 0, 384, (1, 2))], after="w1_bf2")
+        stage([(1, 0, 384, (3,)), (2, 0, 256, every)], after="w1_bf3")
+        prepare_w2()
+        stage([(3, 0, 256, every), (2, 256, 128, every), (3, 256, 128, every)], after="w2_bf")
+        second_layer(0)
+        stage([(1, 384, 128, every), (2, 384, 128, every)], after="z_bf0")
+        second_layer(1)
+        stage([(3, 384, 128, every)], after="z_bf1")
+        second_layer(2)
+
+        for q in range(4):
+            queue = nc.scalar if q % 2 else nc.sync
+            queue.dma_start(
+                out=out_2[0, 4 * q : 4 * q + 4, :].bitcast(I32),
+                in_=y_sc[32 * q : 32 * q + 4, :].bitcast(I32),
+            )

@@ -35,6 +35,9 @@ def tile_picked_wlapl_gelu_lo_kernel(tc, x_words, x_scales, w1, w2, gate, pos1, 
         def sb(name, shape, dtype, tag=None):
             return keep.tile(shape, dtype, name=name, tag=tag or name, align_bytes=64)
 
+        def bank(number, name, shape):
+            return psum.tile(shape, F32, name=name, tag="bank%d" % number)
+
         lists = [keep.tile([P, T // 16], U16, name="list%d" % d) for d in range(D)]
         x_sc = sb("x_sc", [P, PASSES * T], U8)
         nc.vector.memset(x_sc[:].bitcast(I32), 0)
@@ -49,11 +52,8 @@ def tile_picked_wlapl_gelu_lo_kernel(tc, x_words, x_scales, w1, w2, gate, pos1, 
                 rows = w1[g * P * PACK : (g + 1) * P * PACK, t * P : (t + 1) * P]
                 nc.sync.dma_start(out=w1_raw[t][g][:], in_=rows.rearrange("(p j) c -> p j c", j=PACK))
 
-        gate_raw = [sb("gate_raw%d" % d, [P, T], F32) for d in range(D)]
+        gate_cols = sb("gate_cols", [P, D, T // P], F32)
         pos = (pos1, pos2, pos3, pos4)
-
-        def load_gate(d):
-            nc.sync.dma_start(out=gate_raw[d][:], in_=gate[d])
 
         def load_list(d):
             nc.sync.dma_start(out=lists[d][:], in_=pos[d])
@@ -68,11 +68,9 @@ def tile_picked_wlapl_gelu_lo_kernel(tc, x_words, x_scales, w1, w2, gate, pos1, 
                 in_=x_scales.bitcast(I32)[:, 4 * q : 4 * q + 4, :].rearrange("g r c -> r g c"),
             )
         nc.scalar.activation(out=warm_out[:], in_=warm[:], func=ACT.Gelu_apprx_tanh)
-        load_gate(0)
+        nc.sync.dma_start(out=gate_cols[:], in_=gate[:, 0, :].rearrange("d (p c) -> p d c", p=P))
         load_w1(1)
-        load_list(0)
-        for d in range(1, D):
-            load_gate(d)
+        for d in range(D):
             load_list(d)
         load_w1(2)
         load_w1(3)
@@ -104,7 +102,7 @@ def tile_picked_wlapl_gelu_lo_kernel(tc, x_words, x_scales, w1, w2, gate, pos1, 
                     scales=w1_sc[t][:, c : c + width],
                     in_=w1_bf[t][:, c * PACK : (c + width) * PACK],
                 )
-            u = psum.tile([P, T], F32, name="u%d" % t, tag="work", bufs=4)
+            u = bank(4 + t % 2, "u%d" % t, [P, T])
             for g in range(PASSES):
                 nc.tensor.matmul_mx(
                     out=u[:],
@@ -119,30 +117,30 @@ def tile_picked_wlapl_gelu_lo_kernel(tc, x_words, x_scales, w1, w2, gate, pos1, 
 
         neg_gate = [sb("neg_gate%d" % d, [P, T], F32) for d in range(D)]
 
-        def negate_on_vector(d):
-            nc.vector.tensor_scalar(out=neg_gate[d][:], in0=gate_raw[d][:], scalar1=-1.0, scalar2=None, op0=ALU.mult)
-
-        def negate_on_scalar(d):
-            nc.scalar.activation(out=neg_gate[d][:], in_=gate_raw[d][:], func=ACT.Copy, scale=-1.0)
+        def spread_gate(d):
+            rows = bank(d, "gate_rows%d" % d, [P, T // P, P])
+            for c in range(T // P):
+                nc.tensor.transpose(rows[:, c, :], gate_cols[:, d, c : c + 1].to_broadcast([P, P]), ident[:])
+            nc.scalar.activation(
+                out=neg_gate[d][:].rearrange("p (n c) -> p n c", c=T // P),
+                in_=rows[:].rearrange("p c n -> p n c"),
+                func=ACT.Copy,
+                scale=-1.0,
+            )
 
         zT = [sb("zT%d" % c, [P, n // P, 2, 2 * P], BF16) for c, (v0, n) in enumerate(CHUNKS)]
 
-        sums = [psum.tile([P, H], F32, name="sum%d" % b) for b in range(T // P)]
-
-        def transpose_add(t, b, part, start, stop):
-            nc.tensor.matmul(sums[b][:, t * P : (t + 1) * P], lhsT=part, rhs=ident[:], start=start, stop=stop, is_transpose=True)
-
         def stage(jobs, after=None):
-            t, v0, n, ds = jobs[0]
-            terms = sb("terms%d_%d_%d" % (t, v0, ds[0]), [P, sum(n * len(ds) for t, v0, n, ds in jobs)], F32, tag=after)
+            t, v0, n, ds, sums = jobs[0]
+            terms = sb("terms%d_%d_%d" % (t, v0, ds[0]), [P, sum(job[2] * len(job[3]) for job in jobs)], F32, tag=after)
             at = 0
-            for t, v0, n, ds in jobs:
-                neighbours(t, v0, n, ds, terms[:, at : at + n * len(ds)])
+            for t, v0, n, ds, sums in jobs:
+                neighbours(t, v0, n, ds, sums, terms[:, at : at + n * len(ds)])
                 at = at + n * len(ds)
             return terms
 
-        def neighbours(t, v0, n, ds, terms):
-            blocks = range(v0 // P, (v0 + n) // P)
+        def neighbours(t, v0, n, ds, sums, terms):
+            blocks = range(n // P)
             for s, d in enumerate(ds):
                 term = terms[:, s * n : (s + 1) * n]
                 nc.vector.tensor_tensor(
@@ -153,15 +151,21 @@ def tile_picked_wlapl_gelu_lo_kernel(tc, x_words, x_scales, w1, w2, gate, pos1, 
                 )
                 for b in blocks:
                     if d == 0:
-                        transpose_add(t, b, h[t][:, b * P : (b + 1) * P], True, False)
-                    transpose_add(t, b, term[:, b * P - v0 : (b + 1) * P - v0], False, d == D - 1)
+                        own = h[t][:, v0 + b * P : v0 + (b + 1) * P]
+                        nc.tensor.matmul(sums[b], lhsT=own, rhs=ident[:], start=True, stop=False, is_transpose=True)
+                    part = term[:, b * P : (b + 1) * P]
+                    nc.tensor.matmul(sums[b], lhsT=part, rhs=ident[:], start=False, stop=(d == D - 1), is_transpose=True)
             if ds[-1] == D - 1:
                 for b in blocks:
-                    c = max(b - 1, 0)
+                    block = v0 // P + b
+                    c = max(block - 1, 0)
                     nc.scalar.copy(
-                        out=zT[c][:, b - CHUNKS[c][0] // P, :, 64 * t : 64 * (t + 1)].rearrange("p u (q e) -> p u q e", e=2),
-                        in_=sums[b][:, t * P : (t + 1) * P].rearrange("p (q u e) -> p u q e", u=2, e=2),
+                        out=zT[c][:, block - CHUNKS[c][0] // P, :, 64 * t : 64 * (t + 1)].rearrange("p u (q e) -> p u q e", e=2),
+                        in_=sums[b].rearrange("p (q u e) -> p u q e", u=2, e=2),
                     )
+
+        def sum_banks(t, numbers):
+            return [bank(number, "sum%d_%d" % (t, number), [P, P])[:] for number in numbers]
 
         w2_bf = sb("w2_bf", [P, TILES, P, PACK], BF16)
         w2_codes = sb("w2_codes", [P, H], U32)
@@ -169,8 +173,8 @@ def tile_picked_wlapl_gelu_lo_kernel(tc, x_words, x_scales, w1, w2, gate, pos1, 
 
         def prepare_w2():
             nc.scalar.copy(
-                out=w2_bf[:].rearrange("p t m j -> p m j t"),
-                in_=w2_raw[:].rearrange("p j (m t) -> p m j t", t=TILES),
+                out=w2_bf[:].rearrange("p t m j -> p m t j"),
+                in_=w2_raw[:].rearrange("p j (m t) -> p m t j", t=TILES),
             )
             nc.vector.quantize_mx(out=w2_codes[:].bitcast(FP8X4), scales=w2_sc[:], in_=w2_bf[:].rearrange("p t m j -> p (t m j)"))
 
@@ -179,11 +183,10 @@ def tile_picked_wlapl_gelu_lo_kernel(tc, x_words, x_scales, w1, w2, gate, pos1, 
         out_rows = out_0.rearrange("(p t) v -> p t v", t=TILES)
         out_words = out_1[0].rearrange("p v r -> p (v r)").bitcast(I32)
 
-        def second_layer(c):
+        def turn_back(c):
             v0, n = CHUNKS[c]
-            last = c == len(CHUNKS) - 1
             words = zT[c][:].bitcast(F32)
-            back = psum.tile([P, 2, 2, P], F32, name="back%d" % c, tag="work", bufs=4)
+            back = bank(6, "back%d" % c, [P, 2, 2, P])
             for b in range(n // P):
                 for u in range(2):
                     nc.tensor.transpose(back[:, b, u, :], words[:, b, u, :], ident[:])
@@ -192,12 +195,16 @@ def tile_picked_wlapl_gelu_lo_kernel(tc, x_words, x_scales, w1, w2, gate, pos1, 
                 out=z_bf[:].bitcast(F32).rearrange("p (b v u) -> p b v u", v=P, u=2),
                 in_=back[:, : n // P].rearrange("p b u v -> p b v u"),
             )
+            return z_bf
+
+        def second_layer(c, z_bf):
+            v0, n = CHUNKS[c]
             z_codes = sb("z_codes%d" % c, [P, n], U32)
             z_sc = sb("z_sc%d" % c, [P, n], U8)
             nc.vector.quantize_mx(out=z_codes[:].bitcast(FP8X4), scales=z_sc[:], in_=z_bf[:])
             y = sb("y%d" % c, [P, TILES, n], F32)
             for half in range(2):
-                acc = psum.tile([P, 2, 256], F32, name="acc%d_%d" % (c, half), tag="work", bufs=4)
+                acc = bank((4, 5, 2, 3)[2 * (c % 2) + half], "acc%d_%d" % (c, half), [P, 2, 256])
                 for s in range(2):
                     t = 2 * half + s
                     nc.tensor.matmul_mx(
@@ -209,43 +216,59 @@ def tile_picked_wlapl_gelu_lo_kernel(tc, x_words, x_scales, w1, w2, gate, pos1, 
                         start=True,
                         stop=True,
                     )
-                copy = nc.vector.tensor_copy if last and half == 1 else nc.scalar.copy
+                copy = nc.vector.tensor_copy if c > 0 and half == 1 else nc.scalar.copy
                 copy(out=y[:, 2 * half : 2 * half + 2, :], in_=acc[:, :, :n])
             nc.sync.dma_start(out=out_rows[:, :, v0 : v0 + n], in_=y[:])
-            y_bf = sb("y_bf%d" % c, [P, n * PACK], BF16)
-            copy = nc.vector.tensor_copy if c > 0 else nc.scalar.copy
-            copy(
+            return y
+
+        def hand_on(c, y, after=None):
+            v0, n = CHUNKS[c]
+            y_bf = sb("y_bf%d" % c, [P, n * PACK], BF16, tag=after)
+            nc.vector.tensor_copy(
                 out=y_bf[:].rearrange("p (c i t) -> p c t i", i=4, t=TILES),
                 in_=y[:].rearrange("p t (c i) -> p c t i", i=4),
             )
             nc.vector.quantize_mx(out=y_codes[:, v0 : v0 + n].bitcast(FP8X4), scales=y_sc[:, v0 : v0 + n], in_=y_bf[:])
             nc.sync.dma_start(out=out_words[:, v0 : v0 + n], in_=y_codes[:, v0 : v0 + n].bitcast(I32))
 
+        every = (0, 1, 2, 3)
         round_w1(0, nc.vector.tensor_copy)
         first_layer(0)
-        negate_on_vector(0)
-        negate_on_vector(1)
+        for d in range(D):
+            spread_gate(d)
         round_w1(1, nc.scalar.copy)
         first_layer(1)
-        negate_on_scalar(2)
-        negate_on_scalar(3)
-        every = (0, 1, 2, 3)
-        stage([(0, 0, T, (0, 1))])
-        stage([(0, 0, T, (2, 3))], after="w1_bf1")
+        sums = sum_banks(0, (0, 1, 2, 3))
+        stage([(0, 0, T, (0, 1), sums)])
         round_w1(2, nc.scalar.copy)
+        stage([(0, 0, T, (2, 3), sums)], after="w1_bf1")
         first_layer(2)
         round_w1(3, nc.scalar.copy)
+        stage([(1, 0, 256, every, sum_banks(1, (0, 1)))], after="w1_bf2")
         first_layer(3)
-        stage([(1, 0, 384, (0,))])
-        stage([(1, 0, 384, (1, 2))], after="w1_bf2")
-        stage([(1, 0, 384, (3,)), (2, 0, 256, every)], after="w1_bf3")
         prepare_w2()
-        stage([(3, 0, 256, every), (2, 256, 128, every), (3, 256, 128, every)], after="w2_bf")
-        second_layer(0)
-        stage([(1, 384, 128, every), (2, 384, 128, every)], after="z_bf0")
-        second_layer(1)
-        stage([(3, 384, 128, every)], after="z_bf1")
-        second_layer(2)
+        stage([(2, 0, 256, every, sum_banks(2, (2, 3)))], after="w1_bf3")
+        terms = sb("terms_late", [P, 10 * 256], F32, tag="w2_bf")
+        neighbours(3, 0, 256, every, sum_banks(3, (0, 1)), terms[:, :1024])
+        z_bf = turn_back(0)
+        second = bank(1, "sum_second", [P, 3, P])
+        neighbours(1, 256, 128, every, [second[:, 0, :]], terms[:, 1024:1536])
+        neighbours(2, 256, 128, every, [second[:, 1, :]], terms[:, 1536:2048])
+        neighbours(3, 256, 128, (0, 1), [second[:, 2, :]], terms[:, 2048:2304])
+        y0 = second_layer(0, z_bf)
+        terms = sb("terms_later", [P, 10 * 128], F32, tag="z_bf0")
+        neighbours(3, 256, 128, (2, 3), [second[:, 2, :]], terms[:, :256])
+        z_bf = turn_back(1)
+        third = bank(1, "sum_third", [P, 3, P])
+        neighbours(1, 384, 128, every, [third[:, 0, :]], terms[:, 256:768])
+        neighbours(2, 384, 128, every, [third[:, 1, :]], terms[:, 768:1280])
+        y1 = second_layer(1, z_bf)
+        last_terms = stage([(3, 384, 128, every, [third[:, 2, :]])], after="z_bf1")
+        z_bf = turn_back(2)
+        hand_on(0, y0, after="h3")
+        y2 = second_layer(2, z_bf)
+        hand_on(1, y1)
+        hand_on(2, y2)
 
         for q in range(4):
             queue = nc.scalar if q % 2 else nc.sync

@@ -28,6 +28,7 @@ CHUNKS = ((0, 256), (256, 128), (384, 128))
 
 def tile_picked_wlapl_gelu_lo_kernel(tc, x_words, x_scales, w1, w2, gate, pos1, pos2, pos3, pos4, out_0, out_1, out_2):
     nc = tc.nc
+    on_vector, on_scalar = nc.vector.tensor_copy, nc.scalar.copy
     with ExitStack() as ctx:
         keep = ctx.enter_context(tc.tile_pool(name="keep", bufs=1))
         psum = ctx.enter_context(tc.psum_pool(name="psum", bufs=1))
@@ -40,10 +41,8 @@ def tile_picked_wlapl_gelu_lo_kernel(tc, x_words, x_scales, w1, w2, gate, pos1, 
 
         lists = [keep.tile([P, T // 16], U16, name="list%d" % d) for d in range(D)]
         x_sc = sb("x_sc", [P, PASSES * T], U8)
-        nc.vector.memset(x_sc[:].bitcast(I32), 0)
-        warm = sb("warm", [P, 1], F32)
+        nc.gpsimd.memset(x_sc[:].bitcast(I32), 0)
         warm_out = sb("warm_out", [P, 1], F32)
-        nc.vector.memset(warm[:], 0.0)
 
         w1_raw = [[sb("w1_raw%d_%d" % (t, g), [P, PACK, P], F32) for g in range(PASSES)] for t in range(TILES)]
 
@@ -52,11 +51,12 @@ def tile_picked_wlapl_gelu_lo_kernel(tc, x_words, x_scales, w1, w2, gate, pos1, 
                 rows = w1[g * P * PACK : (g + 1) * P * PACK, t * P : (t + 1) * P]
                 nc.sync.dma_start(out=w1_raw[t][g][:], in_=rows.rearrange("(p j) c -> p j c", j=PACK))
 
-        gate_cols = sb("gate_cols", [P, D, T // P], F32)
+        gate_raw = [sb("gate_raw%d" % d, [P, T], F32) for d in range(D)]
         pos = (pos1, pos2, pos3, pos4)
 
-        def load_list(d):
+        def load_gate(d):
             nc.sync.dma_start(out=lists[d][:], in_=pos[d])
+            nc.sync.dma_start(out=gate_raw[d][:], in_=gate[d])
 
         load_w1(0)
         x_w = sb("x_w", [P, PASSES, 2 * T], U8)
@@ -67,11 +67,11 @@ def tile_picked_wlapl_gelu_lo_kernel(tc, x_words, x_scales, w1, w2, gate, pos1, 
                 out=x_sc_rows[32 * q : 32 * q + 4],
                 in_=x_scales.bitcast(I32)[:, 4 * q : 4 * q + 4, :].rearrange("g r c -> r g c"),
             )
-        nc.scalar.activation(out=warm_out[:], in_=warm[:], func=ACT.Gelu_apprx_tanh)
-        nc.sync.dma_start(out=gate_cols[:], in_=gate[:, 0, :].rearrange("d (p c) -> p d c", p=P))
+        load_gate(0)
+        load_gate(1)
         load_w1(1)
-        for d in range(D):
-            load_list(d)
+        load_gate(2)
+        load_gate(3)
         load_w1(2)
         load_w1(3)
         w2_raw = sb("w2_raw", [P, PACK, H], F32)
@@ -79,6 +79,7 @@ def tile_picked_wlapl_gelu_lo_kernel(tc, x_words, x_scales, w1, w2, gate, pos1, 
 
         ident = sb("ident", [P, P], F32)
         make_identity(nc, ident[:])
+        nc.scalar.activation(out=warm_out[:], in_=ident[:, 0:1], func=ACT.Gelu_apprx_tanh)
 
         h = [sb("h%d" % t, [P, T + (SPARE if t == 0 else 0)], F32) for t in range(TILES)]
         nc.gpsimd.memset(h[0][:, T:], 0.0)
@@ -87,8 +88,8 @@ def tile_picked_wlapl_gelu_lo_kernel(tc, x_words, x_scales, w1, w2, gate, pos1, 
         w1_codes = [sb("w1_codes%d" % t, [P, PASSES * P], U32) for t in range(TILES)]
         w1_sc = [sb("w1_sc%d" % t, [P, PASSES * P], U8) for t in range(TILES)]
 
-        def round_w1(t, copy):
-            for g in range(PASSES):
+        def round_w1(t, copies):
+            for g, copy in enumerate(copies):
                 copy(
                     out=w1_bf[t][:, g * P * PACK : (g + 1) * P * PACK].rearrange("p (c i j) -> p c j i", i=4, j=PACK),
                     in_=w1_raw[t][g][:].rearrange("p j (c i) -> p c j i", i=4),
@@ -117,32 +118,30 @@ def tile_picked_wlapl_gelu_lo_kernel(tc, x_words, x_scales, w1, w2, gate, pos1, 
 
         neg_gate = [sb("neg_gate%d" % d, [P, T], F32) for d in range(D)]
 
-        def spread_gate(d):
-            rows = bank(d, "gate_rows%d" % d, [P, T // P, P])
-            for c in range(T // P):
-                nc.tensor.transpose(rows[:, c, :], gate_cols[:, d, c : c + 1].to_broadcast([P, P]), ident[:])
-            nc.scalar.activation(
-                out=neg_gate[d][:].rearrange("p (n c) -> p n c", c=T // P),
-                in_=rows[:].rearrange("p c n -> p n c"),
-                func=ACT.Copy,
-                scale=-1.0,
-            )
+        def negate_on_vector(d):
+            nc.vector.tensor_scalar(out=neg_gate[d][:], in0=gate_raw[d][:], scalar1=-1.0, scalar2=None, op0=ALU.mult)
+
+        def negate_on_scalar(d):
+            nc.scalar.activation(out=neg_gate[d][:], in_=gate_raw[d][:], func=ACT.Copy, scale=-1.0)
 
         zT = [sb("zT%d" % c, [P, n // P, 2, 2 * P], BF16) for c, (v0, n) in enumerate(CHUNKS)]
 
-        def stage(jobs, after=None):
-            t, v0, n, ds, sums = jobs[0]
-            terms = sb("terms%d_%d_%d" % (t, v0, ds[0]), [P, sum(job[2] * len(job[3]) for job in jobs)], F32, tag=after)
-            at = 0
+        made = {}
+
+        def room_for(columns, name, after=None):
+            return sb(name, [P, columns], F32, tag=after)[:]
+
+        def run(jobs, room):
             for t, v0, n, ds, sums in jobs:
-                neighbours(t, v0, n, ds, sums, terms[:, at : at + n * len(ds)])
-                at = at + n * len(ds)
-            return terms
+                neighbours(t, v0, n, ds, sums, room[:, : n * len(ds)])
+                room = room[:, n * len(ds) :]
+            return room
 
         def neighbours(t, v0, n, ds, sums, terms):
             blocks = range(n // P)
             for s, d in enumerate(ds):
                 term = terms[:, s * n : (s + 1) * n]
+                made[t, v0, d] = term
                 nc.vector.tensor_tensor(
                     out=term,
                     in0=h[t][:].indirect(lists[d][:, v0 // 16 : (v0 + n) // 16]),
@@ -186,7 +185,7 @@ def tile_picked_wlapl_gelu_lo_kernel(tc, x_words, x_scales, w1, w2, gate, pos1, 
         def turn_back(c):
             v0, n = CHUNKS[c]
             words = zT[c][:].bitcast(F32)
-            back = bank(6, "back%d" % c, [P, 2, 2, P])
+            back = bank((2, 6, 7)[c], "back%d" % c, [P, 2, 2, P])
             for b in range(n // P):
                 for u in range(2):
                     nc.tensor.transpose(back[:, b, u, :], words[:, b, u, :], ident[:])
@@ -204,7 +203,7 @@ def tile_picked_wlapl_gelu_lo_kernel(tc, x_words, x_scales, w1, w2, gate, pos1, 
             nc.vector.quantize_mx(out=z_codes[:].bitcast(FP8X4), scales=z_sc[:], in_=z_bf[:])
             y = sb("y%d" % c, [P, TILES, n], F32)
             for half in range(2):
-                acc = bank((4, 5, 2, 3)[2 * (c % 2) + half], "acc%d_%d" % (c, half), [P, 2, 256])
+                acc = bank((4, 5, 2, 3, 0, 6)[2 * c + half], "acc%d_%d" % (c, half), [P, 2, 256])
                 for s in range(2):
                     t = 2 * half + s
                     nc.tensor.matmul_mx(
@@ -232,42 +231,41 @@ def tile_picked_wlapl_gelu_lo_kernel(tc, x_words, x_scales, w1, w2, gate, pos1, 
             nc.sync.dma_start(out=out_words[:, v0 : v0 + n], in_=y_codes[:, v0 : v0 + n].bitcast(I32))
 
         every = (0, 1, 2, 3)
-        round_w1(0, nc.vector.tensor_copy)
+        round_w1(0, (on_vector, on_vector))
         first_layer(0)
-        for d in range(D):
-            spread_gate(d)
-        round_w1(1, nc.scalar.copy)
+        negate_on_vector(0)
+        negate_on_vector(1)
+        round_w1(1, (on_scalar, on_scalar))
         first_layer(1)
-        sums = sum_banks(0, (0, 1, 2, 3))
-        stage([(0, 0, T, (0, 1), sums)])
-        round_w1(2, nc.scalar.copy)
-        stage([(0, 0, T, (2, 3), sums)], after="w1_bf1")
+        negate_on_scalar(2)
+        negate_on_scalar(3)
+        round_w1(2, (on_scalar, on_scalar))
         first_layer(2)
-        round_w1(3, nc.scalar.copy)
-        stage([(1, 0, 256, every, sum_banks(1, (0, 1)))], after="w1_bf2")
+        round_w1(3, (on_scalar, on_scalar))
         first_layer(3)
         prepare_w2()
-        stage([(2, 0, 256, every, sum_banks(2, (2, 3)))], after="w1_bf3")
-        terms = sb("terms_late", [P, 10 * 256], F32, tag="w2_bf")
-        neighbours(3, 0, 256, every, sum_banks(3, (0, 1)), terms[:, :1024])
+        sums = sum_banks(0, (0, 1, 2, 3))
+        run([(0, 0, T, (0, 1), sums)], room_for(2 * T, "terms0"))
+        run([(0, 0, T, (2, 3), sums)], room_for(2 * T, "terms1", "w1_bf1"))
+        sums = sum_banks(1, (0, 1, 2))
+        run([(1, 0, 384, (0,), sums)], room_for(384, "terms2"))
+        later = sum_banks(2, (3, 6, 7))
+        run([(1, 0, 384, (1, 2, 3), sums), (2, 0, 384, (0,), later)], room_for(4 * 384, "terms3", "w1_bf2"))
+        run([(2, 0, 384, (1, 2, 3), later)], room_for(3 * 384, "terms4", "w1_bf3"))
+        room = run([(3, 0, 256, every, sum_banks(3, (0, 1)))], room_for(4 * 256 + 10 * 128, "terms5", "w2_bf"))
         z_bf = turn_back(0)
-        second = bank(1, "sum_second", [P, 3, P])
-        neighbours(1, 256, 128, every, [second[:, 0, :]], terms[:, 1024:1536])
-        neighbours(2, 256, 128, every, [second[:, 1, :]], terms[:, 1536:2048])
-        neighbours(3, 256, 128, (0, 1), [second[:, 2, :]], terms[:, 2048:2304])
-        y0 = second_layer(0, z_bf)
-        terms = sb("terms_later", [P, 10 * 128], F32, tag="z_bf0")
-        neighbours(3, 256, 128, (2, 3), [second[:, 2, :]], terms[:, :256])
-        z_bf = turn_back(1)
+        room = run([(3, 256, 128, every, [bank(1, "sum_second", [P, P])[:]])], room)
+        z_next = turn_back(1)
         third = bank(1, "sum_third", [P, 3, P])
-        neighbours(1, 384, 128, every, [third[:, 0, :]], terms[:, 256:768])
-        neighbours(2, 384, 128, every, [third[:, 1, :]], terms[:, 768:1280])
-        y1 = second_layer(1, z_bf)
-        last_terms = stage([(3, 384, 128, every, [third[:, 2, :]])], after="z_bf1")
+        run([(1, 384, 128, every, [third[:, 0, :]]), (2, 384, 128, (0, 1), [third[:, 1, :]])], room)
+        y0 = second_layer(0, z_bf)
+        run([(2, 384, 128, (2, 3), [third[:, 1, :]])], room_for(2 * 128, "terms6", "z_bf0"))
+        y1 = second_layer(1, z_next)
+        run([(3, 384, 128, every, [third[:, 2, :]])], room_for(4 * 128, "terms7", "z_bf1"))
         z_bf = turn_back(2)
         hand_on(0, y0, after="h3")
         y2 = second_layer(2, z_bf)
-        hand_on(1, y1)
+        hand_on(1, y1, after="z_bf2")
         hand_on(2, y2)
 
         for q in range(4):

@@ -24,6 +24,7 @@ ACT = mybir.ActivationFunctionType
 ALU = mybir.AluOpType
 
 CHUNKS = ((0, 256), (256, 128), (384, 128))
+LAST = TILES - 1
 
 
 def tile_picked_wlapl_gelu_lo_kernel(tc, x_words, x_scales, w1, w2, gate, pos1, pos2, pos3, pos4, out_0, out_1, out_2):
@@ -42,23 +43,32 @@ def tile_picked_wlapl_gelu_lo_kernel(tc, x_words, x_scales, w1, w2, gate, pos1, 
         lists = [keep.tile([P, T // 16], U16, name="list%d" % d) for d in range(D)]
         x_sc = sb("x_sc", [P, PASSES * T], U8)
         nc.gpsimd.memset(x_sc[:].bitcast(I32), 0)
+        warm_in = sb("warm_in", [P, 1], F32)
         warm_out = sb("warm_out", [P, 1], F32)
+        nc.gpsimd.memset(warm_in[:], 0.0)
 
-        w1_raw = [[sb("w1_raw%d_%d" % (t, g), [P, PACK, P], F32) for g in range(PASSES)] for t in range(TILES)]
+        groups = ((0, 1), (1, 1), (2, 1), (3, 1))
+        w1_raw = {}
 
-        def load_w1(t):
-            for g in range(PASSES):
-                rows = w1[g * P * PACK : (g + 1) * P * PACK, t * P : (t + 1) * P]
-                nc.sync.dma_start(out=w1_raw[t][g][:], in_=rows.rearrange("(p j) c -> p j c", j=PACK))
+        def load_w1(first, count, passes=range(PASSES)):
+            for g in passes:
+                raw = sb("w1_raw%d_%d" % (first, g), [P, PACK, count * P], F32)
+                rows = w1[g * P * PACK : (g + 1) * P * PACK, first * P : (first + count) * P]
+                nc.sync.dma_start(out=raw[:], in_=rows.rearrange("(p j) c -> p j c", j=PACK))
+                for s in range(count):
+                    w1_raw[first + s, g] = raw[:, :, s * P : (s + 1) * P]
 
-        gate_raw = [sb("gate_raw%d" % d, [P, T], F32) for d in range(D)]
         pos = (pos1, pos2, pos3, pos4)
+        gate_cols = {}
 
-        def load_gate(d):
-            nc.sync.dma_start(out=lists[d][:], in_=pos[d])
-            nc.sync.dma_start(out=gate_raw[d][:], in_=gate[d])
+        def load_gates(first, count):
+            cols = sb("gate_cols%d" % first, [P, count, 4], F32)
+            nc.sync.dma_start(out=cols[:], in_=gate[first : first + count, 0, :].rearrange("d (n m) -> n d m", m=4))
+            for s in range(count):
+                gate_cols[first + s] = cols[:, s, :]
 
-        load_w1(0)
+        load_gates(0, D)
+        load_w1(*groups[0])
         x_w = sb("x_w", [P, PASSES, 2 * T], U8)
         nc.sync.dma_start(out=x_w[:].bitcast(I32), in_=x_words.bitcast(I32).rearrange("g p c -> p g c"))
         x_sc_rows = x_sc[:].bitcast(I32).rearrange("p (g c) -> p g c", g=PASSES)
@@ -67,115 +77,116 @@ def tile_picked_wlapl_gelu_lo_kernel(tc, x_words, x_scales, w1, w2, gate, pos1, 
                 out=x_sc_rows[32 * q : 32 * q + 4],
                 in_=x_scales.bitcast(I32)[:, 4 * q : 4 * q + 4, :].rearrange("g r c -> r g c"),
             )
-        load_gate(0)
-        load_gate(1)
-        load_w1(1)
-        load_gate(2)
-        load_gate(3)
-        load_w1(2)
-        load_w1(3)
+        nc.scalar.activation(out=warm_out[:], in_=warm_in[:], func=ACT.Gelu_apprx_tanh)
+        nc.sync.dma_start(out=lists[0][:], in_=pos[0])
+        load_w1(*groups[1])
+        for d in range(1, D):
+            nc.sync.dma_start(out=lists[d][:], in_=pos[d])
+        load_w1(*groups[2])
+        load_w1(*groups[3])
         w2_raw = sb("w2_raw", [P, PACK, H], F32)
         nc.sync.dma_start(out=w2_raw[:], in_=w2.rearrange("(p j) m -> p j m", j=PACK))
 
         ident = sb("ident", [P, P], F32)
         make_identity(nc, ident[:])
-        nc.scalar.activation(out=warm_out[:], in_=ident[:, 0:1], func=ACT.Gelu_apprx_tanh)
 
-        h = [sb("h%d" % t, [P, T + (SPARE if t == 0 else 0)], F32) for t in range(TILES)]
-        nc.gpsimd.memset(h[0][:, T:], 0.0)
+        h = {}
+        neg_gate = {}
 
-        w1_bf = [sb("w1_bf%d" % t, [P, PASSES * P * PACK], BF16) for t in range(TILES)]
+        def pair(name, shape):
+            return psum.tile([P, 2] + shape, F32, name=name, tag="pair")
+
+        def spread_gate(d, spread):
+            for m in range(4):
+                nc.tensor.transpose(spread[:, m, :], gate_cols[d][:, m : m + 1].to_broadcast([P, P]), ident[:])
+
+        def negate_gate(d, spread):
+            nc.scalar.activation(
+                out=neg_gate[d].rearrange("p (n m) -> p n m", m=4),
+                in_=spread.rearrange("p m n -> p n m"),
+                func=ACT.Copy,
+                scale=-1.0,
+            )
+
+        w1_bf = {}
         w1_codes = [sb("w1_codes%d" % t, [P, PASSES * P], U32) for t in range(TILES)]
-        w1_sc = [sb("w1_sc%d" % t, [P, PASSES * P], U8) for t in range(TILES)]
 
-        def round_w1(t, copies):
+        def round_w1(t, copies, tags):
+            rooms = [sb("w1_bf%d_%d" % (t, s), [P, PASSES * P * PACK // len(tags)], BF16, tag=tag) for s, tag in enumerate(tags)]
+            w1_bf[t] = rooms
             for g, copy in enumerate(copies):
+                room = rooms[g][:] if len(tags) == PASSES else rooms[0][:, g * P * PACK : (g + 1) * P * PACK]
                 copy(
-                    out=w1_bf[t][:, g * P * PACK : (g + 1) * P * PACK].rearrange("p (c i j) -> p c j i", i=4, j=PACK),
-                    in_=w1_raw[t][g][:].rearrange("p j (c i) -> p c j i", i=4),
+                    out=room.rearrange("p (c i j) -> p c j i", i=4, j=PACK),
+                    in_=w1_raw[t, g].rearrange("p j (c i) -> p c j i", i=4),
                 )
 
-        def first_layer(t):
-            width = P if t == 0 else PASSES * P
-            for c in range(0, PASSES * P, width):
+        def first_layer(t, u, after=None):
+            scales = sb("w1_sc%d" % t, [P, PASSES * P], U8, tag=after)
+            width = PASSES * P // len(w1_bf[t])
+            for s, room in enumerate(w1_bf[t]):
+                c = s * width
                 nc.vector.quantize_mx(
                     out=w1_codes[t][:, c : c + width].bitcast(FP8X4),
-                    scales=w1_sc[t][:, c : c + width],
-                    in_=w1_bf[t][:, c * PACK : (c + width) * PACK],
+                    scales=scales[:, c : c + width],
+                    in_=room[:],
                 )
-            u = bank(4 + t % 2, "u%d" % t, [P, T])
             for g in range(PASSES):
                 nc.tensor.matmul_mx(
-                    out=u[:],
+                    out=u,
                     lhsT=w1_codes[t][:, g * P : (g + 1) * P].bitcast(FP8X4),
-                    lhsT_scale=w1_sc[t][:, g * P : (g + 1) * P],
+                    lhsT_scale=scales[:, g * P : (g + 1) * P],
                     rhs=x_w[:, g, :].bitcast(FP4X4),
                     rhs_scale=x_sc[:, g * T : (g + 1) * T],
                     start=(g == 0),
                     stop=(g == PASSES - 1),
                 )
-            nc.scalar.activation(out=h[t][:, :T], in_=u[:], func=ACT.Gelu_apprx_tanh)
+            return u
 
-        neg_gate = [sb("neg_gate%d" % d, [P, T], F32) for d in range(D)]
-
-        def negate_on_vector(d):
-            nc.vector.tensor_scalar(out=neg_gate[d][:], in0=gate_raw[d][:], scalar1=-1.0, scalar2=None, op0=ALU.mult)
-
-        def negate_on_scalar(d):
-            nc.scalar.activation(out=neg_gate[d][:], in_=gate_raw[d][:], func=ACT.Copy, scale=-1.0)
+        def activate(t, u, after=None):
+            h[t] = sb("h%d" % t, [P, T + (SPARE if t < 2 else 0)], F32, tag=after)
+            if t < 2:
+                nc.scalar.copy(out=h[t][:, T:], in_=ident[:, :SPARE])
+            nc.scalar.activation(out=h[t][:, :T], in_=u, func=ACT.Gelu_apprx_tanh, bias=warm_in[:] if t == 0 else 0.0)
 
         zT = [sb("zT%d" % c, [P, n // P, 2, 2 * P], BF16) for c, (v0, n) in enumerate(CHUNKS)]
 
-        made = {}
+        def neighbour(t, v0, n, d, sums, term):
+            nc.vector.tensor_tensor(
+                out=term,
+                in0=h[t][:].indirect(lists[d][:, v0 // 16 : (v0 + n) // 16]),
+                in1=neg_gate[d][:, v0 : v0 + n],
+                op=ALU.mult,
+            )
+            for b in range(n // P):
+                if d == 0:
+                    own = h[t][:, v0 + b * P : v0 + (b + 1) * P]
+                    nc.tensor.matmul(sums[b], lhsT=own, rhs=ident[:], start=True, stop=False, is_transpose=True)
+                nc.tensor.matmul(sums[b], lhsT=term[:, b * P : (b + 1) * P], rhs=ident[:], start=False, stop=(d == D - 1), is_transpose=True)
 
-        def room_for(columns, name, after=None):
-            return sb(name, [P, columns], F32, tag=after)[:]
+        def round_z(block, first, sums):
+            c = max(block - 1, 0)
+            count = sums.shape[1] // P
+            nc.scalar.copy(
+                out=zT[c][:, block - CHUNKS[c][0] // P, :, 64 * first : 64 * (first + count)].rearrange("p u (q e) -> p u q e", e=2),
+                in_=sums.rearrange("p (q u e) -> p u q e", u=2, e=2),
+            )
 
-        def run(jobs, room):
-            for t, v0, n, ds, sums in jobs:
-                neighbours(t, v0, n, ds, sums, room[:, : n * len(ds)])
-                room = room[:, n * len(ds) :]
-            return room
-
-        def neighbours(t, v0, n, ds, sums, terms):
-            blocks = range(n // P)
-            for s, d in enumerate(ds):
-                term = terms[:, s * n : (s + 1) * n]
-                made[t, v0, d] = term
-                nc.vector.tensor_tensor(
-                    out=term,
-                    in0=h[t][:].indirect(lists[d][:, v0 // 16 : (v0 + n) // 16]),
-                    in1=neg_gate[d][:, v0 : v0 + n],
-                    op=ALU.mult,
-                )
-                for b in blocks:
-                    if d == 0:
-                        own = h[t][:, v0 + b * P : v0 + (b + 1) * P]
-                        nc.tensor.matmul(sums[b], lhsT=own, rhs=ident[:], start=True, stop=False, is_transpose=True)
-                    part = term[:, b * P : (b + 1) * P]
-                    nc.tensor.matmul(sums[b], lhsT=part, rhs=ident[:], start=False, stop=(d == D - 1), is_transpose=True)
-            if ds[-1] == D - 1:
-                for b in blocks:
-                    block = v0 // P + b
-                    c = max(block - 1, 0)
-                    nc.scalar.copy(
-                        out=zT[c][:, block - CHUNKS[c][0] // P, :, 64 * t : 64 * (t + 1)].rearrange("p u (q e) -> p u q e", e=2),
-                        in_=sums[b].rearrange("p (q u e) -> p u q e", u=2, e=2),
-                    )
-
-        def sum_banks(t, numbers):
-            return [bank(number, "sum%d_%d" % (t, number), [P, P])[:] for number in numbers]
-
-        w2_bf = sb("w2_bf", [P, TILES, P, PACK], BF16)
-        w2_codes = sb("w2_codes", [P, H], U32)
         w2_sc = sb("w2_sc", [P, H], U8)
 
-        def prepare_w2():
-            nc.scalar.copy(
-                out=w2_bf[:].rearrange("p t m j -> p m t j"),
-                in_=w2_raw[:].rearrange("p j (m t) -> p m t j", t=TILES),
-            )
-            nc.vector.quantize_mx(out=w2_codes[:].bitcast(FP8X4), scales=w2_sc[:], in_=w2_bf[:].rearrange("p t m j -> p (t m j)"))
+        def round_w2():
+            w2_bf = sb("w2_bf", [P, TILES, P, PACK], BF16, tag="w1_codes3")
+            for m0 in range(0, P, 64):
+                nc.scalar.copy(
+                    out=w2_bf[:, :, m0 : m0 + 64, :].rearrange("p t m j -> p m t j"),
+                    in_=w2_raw[:, :, TILES * m0 : TILES * (m0 + 64)].rearrange("p j (m t) -> p m t j", t=TILES),
+                )
+            return w2_bf
+
+        def quantise_w2(w2_bf, after):
+            codes = sb("w2_codes", [P, H], U32, tag=after)
+            nc.vector.quantize_mx(out=codes[:].bitcast(FP8X4), scales=w2_sc[:], in_=w2_bf[:].rearrange("p t m j -> p (t m j)"))
+            return codes
 
         y_codes = sb("y_codes", [P, T], U32)
         y_sc = sb("y_sc", [P, T], U8)
@@ -185,7 +196,7 @@ def tile_picked_wlapl_gelu_lo_kernel(tc, x_words, x_scales, w1, w2, gate, pos1, 
         def turn_back(c):
             v0, n = CHUNKS[c]
             words = zT[c][:].bitcast(F32)
-            back = bank((2, 6, 7)[c], "back%d" % c, [P, 2, 2, P])
+            back = bank((0, 1, 5)[c], "back%d" % c, [P, 2, 2, P])
             for b in range(n // P):
                 for u in range(2):
                     nc.tensor.transpose(back[:, b, u, :], words[:, b, u, :], ident[:])
@@ -196,18 +207,24 @@ def tile_picked_wlapl_gelu_lo_kernel(tc, x_words, x_scales, w1, w2, gate, pos1, 
             )
             return z_bf
 
-        def second_layer(c, z_bf):
+        def quantise_z(c, z_bf):
             v0, n = CHUNKS[c]
             z_codes = sb("z_codes%d" % c, [P, n], U32)
             z_sc = sb("z_sc%d" % c, [P, n], U8)
             nc.vector.quantize_mx(out=z_codes[:].bitcast(FP8X4), scales=z_sc[:], in_=z_bf[:])
-            y = sb("y%d" % c, [P, TILES, n], F32)
-            for half in range(2):
-                acc = bank((4, 5, 2, 3, 0, 6)[2 * c + half], "acc%d_%d" % (c, half), [P, 2, 256])
-                for s in range(2):
-                    t = 2 * half + s
+            return z_codes, z_sc
+
+        def second_layer(c, w2_codes, z_codes, z_sc, numbers):
+            v0, n = CHUNKS[c]
+            per_bank = TILES // len(numbers)
+            accs = []
+            both = pair("acc0", [per_bank, n]) if c == 0 else None
+            for half, number in enumerate(numbers):
+                acc = both[:, half] if c == 0 else bank(number, "acc%d_%d" % (c, half), [P, per_bank, n])[:]
+                for s in range(per_bank):
+                    t = per_bank * half + s
                     nc.tensor.matmul_mx(
-                        out=acc[:, s, :n],
+                        out=acc[:, s, :],
                         lhsT=w2_codes[:, t * P : (t + 1) * P].bitcast(FP8X4),
                         lhsT_scale=w2_sc[:, t * P : (t + 1) * P],
                         rhs=z_codes[:].bitcast(FP8X4),
@@ -215,58 +232,107 @@ def tile_picked_wlapl_gelu_lo_kernel(tc, x_words, x_scales, w1, w2, gate, pos1, 
                         start=True,
                         stop=True,
                     )
-                copy = nc.vector.tensor_copy if c > 0 and half == 1 else nc.scalar.copy
-                copy(out=y[:, 2 * half : 2 * half + 2, :], in_=acc[:, :, :n])
+                accs.append(acc)
+            return accs
+
+        def store_y(c, accs, copies):
+            v0, n = CHUNKS[c]
+            y = sb("y%d" % c, [P, TILES, n], F32)
+            per_bank = TILES // len(accs)
+            for half, acc in enumerate(accs):
+                copies[half](out=y[:, per_bank * half : per_bank * (half + 1), :], in_=acc)
             nc.sync.dma_start(out=out_rows[:, :, v0 : v0 + n], in_=y[:])
             return y
 
-        def hand_on(c, y, after=None):
-            v0, n = CHUNKS[c]
-            y_bf = sb("y_bf%d" % c, [P, n * PACK], BF16, tag=after)
-            nc.vector.tensor_copy(
-                out=y_bf[:].rearrange("p (c i t) -> p c t i", i=4, t=TILES),
-                in_=y[:].rearrange("p t (c i) -> p c t i", i=4),
-            )
+        def hand_on(v0, ys):
+            n = sum(y.shape[2] for y in ys)
+            y_bf = sb("y_bf%d" % v0, [P, n * PACK], BF16)
+            at = 0
+            for y in ys:
+                nc.vector.tensor_copy(
+                    out=y_bf[:, at : at + y.shape[2] * PACK].rearrange("p (c i t) -> p c t i", i=4, t=TILES),
+                    in_=y[:].rearrange("p t (c i) -> p c t i", i=4),
+                )
+                at += y.shape[2] * PACK
             nc.vector.quantize_mx(out=y_codes[:, v0 : v0 + n].bitcast(FP8X4), scales=y_sc[:, v0 : v0 + n], in_=y_bf[:])
             nc.sync.dma_start(out=out_words[:, v0 : v0 + n], in_=y_codes[:, v0 : v0 + n].bitcast(I32))
 
-        every = (0, 1, 2, 3)
-        round_w1(0, (on_vector, on_vector))
-        first_layer(0)
-        negate_on_vector(0)
-        negate_on_vector(1)
-        round_w1(1, (on_scalar, on_scalar))
-        first_layer(1)
-        negate_on_scalar(2)
-        negate_on_scalar(3)
-        round_w1(2, (on_scalar, on_scalar))
-        first_layer(2)
-        round_w1(3, (on_scalar, on_scalar))
-        first_layer(3)
-        prepare_w2()
-        sums = sum_banks(0, (0, 1, 2, 3))
-        run([(0, 0, T, (0, 1), sums)], room_for(2 * T, "terms0"))
-        run([(0, 0, T, (2, 3), sums)], room_for(2 * T, "terms1", "w1_bf1"))
-        sums = sum_banks(1, (0, 1, 2))
-        run([(1, 0, 384, (0,), sums)], room_for(384, "terms2"))
-        later = sum_banks(2, (3, 6, 7))
-        run([(1, 0, 384, (1, 2, 3), sums), (2, 0, 384, (0,), later)], room_for(4 * 384, "terms3", "w1_bf2"))
-        run([(2, 0, 384, (1, 2, 3), later)], room_for(3 * 384, "terms4", "w1_bf3"))
-        room = run([(3, 0, 256, every, sum_banks(3, (0, 1)))], room_for(4 * 256 + 10 * 128, "terms5", "w2_bf"))
-        z_bf = turn_back(0)
-        room = run([(3, 256, 128, every, [bank(1, "sum_second", [P, P])[:]])], room)
-        z_next = turn_back(1)
-        third = bank(1, "sum_third", [P, 3, P])
-        run([(1, 384, 128, every, [third[:, 0, :]]), (2, 384, 128, (0, 1), [third[:, 1, :]])], room)
-        y0 = second_layer(0, z_bf)
-        run([(2, 384, 128, (2, 3), [third[:, 1, :]])], room_for(2 * 128, "terms6", "z_bf0"))
-        y1 = second_layer(1, z_next)
-        run([(3, 384, 128, every, [third[:, 2, :]])], room_for(4 * 128, "terms7", "z_bf1"))
-        z_bf = turn_back(2)
-        hand_on(0, y0, after="h3")
-        y2 = second_layer(2, z_bf)
-        hand_on(1, y1, after="z_bf2")
-        hand_on(2, y2)
+        blocks = range(T // P)
+        home, closes = {}, {}
+
+        def sum_bank(number, b, tiles, pieces, sums=None):
+            if sums is None:
+                sums = bank(number, "sums%d_%d" % (b, tiles[0]), [P, len(tiles) * P])[:]
+            for s, t in enumerate(tiles):
+                home[t, b] = sums[:, s * P : (s + 1) * P]
+            at = 0
+            for count in pieces:
+                closes[tiles[at + count - 1], b] = (tiles[at], sums[:, at * P : (at + count) * P])
+                at += count
+
+        for b in range(3):
+            sum_bank(b, b, (0, 1, 2), (3,))
+        sum_bank(3, 3, (0, 1), (2,))
+
+        def gathers(t, v0, n, ds=range(D), after=None):
+            mine = range(v0 // P, (v0 + n) // P)
+            sums = [home[t, b] for b in mine]
+            terms = sb("terms%d_%d_%d" % (t, v0, ds[0]), [P, len(ds) * n], F32, tag=after)
+            for s, d in enumerate(ds):
+                neighbour(t, v0, n, d, sums, terms[:, s * n : (s + 1) * n])
+            for b in mine:
+                if ds[-1] == D - 1 and (t, b) in closes:
+                    round_z(b, *closes[t, b])
+
+        neg_gate[0] = sb("neg_gate0", [P, T], F32)[:]
+        spread = pair("spread0", [4, P])[:, 0]
+        spread_gate(0, spread)
+        negate_gate(0, spread)
+        neg_gate[1] = sb("neg_gate1", [P, T], F32)[:]
+        spread = bank(4, "spread1", [P, 4, P])[:]
+        spread_gate(1, spread)
+        negate_gate(1, spread)
+        round_w1(0, (on_vector, on_vector), (None, None))
+        activate(0, first_layer(0, pair("u0", [T])[:, 0]))
+        round_w1(1, (on_scalar, on_scalar), ("warm_in",))
+        later_gates = sb("later_gates", [P, 2 * T], F32, tag="w1_raw1_1")
+        last_two = pair("spread23", [4, P])
+        for d in range(2, D):
+            spread_gate(d, last_two[:, d - 2])
+        for d in range(2, D):
+            neg_gate[d] = later_gates[:, (d - 2) * T : (d - 1) * T]
+            negate_gate(d, last_two[:, d - 2])
+        gathers(0, 0, T, (0, 1))
+        u = first_layer(1, bank(4, "u1", [P, T])[:])
+        gathers(0, 0, T, (2, 3))
+        round_w1(2, (on_scalar, on_scalar), ("gate_cols0",))
+        activate(1, u, "w1_raw2_1")
+        u = first_layer(2, bank(5, "u2", [P, T])[:])
+        gathers(1, 0, T)
+        round_w1(3, (on_scalar, on_scalar), ("gate_cols0",))
+        activate(2, u, "w1_raw3_1")
+        activate(3, first_layer(3, bank(4, "u3", [P, T])[:]))
+        w2_bf = round_w2()
+        gathers(2, 0, 384)
+        first_two = pair("sums_last01", [T])
+        for b in range(2):
+            sum_bank(None, b, (LAST,), (1,), first_two[:, b, :P])
+        sum_bank(5, 2, (LAST,), (1,))
+        gathers(LAST, 0, 256)
+        z0 = turn_back(0)
+        gathers(LAST, 256, 128)
+        z1 = turn_back(1)
+        sum_bank(0, 3, (2,), (1,))
+        sum_bank(4, 3, (LAST,), (1,))
+        gathers(2, 384, 128)
+        w2_codes = quantise_w2(w2_bf, None)
+        y0 = store_y(0, second_layer(0, w2_codes, *quantise_z(0, z0), (2, 6)), (on_scalar, on_scalar))
+        gathers(LAST, 384, 128, after="z_bf0")
+        y1 = store_y(1, second_layer(1, w2_codes, *quantise_z(1, z1), (2,)), (on_scalar,))
+        z2 = turn_back(2)
+        hand_on(0, [y0])
+        y2 = store_y(2, second_layer(2, w2_codes, *quantise_z(2, z2), (3, 1)), (on_scalar, on_vector))
+        hand_on(256, [y1, y2])
 
         for q in range(4):
             queue = nc.scalar if q % 2 else nc.sync

@@ -46,6 +46,8 @@ def tile_picked_wlapl_gelu_lo_kernel(tc, x_words, x_scales, w1, w2, gate, pos1, 
         warm_in = sb("warm_in", [P, 1], F32)
         warm_out = sb("warm_out", [P, 1], F32)
         nc.gpsimd.memset(warm_in[:], 0.0)
+        zero = sb("zero", [P, 1], F32)
+        nc.gpsimd.memset(zero[:], 0.0)
 
         groups = ((0, 1), (1, 1), (2, 1), (3, 1))
         w1_raw = {}
@@ -67,7 +69,8 @@ def tile_picked_wlapl_gelu_lo_kernel(tc, x_words, x_scales, w1, w2, gate, pos1, 
             for s in range(count):
                 gate_cols[first + s] = cols[:, s, :]
 
-        load_gates(0, D)
+        nc.sync.dma_start(out=lists[0][:], in_=pos[0])
+        load_gates(0, 2)
         load_w1(*groups[0])
         x_w = sb("x_w", [P, PASSES, 2 * T], U8)
         nc.sync.dma_start(out=x_w[:].bitcast(I32), in_=x_words.bitcast(I32).rearrange("g p c -> p g c"))
@@ -78,9 +81,11 @@ def tile_picked_wlapl_gelu_lo_kernel(tc, x_words, x_scales, w1, w2, gate, pos1, 
                 in_=x_scales.bitcast(I32)[:, 4 * q : 4 * q + 4, :].rearrange("g r c -> r g c"),
             )
         nc.scalar.activation(out=warm_out[:], in_=warm_in[:], func=ACT.Gelu_apprx_tanh)
-        nc.sync.dma_start(out=lists[0][:], in_=pos[0])
         load_w1(*groups[1])
-        for d in range(1, D):
+        nc.sync.dma_start(out=lists[1][:], in_=pos[1])
+        gate_raw = sb("gate_raw", [P, 2, T], F32)
+        nc.sync.dma_start(out=gate_raw[:], in_=gate[2:].rearrange("d p v -> p d v"))
+        for d in range(2, D):
             nc.sync.dma_start(out=lists[d][:], in_=pos[d])
         load_w1(*groups[2])
         load_w1(*groups[3])
@@ -146,8 +151,8 @@ def tile_picked_wlapl_gelu_lo_kernel(tc, x_words, x_scales, w1, w2, gate, pos1, 
         def activate(t, u, after=None):
             h[t] = sb("h%d" % t, [P, T + (SPARE if t < 2 else 0)], F32, tag=after)
             if t < 2:
-                nc.scalar.copy(out=h[t][:, T:], in_=ident[:, :SPARE])
-            nc.scalar.activation(out=h[t][:, :T], in_=u, func=ACT.Gelu_apprx_tanh, bias=warm_in[:] if t == 0 else 0.0)
+                nc.gpsimd.memset(h[t][:, T:], 0.0)
+            nc.scalar.activation(out=h[t][:, :T], in_=u, func=ACT.Gelu_apprx_tanh, bias=(warm_in[:], zero[:], 0.0, 0.0)[t])
 
         zT = [sb("zT%d" % c, [P, n // P, 2, 2 * P], BF16) for c, (v0, n) in enumerate(CHUNKS)]
 
@@ -295,23 +300,22 @@ def tile_picked_wlapl_gelu_lo_kernel(tc, x_words, x_scales, w1, w2, gate, pos1, 
         round_w1(0, (on_vector, on_vector), (None, None))
         activate(0, first_layer(0, pair("u0", [T])[:, 0]))
         round_w1(1, (on_scalar, on_scalar), ("warm_in",))
-        later_gates = sb("later_gates", [P, 2 * T], F32, tag="w1_raw1_1")
-        last_two = pair("spread23", [4, P])
-        for d in range(2, D):
-            spread_gate(d, last_two[:, d - 2])
+        later_gates = sb("later_gates", [P, 2 * T], F32, tag="w1_raw1_0")
         for d in range(2, D):
             neg_gate[d] = later_gates[:, (d - 2) * T : (d - 1) * T]
-            negate_gate(d, last_two[:, d - 2])
-        gathers(0, 0, T, (0, 1))
-        u = first_layer(1, bank(4, "u1", [P, T])[:])
+            nc.scalar.activation(out=neg_gate[d], in_=gate_raw[:, d - 2, :], func=ACT.Copy, scale=-1.0)
+        gathers(0, 0, T, (0,))
+        gathers(0, 0, T // 2, (1,))
+        activate(1, first_layer(1, bank(4, "u1", [P, T])[:]))
+        gathers(0, T // 2, T // 2, (1,), "w1_raw1_1")
         gathers(0, 0, T, (2, 3))
-        round_w1(2, (on_scalar, on_scalar), ("gate_cols0",))
-        activate(1, u, "w1_raw2_1")
-        u = first_layer(2, bank(5, "u2", [P, T])[:])
-        gathers(1, 0, T)
-        round_w1(3, (on_scalar, on_scalar), ("gate_cols0",))
-        activate(2, u, "w1_raw3_1")
+        round_w1(2, (on_scalar, on_scalar), ("zero",))
+        gathers(1, 0, T, (0,))
+        activate(2, first_layer(2, bank(5, "u2", [P, T])[:]))
+        gathers(1, 0, T, (1, 2), "w1_raw2_1")
+        round_w1(3, (on_scalar, on_scalar), ("zero",))
         activate(3, first_layer(3, bank(4, "u3", [P, T])[:]))
+        gathers(1, 0, T, (3,), "w1_raw3_1")
         w2_bf = round_w2()
         gathers(2, 0, 384)
         first_two = pair("sums_last01", [T])

@@ -156,14 +156,16 @@ def tile_picked_wlapl_gelu_lo_kernel(tc, x_words, x_scales, w1, w2, gate, pos1, 
 
         zT = [sb("zT%d" % c, [P, n // P, 2, 2 * P], BF16) for c, (v0, n) in enumerate(CHUNKS)]
 
-        def neighbour(t, v0, n, d, sums, term):
+        def neighbour(t, v0, n, d, term):
             nc.vector.tensor_tensor(
                 out=term,
                 in0=h[t][:].indirect(lists[d][:, v0 // 16 : (v0 + n) // 16]),
                 in1=neg_gate[d][:, v0 : v0 + n],
                 op=ALU.mult,
             )
-            for b in range(n // P):
+
+        def add_term(t, v0, d, sums, term, which):
+            for b in which:
                 if d == 0:
                     own = h[t][:, v0 + b * P : v0 + (b + 1) * P]
                     nc.tensor.matmul(sums[b], lhsT=own, rhs=ident[:], start=True, stop=False, is_transpose=True)
@@ -275,16 +277,22 @@ def tile_picked_wlapl_gelu_lo_kernel(tc, x_words, x_scales, w1, w2, gate, pos1, 
                 closes[tiles[at + count - 1], b] = (tiles[at], sums[:, at * P : (at + count) * P])
                 at += count
 
-        for b in range(3):
-            sum_bank(b, b, (0, 1, 2), (3,))
-        sum_bank(3, 3, (0, 1), (2,))
+        for b in blocks:
+            sum_bank(b, b, (0, 1, 2) if b < 2 else (0, 1), (3,) if b < 2 else (2,))
 
-        def gathers(t, v0, n, ds=range(D), after=None):
+        def gathers(t, v0, n, ds=range(D), after=None, block_by_block=False, terms=None):
             mine = range(v0 // P, (v0 + n) // P)
             sums = [home[t, b] for b in mine]
-            terms = sb("terms%d_%d_%d" % (t, v0, ds[0]), [P, len(ds) * n], F32, tag=after)
+            if terms is None:
+                terms = sb("terms%d_%d_%d" % (t, v0, ds[0]), [P, len(ds) * n], F32, tag=after)[:]
             for s, d in enumerate(ds):
-                neighbour(t, v0, n, d, sums, terms[:, s * n : (s + 1) * n])
+                neighbour(t, v0, n, d, terms[:, s * n : (s + 1) * n])
+                if not block_by_block:
+                    add_term(t, v0, d, sums, terms[:, s * n : (s + 1) * n], range(n // P))
+            if block_by_block:
+                for b in range(n // P):
+                    for s, d in enumerate(ds):
+                        add_term(t, v0, d, sums, terms[:, s * n : (s + 1) * n], (b,))
             for b in mine:
                 if ds[-1] == D - 1 and (t, b) in closes:
                     round_z(b, *closes[t, b])
@@ -317,25 +325,29 @@ def tile_picked_wlapl_gelu_lo_kernel(tc, x_words, x_scales, w1, w2, gate, pos1, 
         activate(3, first_layer(3, bank(4, "u3", [P, T])[:]))
         gathers(1, 0, T, (3,), "w1_raw3_1")
         w2_bf = round_w2()
-        gathers(2, 0, 384)
+        gathers(2, 0, 256)
         first_two = pair("sums_last01", [T])
         for b in range(2):
             sum_bank(None, b, (LAST,), (1,), first_two[:, b, :P])
-        sum_bank(5, 2, (LAST,), (1,))
         gathers(LAST, 0, 256)
         z0 = turn_back(0)
-        gathers(LAST, 256, 128)
+        shared = bank(0, "sums_shared", [P, 2, P])
+        for b in range(2, 4):
+            sum_bank(None, b, (2,), (1,), shared[:, b - 2])
+        gathers(2, 256, 256, after="w2_raw", block_by_block=True)
+        w2_codes = quantise_w2(w2_bf, "terms3_0_0")
+        sum_bank(5, 2, (LAST,), (1,))
+        gathers(LAST, 256, 128, (0, 1))
+        y0 = store_y(0, second_layer(0, w2_codes, *quantise_z(0, z0), (6, 7)), (on_scalar, on_scalar))
+        last_terms = sb("last_terms", [P, (2 + D) * P], F32, tag="z_bf0")
+        gathers(LAST, 256, 128, (2, 3), terms=last_terms[:, : 2 * P])
         z1 = turn_back(1)
-        sum_bank(0, 3, (2,), (1,))
         sum_bank(4, 3, (LAST,), (1,))
-        gathers(2, 384, 128)
-        w2_codes = quantise_w2(w2_bf, None)
-        y0 = store_y(0, second_layer(0, w2_codes, *quantise_z(0, z0), (2, 6)), (on_scalar, on_scalar))
-        gathers(LAST, 384, 128, after="z_bf0")
-        y1 = store_y(1, second_layer(1, w2_codes, *quantise_z(1, z1), (2,)), (on_scalar,))
+        gathers(LAST, 384, 128, terms=last_terms[:, 2 * P :])
         z2 = turn_back(2)
         hand_on(0, [y0])
-        y2 = store_y(2, second_layer(2, w2_codes, *quantise_z(2, z2), (3, 1)), (on_scalar, on_vector))
+        y1 = store_y(1, second_layer(1, w2_codes, *quantise_z(1, z1), (4,)), (on_scalar,))
+        y2 = store_y(2, second_layer(2, w2_codes, *quantise_z(2, z2), (3, 2)), (on_scalar, on_vector))
         hand_on(256, [y1, y2])
 
         for q in range(4):

@@ -8,7 +8,11 @@ P = 128
 PACK = 4
 PASSES = K // (P * PACK)
 TILES = H // P
+LAST = TILES - 1
 SPARE = 16
+SPREAD = 2
+
+CHUNKS = ((0, 256), (256, 128), (384, 128))
 
 FLOPS = 2 * K * H * T + 2 * H * H * T
 
@@ -23,9 +27,6 @@ FP4X4 = mybir.dt.float4_e2m1fn_x4
 ACT = mybir.ActivationFunctionType
 ALU = mybir.AluOpType
 
-CHUNKS = ((0, 256), (256, 128), (384, 128))
-LAST = TILES - 1
-
 
 def tile_picked_wlapl_gelu_lo_kernel(tc, x_words, x_scales, w1, w2, gate, pos1, pos2, pos3, pos4, out_0, out_1, out_2):
     nc = tc.nc
@@ -34,44 +35,34 @@ def tile_picked_wlapl_gelu_lo_kernel(tc, x_words, x_scales, w1, w2, gate, pos1, 
         keep = ctx.enter_context(tc.tile_pool(name="keep", bufs=1))
         psum = ctx.enter_context(tc.psum_pool(name="psum", bufs=1))
 
-        def sb(name, shape, dtype, tag=None):
-            return keep.tile(shape, dtype, name=name, tag=tag or name, align_bytes=64)
+        def sb(name, shape, dtype, room=None):
+            return keep.tile(shape, dtype, name=name, tag=room or name, align_bytes=64)
 
         def bank(number, name, shape):
             return psum.tile(shape, F32, name=name, tag="bank%d" % number)
 
+        def pair(name, shape):
+            return psum.tile([P, 2] + shape, F32, name=name, tag="pair")
+
         lists = [keep.tile([P, T // 16], U16, name="list%d" % d) for d in range(D)]
         x_sc = sb("x_sc", [P, PASSES * T], U8)
         nc.gpsimd.memset(x_sc[:].bitcast(I32), 0)
-        warm_in = sb("warm_in", [P, 1], F32)
-        warm_out = sb("warm_out", [P, 1], F32)
-        nc.gpsimd.memset(warm_in[:], 0.0)
-        zero = sb("zero", [P, 1], F32)
-        nc.gpsimd.memset(zero[:], 0.0)
+        bias = [sb("bias%d" % t, [P, 1], F32) for t in range(2)]
+        nc.gpsimd.memset(bias[0][:], 0.0)
 
-        groups = ((0, 1), (1, 1), (2, 1), (3, 1))
         w1_raw = {}
 
-        def load_w1(first, count, passes=range(PASSES)):
-            for g in passes:
-                raw = sb("w1_raw%d_%d" % (first, g), [P, PACK, count * P], F32)
-                rows = w1[g * P * PACK : (g + 1) * P * PACK, first * P : (first + count) * P]
-                nc.sync.dma_start(out=raw[:], in_=rows.rearrange("(p j) c -> p j c", j=PACK))
-                for s in range(count):
-                    w1_raw[first + s, g] = raw[:, :, s * P : (s + 1) * P]
+        def load_w1(t):
+            for g in range(PASSES):
+                w1_raw[t, g] = sb("w1_raw%d_%d" % (t, g), [P, PACK, P], F32)
+                rows = w1[g * P * PACK : (g + 1) * P * PACK, t * P : (t + 1) * P]
+                nc.sync.dma_start(out=w1_raw[t, g][:], in_=rows.rearrange("(p j) c -> p j c", j=PACK))
 
         pos = (pos1, pos2, pos3, pos4)
-        gate_cols = {}
-
-        def load_gates(first, count):
-            cols = sb("gate_cols%d" % first, [P, count, 4], F32)
-            nc.sync.dma_start(out=cols[:], in_=gate[first : first + count, 0, :].rearrange("d (n m) -> n d m", m=4))
-            for s in range(count):
-                gate_cols[first + s] = cols[:, s, :]
-
         nc.sync.dma_start(out=lists[0][:], in_=pos[0])
-        load_gates(0, 2)
-        load_w1(*groups[0])
+        gate_cols = sb("gate_cols", [P, SPREAD, 4], F32)
+        nc.sync.dma_start(out=gate_cols[:], in_=gate[:SPREAD, 0, :].rearrange("d (n m) -> n d m", m=4))
+        load_w1(0)
         x_w = sb("x_w", [P, PASSES, 2 * T], U8)
         nc.sync.dma_start(out=x_w[:].bitcast(I32), in_=x_words.bitcast(I32).rearrange("g p c -> p g c"))
         x_sc_rows = x_sc[:].bitcast(I32).rearrange("p (g c) -> p g c", g=PASSES)
@@ -80,32 +71,27 @@ def tile_picked_wlapl_gelu_lo_kernel(tc, x_words, x_scales, w1, w2, gate, pos1, 
                 out=x_sc_rows[32 * q : 32 * q + 4],
                 in_=x_scales.bitcast(I32)[:, 4 * q : 4 * q + 4, :].rearrange("g r c -> r g c"),
             )
-        nc.scalar.activation(out=warm_out[:], in_=warm_in[:], func=ACT.Gelu_apprx_tanh)
-        load_w1(*groups[1])
+        nc.scalar.activation(out=bias[1][:], in_=bias[0][:], func=ACT.Gelu_apprx_tanh)
+        load_w1(1)
         nc.sync.dma_start(out=lists[1][:], in_=pos[1])
-        gate_raw = sb("gate_raw", [P, 2, T], F32)
-        nc.sync.dma_start(out=gate_raw[:], in_=gate[2:].rearrange("d p v -> p d v"))
+        gate_raw = sb("gate_raw", [P, D - SPREAD, T], F32)
+        nc.sync.dma_start(out=gate_raw[:], in_=gate[SPREAD:].rearrange("d p v -> p d v"))
         for d in range(2, D):
             nc.sync.dma_start(out=lists[d][:], in_=pos[d])
-        load_w1(*groups[2])
-        load_w1(*groups[3])
+        load_w1(2)
+        load_w1(3)
         w2_raw = sb("w2_raw", [P, PACK, H], F32)
         nc.sync.dma_start(out=w2_raw[:], in_=w2.rearrange("(p j) m -> p j m", j=PACK))
 
         ident = sb("ident", [P, P], F32)
         make_identity(nc, ident[:])
 
-        h = {}
         neg_gate = {}
 
-        def pair(name, shape):
-            return psum.tile([P, 2] + shape, F32, name=name, tag="pair")
-
         def spread_gate(d, spread):
+            neg_gate[d] = sb("neg_gate%d" % d, [P, T], F32)[:]
             for m in range(4):
-                nc.tensor.transpose(spread[:, m, :], gate_cols[d][:, m : m + 1].to_broadcast([P, P]), ident[:])
-
-        def negate_gate(d, spread):
+                nc.tensor.transpose(spread[:, m, :], gate_cols[:, d, m : m + 1].to_broadcast([P, P]), ident[:])
             nc.scalar.activation(
                 out=neg_gate[d].rearrange("p (n m) -> p n m", m=4),
                 in_=spread.rearrange("p m n -> p n m"),
@@ -113,29 +99,39 @@ def tile_picked_wlapl_gelu_lo_kernel(tc, x_words, x_scales, w1, w2, gate, pos1, 
                 scale=-1.0,
             )
 
-        w1_bf = {}
+        def negate_loaded_gates(room):
+            negated = sb("later_gates", [P, (D - SPREAD) * T], F32, room)
+            for s in range(D - SPREAD):
+                neg_gate[SPREAD + s] = negated[:, s * T : (s + 1) * T]
+                nc.scalar.activation(out=neg_gate[SPREAD + s], in_=gate_raw[:, s, :], func=ACT.Copy, scale=-1.0)
+
         w1_codes = [sb("w1_codes%d" % t, [P, PASSES * P], U32) for t in range(TILES)]
+        h = {}
 
-        def round_w1(t, copies, tags):
-            rooms = [sb("w1_bf%d_%d" % (t, s), [P, PASSES * P * PACK // len(tags)], BF16, tag=tag) for s, tag in enumerate(tags)]
-            w1_bf[t] = rooms
-            for g, copy in enumerate(copies):
-                room = rooms[g][:] if len(tags) == PASSES else rooms[0][:, g * P * PACK : (g + 1) * P * PACK]
-                copy(
-                    out=room.rearrange("p (c i j) -> p c j i", i=4, j=PACK),
-                    in_=w1_raw[t, g].rearrange("p j (c i) -> p c j i", i=4),
-                )
+        def round_pass(copy, t, g, rounded):
+            copy(
+                out=rounded.rearrange("p (c i j) -> p c j i", i=4, j=PACK),
+                in_=w1_raw[t, g][:].rearrange("p j (c i) -> p c j i", i=4),
+            )
 
-        def first_layer(t, u, after=None):
-            scales = sb("w1_sc%d" % t, [P, PASSES * P], U8, tag=after)
-            width = PASSES * P // len(w1_bf[t])
-            for s, room in enumerate(w1_bf[t]):
-                c = s * width
-                nc.vector.quantize_mx(
-                    out=w1_codes[t][:, c : c + width].bitcast(FP8X4),
-                    scales=scales[:, c : c + width],
-                    in_=room[:],
-                )
+        def round_first_tile():
+            pieces = [sb("w1_bf0_%d" % g, [P, P * PACK], BF16) for g in range(PASSES)]
+            for g in range(PASSES):
+                round_pass(on_vector, 0, g, pieces[g][:])
+            return pieces
+
+        def round_later_tile(t, room):
+            rounded = sb("w1_bf%d" % t, [P, PASSES * P * PACK], BF16, room)
+            for g in range(PASSES):
+                round_pass(on_scalar, t, g, rounded[:, g * P * PACK : (g + 1) * P * PACK])
+            return [rounded]
+
+        def first_layer(t, pieces, u):
+            scales = sb("w1_sc%d" % t, [P, PASSES * P], U8)
+            width = PASSES * P // len(pieces)
+            for s, piece in enumerate(pieces):
+                cols = slice(s * width, (s + 1) * width)
+                nc.vector.quantize_mx(out=w1_codes[t][:, cols].bitcast(FP8X4), scales=scales[:, cols], in_=piece[:])
             for g in range(PASSES):
                 nc.tensor.matmul_mx(
                     out=u,
@@ -146,64 +142,68 @@ def tile_picked_wlapl_gelu_lo_kernel(tc, x_words, x_scales, w1, w2, gate, pos1, 
                     start=(g == 0),
                     stop=(g == PASSES - 1),
                 )
-            return u
-
-        def activate(t, u, after=None):
-            h[t] = sb("h%d" % t, [P, T + (SPARE if t < 2 else 0)], F32, tag=after)
-            if t < 2:
+            whole = t < 2
+            h[t] = sb("h%d" % t, [P, T + (SPARE if whole else 0)], F32)
+            if whole:
                 nc.gpsimd.memset(h[t][:, T:], 0.0)
-            nc.scalar.activation(out=h[t][:, :T], in_=u, func=ACT.Gelu_apprx_tanh, bias=(warm_in[:], zero[:], 0.0, 0.0)[t])
+            nc.scalar.activation(out=h[t][:, :T], in_=u, func=ACT.Gelu_apprx_tanh, bias=bias[t][:] if whole else 0.0)
 
         zT = [sb("zT%d" % c, [P, n // P, 2, 2 * P], BF16) for c, (v0, n) in enumerate(CHUNKS)]
+        home = {}
+        closes = {}
 
-        def neighbour(t, v0, n, d, term):
-            nc.vector.tensor_tensor(
-                out=term,
-                in0=h[t][:].indirect(lists[d][:, v0 // 16 : (v0 + n) // 16]),
-                in1=neg_gate[d][:, v0 : v0 + n],
-                op=ALU.mult,
-            )
+        def sums_in(columns, block, tiles):
+            for s, t in enumerate(tiles):
+                home[t, block] = columns[:, s * P : (s + 1) * P]
+            closes[tiles[-1], block] = (tiles[0], columns)
 
-        def add_term(t, v0, d, sums, term, which):
-            for b in which:
-                if d == 0:
-                    own = h[t][:, v0 + b * P : v0 + (b + 1) * P]
-                    nc.tensor.matmul(sums[b], lhsT=own, rhs=ident[:], start=True, stop=False, is_transpose=True)
-                nc.tensor.matmul(sums[b], lhsT=term[:, b * P : (b + 1) * P], rhs=ident[:], start=False, stop=(d == D - 1), is_transpose=True)
+        def add_term(t, block, d, term):
+            if d == 0:
+                own = h[t][:, block * P : (block + 1) * P]
+                nc.tensor.matmul(home[t, block], lhsT=own, rhs=ident[:], start=True, stop=False, is_transpose=True)
+            nc.tensor.matmul(home[t, block], lhsT=term, rhs=ident[:], start=False, stop=(d == D - 1), is_transpose=True)
 
-        def round_z(block, first, sums):
+        def round_z(block, first, columns):
             c = max(block - 1, 0)
-            count = sums.shape[1] // P
+            words = slice(64 * first, 64 * (first + columns.shape[1] // P))
             nc.scalar.copy(
-                out=zT[c][:, block - CHUNKS[c][0] // P, :, 64 * first : 64 * (first + count)].rearrange("p u (q e) -> p u q e", e=2),
-                in_=sums.rearrange("p (q u e) -> p u q e", u=2, e=2),
+                out=zT[c][:, block - CHUNKS[c][0] // P, :, words].rearrange("p u (q e) -> p u q e", e=2),
+                in_=columns.rearrange("p (q u e) -> p u q e", u=2, e=2),
             )
 
-        w2_sc = sb("w2_sc", [P, H], U8)
+        def terms_tile(name, columns, room=None):
+            return sb(name, [P, columns], F32, room)[:]
 
-        def round_w2():
-            w2_bf = sb("w2_bf", [P, TILES, P, PACK], BF16, tag="w1_codes3")
-            for m0 in range(0, P, 64):
-                nc.scalar.copy(
-                    out=w2_bf[:, :, m0 : m0 + 64, :].rearrange("p t m j -> p m t j"),
-                    in_=w2_raw[:, :, TILES * m0 : TILES * (m0 + 64)].rearrange("p j (m t) -> p m t j", t=TILES),
+        def gathers(t, v0, n, ds, terms, one_bank=False):
+            mine = range(v0 // P, (v0 + n) // P)
+
+            def part(s, block):
+                at = s * n + block * P - v0
+                return terms[:, at : at + P]
+
+            for s, d in enumerate(ds):
+                nc.vector.tensor_tensor(
+                    out=terms[:, s * n : (s + 1) * n],
+                    in0=h[t][:].indirect(lists[d][:, v0 // 16 : (v0 + n) // 16]),
+                    in1=neg_gate[d][:, v0 : v0 + n],
+                    op=ALU.mult,
                 )
-            return w2_bf
+                if not one_bank:
+                    for block in mine:
+                        add_term(t, block, d, part(s, block))
+            if one_bank:
+                for block in mine:
+                    for s, d in enumerate(ds):
+                        add_term(t, block, d, part(s, block))
+            if ds[-1] == D - 1:
+                for block in mine:
+                    if (t, block) in closes:
+                        round_z(block, *closes[t, block])
 
-        def quantise_w2(w2_bf, after):
-            codes = sb("w2_codes", [P, H], U32, tag=after)
-            nc.vector.quantize_mx(out=codes[:].bitcast(FP8X4), scales=w2_sc[:], in_=w2_bf[:].rearrange("p t m j -> p (t m j)"))
-            return codes
-
-        y_codes = sb("y_codes", [P, T], U32)
-        y_sc = sb("y_sc", [P, T], U8)
-        out_rows = out_0.rearrange("(p t) v -> p t v", t=TILES)
-        out_words = out_1[0].rearrange("p v r -> p (v r)").bitcast(I32)
-
-        def turn_back(c):
-            v0, n = CHUNKS[c]
+        def turn_back(c, number):
+            n = CHUNKS[c][1]
             words = zT[c][:].bitcast(F32)
-            back = bank((0, 1, 5)[c], "back%d" % c, [P, 2, 2, P])
+            back = bank(number, "back%d" % c, [P, 2, 2, P])
             for b in range(n // P):
                 for u in range(2):
                     nc.tensor.transpose(back[:, b, u, :], words[:, b, u, :], ident[:])
@@ -214,141 +214,115 @@ def tile_picked_wlapl_gelu_lo_kernel(tc, x_words, x_scales, w1, w2, gate, pos1, 
             )
             return z_bf
 
-        def quantise_z(c, z_bf):
+        w2_sc = sb("w2_sc", [P, H], U8)
+
+        def round_w2(room):
+            w2_bf = sb("w2_bf", [P, TILES, P, PACK], BF16, room)
+            for m0 in range(0, P, P // 2):
+                nc.scalar.copy(
+                    out=w2_bf[:, :, m0 : m0 + P // 2, :].rearrange("p t m j -> p m t j"),
+                    in_=w2_raw[:, :, TILES * m0 : TILES * (m0 + P // 2)].rearrange("p j (m t) -> p m t j", t=TILES),
+                )
+            return w2_bf
+
+        y_codes = sb("y_codes", [P, T], U32)
+        y_sc = sb("y_sc", [P, T], U8)
+        out_rows = out_0.rearrange("(p t) v -> p t v", t=TILES)
+        out_words = out_1[0].rearrange("p v r -> p (v r)").bitcast(I32)
+
+        def second_layer(c, w2_codes, z_bf, make_accs, copies):
             v0, n = CHUNKS[c]
             z_codes = sb("z_codes%d" % c, [P, n], U32)
             z_sc = sb("z_sc%d" % c, [P, n], U8)
             nc.vector.quantize_mx(out=z_codes[:].bitcast(FP8X4), scales=z_sc[:], in_=z_bf[:])
-            return z_codes, z_sc
-
-        def second_layer(c, w2_codes, z_codes, z_sc, numbers):
-            v0, n = CHUNKS[c]
-            per_bank = TILES // len(numbers)
-            accs = []
-            both = pair("acc0", [per_bank, n]) if c == 0 else None
-            for half, number in enumerate(numbers):
-                acc = both[:, half] if c == 0 else bank(number, "acc%d_%d" % (c, half), [P, per_bank, n])[:]
-                for s in range(per_bank):
-                    t = per_bank * half + s
-                    nc.tensor.matmul_mx(
-                        out=acc[:, s, :],
-                        lhsT=w2_codes[:, t * P : (t + 1) * P].bitcast(FP8X4),
-                        lhsT_scale=w2_sc[:, t * P : (t + 1) * P],
-                        rhs=z_codes[:].bitcast(FP8X4),
-                        rhs_scale=z_sc[:],
-                        start=True,
-                        stop=True,
-                    )
-                accs.append(acc)
-            return accs
-
-        def store_y(c, accs, copies):
-            v0, n = CHUNKS[c]
+            per_bank = TILES // len(copies)
+            accs = make_accs([per_bank, n])
+            for t in range(TILES):
+                nc.tensor.matmul_mx(
+                    out=accs[t // per_bank][:, t % per_bank, :],
+                    lhsT=w2_codes[:, t * P : (t + 1) * P].bitcast(FP8X4),
+                    lhsT_scale=w2_sc[:, t * P : (t + 1) * P],
+                    rhs=z_codes[:].bitcast(FP8X4),
+                    rhs_scale=z_sc[:],
+                    start=True,
+                    stop=True,
+                )
             y = sb("y%d" % c, [P, TILES, n], F32)
-            per_bank = TILES // len(accs)
-            for half, acc in enumerate(accs):
-                copies[half](out=y[:, per_bank * half : per_bank * (half + 1), :], in_=acc)
+            for s, copy in enumerate(copies):
+                copy(out=y[:, per_bank * s : per_bank * (s + 1), :], in_=accs[s])
             nc.sync.dma_start(out=out_rows[:, :, v0 : v0 + n], in_=y[:])
             return y
 
-        def hand_on(v0, ys):
-            n = sum(y.shape[2] for y in ys)
-            y_bf = sb("y_bf%d" % v0, [P, n * PACK], BF16)
-            at = 0
-            for y in ys:
-                nc.vector.tensor_copy(
-                    out=y_bf[:, at : at + y.shape[2] * PACK].rearrange("p (c i t) -> p c t i", i=4, t=TILES),
-                    in_=y[:].rearrange("p t (c i) -> p c t i", i=4),
-                )
-                at += y.shape[2] * PACK
+        def in_pair(shape):
+            both = pair("acc_pair", shape)
+            return [both[:, 0], both[:, 1]]
+
+        def in_banks(*numbers):
+            return lambda shape: [bank(number, "acc%d" % number, [P] + shape)[:] for number in numbers]
+
+        def hand_on(c, y):
+            v0, n = CHUNKS[c]
+            y_bf = sb("y_bf%d" % c, [P, n * PACK], BF16)
+            nc.vector.tensor_copy(
+                out=y_bf[:].rearrange("p (c i t) -> p c t i", i=4, t=TILES),
+                in_=y[:].rearrange("p t (c i) -> p c t i", i=4),
+            )
             nc.vector.quantize_mx(out=y_codes[:, v0 : v0 + n].bitcast(FP8X4), scales=y_sc[:, v0 : v0 + n], in_=y_bf[:])
             nc.sync.dma_start(out=out_words[:, v0 : v0 + n], in_=y_codes[:, v0 : v0 + n].bitcast(I32))
 
-        blocks = range(T // P)
-        home, closes = {}, {}
+        every = tuple(range(D))
+        half = T // 2
+        for block in range(T // P):
+            tiles = (0, 1, 2) if block < 2 else (0, 1)
+            sums_in(bank(block, "sums%d" % block, [P, len(tiles) * P])[:], block, tiles)
 
-        def sum_bank(number, b, tiles, pieces, sums=None):
-            if sums is None:
-                sums = bank(number, "sums%d_%d" % (b, tiles[0]), [P, len(tiles) * P])[:]
-            for s, t in enumerate(tiles):
-                home[t, b] = sums[:, s * P : (s + 1) * P]
-            at = 0
-            for count in pieces:
-                closes[tiles[at + count - 1], b] = (tiles[at], sums[:, at * P : (at + count) * P])
-                at += count
+        spread_gate(0, pair("spread0", [4, P])[:, 0])
+        spread_gate(1, bank(4, "spread1", [P, 4, P])[:])
+        first_layer(0, round_first_tile(), pair("u0", [T])[:, 0])
 
-        for b in blocks:
-            sum_bank(b, b, (0, 1, 2) if b < 2 else (0, 1), (3,) if b < 2 else (2,))
+        rounded = round_later_tile(1, "bias0")
+        negate_loaded_gates("w1_raw1_0")
+        gathers(0, 0, T, (0,), terms_tile("terms0a", T))
+        gathers(0, 0, half, (1,), terms_tile("terms0b", half))
+        first_layer(1, rounded, bank(4, "u1", [P, T])[:])
+        gathers(0, half, half, (1,), terms_tile("terms0c", half, "w1_raw1_1"))
+        gathers(0, 0, T, (2, 3), terms_tile("terms0d", 2 * T))
 
-        def gathers(t, v0, n, ds=range(D), after=None, block_by_block=False, terms=None):
-            mine = range(v0 // P, (v0 + n) // P)
-            sums = [home[t, b] for b in mine]
-            if terms is None:
-                terms = sb("terms%d_%d_%d" % (t, v0, ds[0]), [P, len(ds) * n], F32, tag=after)[:]
-            for s, d in enumerate(ds):
-                neighbour(t, v0, n, d, terms[:, s * n : (s + 1) * n])
-                if not block_by_block:
-                    add_term(t, v0, d, sums, terms[:, s * n : (s + 1) * n], range(n // P))
-            if block_by_block:
-                for b in range(n // P):
-                    for s, d in enumerate(ds):
-                        add_term(t, v0, d, sums, terms[:, s * n : (s + 1) * n], (b,))
-            for b in mine:
-                if ds[-1] == D - 1 and (t, b) in closes:
-                    round_z(b, *closes[t, b])
+        rounded = round_later_tile(2, "bias1")
+        gathers(1, 0, T, (0,), terms_tile("terms1a", T))
+        first_layer(2, rounded, bank(5, "u2", [P, T])[:])
+        gathers(1, 0, T, (1,), terms_tile("terms1b", T, "w1_raw2_1"))
+        first_layer(3, round_later_tile(3, "w1_raw2_0"), bank(4, "u3", [P, T])[:])
+        gathers(1, 0, T, (2, 3), terms_tile("terms1c", 2 * T, "w1_raw3_1"))
+        w2_bf = round_w2("w1_codes3")
 
-        neg_gate[0] = sb("neg_gate0", [P, T], F32)[:]
-        spread = pair("spread0", [4, P])[:, 0]
-        spread_gate(0, spread)
-        negate_gate(0, spread)
-        neg_gate[1] = sb("neg_gate1", [P, T], F32)[:]
-        spread = bank(4, "spread1", [P, 4, P])[:]
-        spread_gate(1, spread)
-        negate_gate(1, spread)
-        round_w1(0, (on_vector, on_vector), (None, None))
-        activate(0, first_layer(0, pair("u0", [T])[:, 0]))
-        round_w1(1, (on_scalar, on_scalar), ("warm_in",))
-        later_gates = sb("later_gates", [P, 2 * T], F32, tag="w1_raw1_0")
-        for d in range(2, D):
-            neg_gate[d] = later_gates[:, (d - 2) * T : (d - 1) * T]
-            nc.scalar.activation(out=neg_gate[d], in_=gate_raw[:, d - 2, :], func=ACT.Copy, scale=-1.0)
-        gathers(0, 0, T, (0,))
-        gathers(0, 0, T // 2, (1,))
-        activate(1, first_layer(1, bank(4, "u1", [P, T])[:]))
-        gathers(0, T // 2, T // 2, (1,), "w1_raw1_1")
-        gathers(0, 0, T, (2, 3))
-        round_w1(2, (on_scalar, on_scalar), ("zero",))
-        gathers(1, 0, T, (0,))
-        activate(2, first_layer(2, bank(5, "u2", [P, T])[:]))
-        gathers(1, 0, T, (1, 2), "w1_raw2_1")
-        round_w1(3, (on_scalar, on_scalar), ("zero",))
-        activate(3, first_layer(3, bank(4, "u3", [P, T])[:]))
-        gathers(1, 0, T, (3,), "w1_raw3_1")
-        w2_bf = round_w2()
-        gathers(2, 0, 256)
-        first_two = pair("sums_last01", [T])
-        for b in range(2):
-            sum_bank(None, b, (LAST,), (1,), first_two[:, b, :P])
-        gathers(LAST, 0, 256)
-        z0 = turn_back(0)
+        gathers(2, 0, half, every, terms_tile("terms2a", D * half))
+        last_sums = pair("last_sums", [T])
+        for block in range(2):
+            sums_in(last_sums[:, block, :P], block, (LAST,))
+        gathers(LAST, 0, half, every, terms_tile("terms3a", D * half))
+        z_first = turn_back(0, 0)
+
         shared = bank(0, "sums_shared", [P, 2, P])
-        for b in range(2, 4):
-            sum_bank(None, b, (2,), (1,), shared[:, b - 2])
-        gathers(2, 256, 256, after="w2_raw", block_by_block=True)
-        w2_codes = quantise_w2(w2_bf, "terms3_0_0")
-        sum_bank(5, 2, (LAST,), (1,))
-        gathers(LAST, 256, 128, (0, 1))
-        y0 = store_y(0, second_layer(0, w2_codes, *quantise_z(0, z0), (6, 7)), (on_scalar, on_scalar))
-        last_terms = sb("last_terms", [P, (2 + D) * P], F32, tag="z_bf0")
-        gathers(LAST, 256, 128, (2, 3), terms=last_terms[:, : 2 * P])
-        z1 = turn_back(1)
-        sum_bank(4, 3, (LAST,), (1,))
-        gathers(LAST, 384, 128, terms=last_terms[:, 2 * P :])
-        z2 = turn_back(2)
-        hand_on(0, [y0])
-        y1 = store_y(1, second_layer(1, w2_codes, *quantise_z(1, z1), (4,)), (on_scalar,))
-        y2 = store_y(2, second_layer(2, w2_codes, *quantise_z(2, z2), (3, 2)), (on_scalar, on_vector))
-        hand_on(256, [y1, y2])
+        for block in range(2, 4):
+            sums_in(shared[:, block - 2], block, (2,))
+        gathers(2, half, half, every, terms_tile("terms2b", D * half, "w2_raw"), one_bank=True)
+        w2_codes = sb("w2_codes", [P, H], U32, "terms3a")
+        nc.vector.quantize_mx(out=w2_codes[:].bitcast(FP8X4), scales=w2_sc[:], in_=w2_bf[:].rearrange("p t m j -> p (t m j)"))
+
+        sums_in(bank(5, "sums_second", [P, P])[:], 2, (LAST,))
+        gathers(LAST, CHUNKS[1][0], P, (0, 1), terms_tile("terms3b", 2 * P))
+        y_first = second_layer(0, w2_codes, z_first, in_pair, (on_scalar, on_scalar))
+        last_terms = terms_tile("terms3c", (2 + D) * P, "z_bf0")
+        gathers(LAST, CHUNKS[1][0], P, (2, 3), last_terms[:, : 2 * P])
+        z_second = turn_back(1, 1)
+        sums_in(bank(4, "sums_third", [P, P])[:], 3, (LAST,))
+        gathers(LAST, CHUNKS[2][0], P, every, last_terms[:, 2 * P :])
+        z_third = turn_back(2, 5)
+
+        hand_on(0, y_first)
+        hand_on(1, second_layer(1, w2_codes, z_second, in_banks(4), (on_scalar,)))
+        hand_on(2, second_layer(2, w2_codes, z_third, in_banks(3, 2), (on_scalar, on_vector)))
 
         for q in range(4):
             queue = nc.scalar if q % 2 else nc.sync

@@ -174,13 +174,8 @@ def tile_picked_wlapl_gelu_lo_kernel(tc, x_words, x_scales, w1, w2, gate, pos1, 
         def terms_tile(name, columns, room=None):
             return sb(name, [P, columns], F32, room)[:]
 
-        def gathers(t, v0, n, ds, terms, one_bank=False):
+        def gathers(t, v0, n, ds, terms):
             mine = range(v0 // P, (v0 + n) // P)
-
-            def part(s, block):
-                at = s * n + block * P - v0
-                return terms[:, at : at + P]
-
             for s, d in enumerate(ds):
                 nc.vector.tensor_tensor(
                     out=terms[:, s * n : (s + 1) * n],
@@ -188,30 +183,25 @@ def tile_picked_wlapl_gelu_lo_kernel(tc, x_words, x_scales, w1, w2, gate, pos1, 
                     in1=neg_gate[d][:, v0 : v0 + n],
                     op=ALU.mult,
                 )
-                if not one_bank:
-                    for block in mine:
-                        add_term(t, block, d, part(s, block))
-            if one_bank:
                 for block in mine:
-                    for s, d in enumerate(ds):
-                        add_term(t, block, d, part(s, block))
+                    at = s * n + block * P - v0
+                    add_term(t, block, d, terms[:, at : at + P])
             if ds[-1] == D - 1:
                 for block in mine:
                     if (t, block) in closes:
                         round_z(block, *closes[t, block])
 
-        def turn_back(c, number):
-            n = CHUNKS[c][1]
+        def turn_back(c, numbers):
             words = zT[c][:].bitcast(F32)
-            back = bank(number, "back%d" % c, [P, 2, 2, P])
-            for b in range(n // P):
+            z_bf = sb("z_bf%d" % c, [P, CHUNKS[c][1] * PACK], BF16)
+            for b, number in enumerate(numbers):
+                back = bank(number, "back%d_%d" % (c, b), [P, 2, P])
                 for u in range(2):
-                    nc.tensor.transpose(back[:, b, u, :], words[:, b, u, :], ident[:])
-            z_bf = sb("z_bf%d" % c, [P, n * PACK], BF16)
-            nc.scalar.copy(
-                out=z_bf[:].bitcast(F32).rearrange("p (b v u) -> p b v u", v=P, u=2),
-                in_=back[:, : n // P].rearrange("p b u v -> p b v u"),
-            )
+                    nc.tensor.transpose(back[:, u, :], words[:, b, u, :], ident[:])
+                nc.scalar.copy(
+                    out=z_bf[:, b * P * PACK : (b + 1) * P * PACK].bitcast(F32).rearrange("p (v u) -> p v u", u=2),
+                    in_=back[:].rearrange("p u v -> p v u"),
+                )
             return z_bf
 
         w2_sc = sb("w2_sc", [P, H], U8)
@@ -301,24 +291,22 @@ def tile_picked_wlapl_gelu_lo_kernel(tc, x_words, x_scales, w1, w2, gate, pos1, 
         for block in range(2):
             sums_in(last_sums[:, block, :P], block, (LAST,))
         gathers(LAST, 0, half, every, terms_tile("terms3a", D * half))
-        z_first = turn_back(0, 0)
+        z_first = turn_back(0, (0, 1))
 
-        shared = bank(0, "sums_shared", [P, 2, P])
         for block in range(2, 4):
-            sums_in(shared[:, block - 2], block, (2,))
-        gathers(2, half, half, every, terms_tile("terms2b", D * half, "w2_raw"), one_bank=True)
+            sums_in(bank(block - 2, "sums_rest%d" % block, [P, P])[:], block, (2,))
+        gathers(2, half, half, every, terms_tile("terms2b", D * half, "w2_raw"))
         w2_codes = sb("w2_codes", [P, H], U32, "terms3a")
         nc.vector.quantize_mx(out=w2_codes[:].bitcast(FP8X4), scales=w2_sc[:], in_=w2_bf[:].rearrange("p t m j -> p (t m j)"))
 
-        sums_in(bank(5, "sums_second", [P, P])[:], 2, (LAST,))
-        gathers(LAST, CHUNKS[1][0], P, (0, 1), terms_tile("terms3b", 2 * P))
         y_first = second_layer(0, w2_codes, z_first, in_pair, (on_scalar, on_scalar))
-        last_terms = terms_tile("terms3c", (2 + D) * P, "z_bf0")
-        gathers(LAST, CHUNKS[1][0], P, (2, 3), last_terms[:, : 2 * P])
-        z_second = turn_back(1, 1)
+        last_terms = terms_tile("terms3b", 2 * D * P, "z_bf0")
+        sums_in(bank(5, "sums_second", [P, P])[:], 2, (LAST,))
+        gathers(LAST, CHUNKS[1][0], P, every, last_terms[:, : D * P])
+        z_second = turn_back(1, (2,))
         sums_in(bank(4, "sums_third", [P, P])[:], 3, (LAST,))
-        gathers(LAST, CHUNKS[2][0], P, every, last_terms[:, 2 * P :])
-        z_third = turn_back(2, 5)
+        gathers(LAST, CHUNKS[2][0], P, every, last_terms[:, D * P :])
+        z_third = turn_back(2, (5,))
 
         hand_on(0, y_first)
         hand_on(1, second_layer(1, w2_codes, z_second, in_banks(4), (on_scalar,)))

@@ -59,7 +59,6 @@ def tile_picked_wlapl_gelu_lo_kernel(tc, x_words, x_scales, w1, w2, gate, pos1, 
                 nc.sync.dma_start(out=w1_raw[t, g][:], in_=rows.rearrange("(p j) c -> p j c", j=PACK))
 
         pos = (pos1, pos2, pos3, pos4)
-        nc.sync.dma_start(out=lists[0][:], in_=pos[0])
         gate_cols = sb("gate_cols", [P, SPREAD, 4], F32)
         nc.sync.dma_start(out=gate_cols[:], in_=gate[:SPREAD, 0, :].rearrange("d (n m) -> n d m", m=4))
         load_w1(0)
@@ -72,6 +71,7 @@ def tile_picked_wlapl_gelu_lo_kernel(tc, x_words, x_scales, w1, w2, gate, pos1, 
                 in_=x_scales.bitcast(I32)[:, 4 * q : 4 * q + 4, :].rearrange("g r c -> r g c"),
             )
         nc.scalar.activation(out=bias[1][:], in_=bias[0][:], func=ACT.Gelu_apprx_tanh)
+        nc.sync.dma_start(out=lists[0][:], in_=pos[0])
         load_w1(1)
         nc.sync.dma_start(out=lists[1][:], in_=pos[1])
         gate_raw = sb("gate_raw", [P, D - SPREAD, T], F32)

@@ -33,10 +33,14 @@ def tile_picked_wlapl_gelu_lo_kernel(tc, x_words, x_scales, w1, w2, gate, pos1, 
     on_vector, on_scalar = nc.vector.tensor_copy, nc.scalar.copy
     with ExitStack() as ctx:
         keep = ctx.enter_context(tc.tile_pool(name="keep", bufs=1))
+        w2_room = ctx.enter_context(tc.tile_pool(name="w2_room", bufs=1))
         psum = ctx.enter_context(tc.psum_pool(name="psum", bufs=1))
 
         def sb(name, shape, dtype, room=None):
             return keep.tile(shape, dtype, name=name, tag=room or name, align_bytes=64)
+
+        def in_w2_room(name, shape, dtype, at):
+            return w2_room.tile(shape, dtype, name=name, offset=at, align_bytes=64)
 
         def bank(number, name, shape):
             return psum.tile(shape, F32, name=name, tag="bank%d" % number)
@@ -80,7 +84,7 @@ def tile_picked_wlapl_gelu_lo_kernel(tc, x_words, x_scales, w1, w2, gate, pos1, 
             nc.sync.dma_start(out=lists[d][:], in_=pos[d])
         load_w1(2)
         load_w1(3)
-        w2_raw = sb("w2_raw", [P, PACK, H], F32)
+        w2_raw = in_w2_room("w2_raw", [P, PACK, H], F32, 0)
         nc.sync.dma_start(out=w2_raw[:], in_=w2.rearrange("(p j) m -> p j m", j=PACK))
 
         ident = sb("ident", [P, P], F32)
@@ -222,7 +226,7 @@ def tile_picked_wlapl_gelu_lo_kernel(tc, x_words, x_scales, w1, w2, gate, pos1, 
 
         def second_layer(c, w2_codes, z_bf, make_accs, copies):
             v0, n = CHUNKS[c]
-            z_codes = sb("z_codes%d" % c, [P, n], U32)
+            z_codes = sb("z_codes%d" % c, [P, n], U32) if c else in_w2_room("z_codes0", [P, n], U32, 0)
             z_sc = sb("z_sc%d" % c, [P, n], U8)
             nc.vector.quantize_mx(out=z_codes[:].bitcast(FP8X4), scales=z_sc[:], in_=z_bf[:])
             per_bank = TILES // len(copies)
@@ -294,12 +298,15 @@ def tile_picked_wlapl_gelu_lo_kernel(tc, x_words, x_scales, w1, w2, gate, pos1, 
         z_first = turn_back(0, (0, 1))
 
         for block in range(2, 4):
-            sums_in(bank(block - 2, "sums_rest%d" % block, [P, P])[:], block, (2,))
-        gathers(2, half, half, every, terms_tile("terms2b", D * half, "w2_raw"))
+            sums_in(bank(block, "sums_rest%d" % block, [P, P])[:], block, (2,))
+        rest = [in_w2_room("terms2b_%d" % d, [P, half], F32, d * half * 4)[:] for d in range(D)]
+        for d in range(D - 1):
+            gathers(2, half, half, (d,), rest[d])
         w2_codes = sb("w2_codes", [P, H], U32, "terms3a")
         nc.vector.quantize_mx(out=w2_codes[:].bitcast(FP8X4), scales=w2_sc[:], in_=w2_bf[:].rearrange("p t m j -> p (t m j)"))
-
         y_first = second_layer(0, w2_codes, z_first, in_pair, (on_scalar, on_scalar))
+        gathers(2, half, half, (D - 1,), rest[D - 1])
+
         last_terms = terms_tile("terms3b", 2 * D * P, "z_bf0")
         sums_in(bank(5, "sums_second", [P, P])[:], 2, (LAST,))
         gathers(LAST, CHUNKS[1][0], P, every, last_terms[:, : D * P])

@@ -9,6 +9,7 @@ PACK = 4
 PASSES = K // (P * PACK)
 TILES = H // P
 LAST = TILES - 1
+BANK = 2048
 SPARE = 16
 SPREAD = 2
 
@@ -43,10 +44,7 @@ def tile_picked_wlapl_gelu_lo_kernel(tc, x_words, x_scales, w1, w2, gate, pos1, 
             return w2_room.tile(shape, dtype, name=name, offset=at, align_bytes=64)
 
         def bank(number, name, shape):
-            return psum.tile(shape, F32, name=name, tag="bank%d" % number)
-
-        def pair(name, shape):
-            return psum.tile([P, 2] + shape, F32, name=name, tag="pair")
+            return psum.tile(shape, F32, name=name, offset=number * BANK)
 
         lists = [keep.tile([P, T // 16], U16, name="list%d" % d) for d in range(D)]
         x_sc = sb("x_sc", [P, PASSES * T], U8)
@@ -112,45 +110,53 @@ def tile_picked_wlapl_gelu_lo_kernel(tc, x_words, x_scales, w1, w2, gate, pos1, 
         w1_codes = [sb("w1_codes%d" % t, [P, PASSES * P], U32) for t in range(TILES)]
         h = {}
 
-        def round_pass(copy, t, g, rounded):
+        def round_pass(copy, raw, rounded):
             copy(
                 out=rounded.rearrange("p (c i j) -> p c j i", i=4, j=PACK),
-                in_=w1_raw[t, g][:].rearrange("p j (c i) -> p c j i", i=4),
+                in_=raw.rearrange("p j (c i) -> p c j i", i=4),
             )
 
         def round_first_tile():
-            pieces = [sb("w1_bf0_%d" % g, [P, P * PACK], BF16) for g in range(PASSES)]
-            for g in range(PASSES):
-                round_pass(on_vector, 0, g, pieces[g][:])
+            pieces = [sb("w1_bf0_0", [P, P * PACK], BF16)]
+            round_pass(on_vector, w1_raw[0, 0][:], pieces[0][:])
+            for s in range(2):
+                pieces.append(sb("w1_bf0_1%d" % s, [P, P * PACK // 2], BF16))
+                round_pass(on_vector, w1_raw[0, 1][:, :, s * P // 2 : (s + 1) * P // 2], pieces[-1][:])
             return pieces
 
         def round_later_tile(t, room):
             rounded = sb("w1_bf%d" % t, [P, PASSES * P * PACK], BF16, room)
             for g in range(PASSES):
-                round_pass(on_scalar, t, g, rounded[:, g * P * PACK : (g + 1) * P * PACK])
+                round_pass(on_scalar, w1_raw[t, g][:], rounded[:, g * P * PACK : (g + 1) * P * PACK])
             return [rounded]
 
-        def first_layer(t, pieces, u):
+        def first_layer(t, pieces, us):
             scales = sb("w1_sc%d" % t, [P, PASSES * P], U8)
-            width = PASSES * P // len(pieces)
-            for s, piece in enumerate(pieces):
-                cols = slice(s * width, (s + 1) * width)
+            at = 0
+            for piece in pieces:
+                cols = slice(at, at + piece.shape[1] // PACK)
                 nc.vector.quantize_mx(out=w1_codes[t][:, cols].bitcast(FP8X4), scales=scales[:, cols], in_=piece[:])
+                at = cols.stop
+            n = T // len(us)
             for g in range(PASSES):
-                nc.tensor.matmul_mx(
-                    out=u,
-                    lhsT=w1_codes[t][:, g * P : (g + 1) * P].bitcast(FP8X4),
-                    lhsT_scale=scales[:, g * P : (g + 1) * P],
-                    rhs=x_w[:, g, :].bitcast(FP4X4),
-                    rhs_scale=x_sc[:, g * T : (g + 1) * T],
-                    start=(g == 0),
-                    stop=(g == PASSES - 1),
-                )
+                for s, u in enumerate(us):
+                    nc.tensor.matmul_mx(
+                        out=u,
+                        lhsT=w1_codes[t][:, g * P : (g + 1) * P].bitcast(FP8X4),
+                        lhsT_scale=scales[:, g * P : (g + 1) * P],
+                        rhs=x_w[:, g, 2 * s * n : 2 * (s + 1) * n].bitcast(FP4X4),
+                        rhs_scale=x_sc[:, g * T + s * n : g * T + (s + 1) * n],
+                        start=(g == 0),
+                        stop=(g == PASSES - 1),
+                    )
             whole = t < 2
             h[t] = sb("h%d" % t, [P, T + (SPARE if whole else 0)], F32)
             if whole:
                 nc.gpsimd.memset(h[t][:, T:], 0.0)
-            nc.scalar.activation(out=h[t][:, :T], in_=u, func=ACT.Gelu_apprx_tanh, bias=bias[t][:] if whole else 0.0)
+            for s, u in enumerate(us):
+                nc.scalar.activation(
+                    out=h[t][:, s * n : (s + 1) * n], in_=u, func=ACT.Gelu_apprx_tanh, bias=bias[t][:] if whole else 0.0
+                )
 
         zT = [sb("zT%d" % c, [P, n // P, 2, 2 * P], BF16) for c, (v0, n) in enumerate(CHUNKS)]
         home = {}
@@ -247,12 +253,8 @@ def tile_picked_wlapl_gelu_lo_kernel(tc, x_words, x_scales, w1, w2, gate, pos1, 
             nc.sync.dma_start(out=out_rows[:, :, v0 : v0 + n], in_=y[:])
             return y
 
-        def in_pair(shape):
-            both = pair("acc_pair", shape)
-            return [both[:, 0], both[:, 1]]
-
         def in_banks(*numbers):
-            return lambda shape: [bank(number, "acc%d" % number, [P] + shape)[:] for number in numbers]
+            return lambda shape: [bank(number, "acc%d_%d" % (number, shape[1]), [P] + shape)[:] for number in numbers]
 
         def hand_on(c, y):
             v0, n = CHUNKS[c]
@@ -266,35 +268,38 @@ def tile_picked_wlapl_gelu_lo_kernel(tc, x_words, x_scales, w1, w2, gate, pos1, 
 
         every = tuple(range(D))
         half = T // 2
+        for d in range(SPREAD):
+            spread_gate(d, bank(2 * d, "spread%d" % d, [P, 2, 4, P])[:, 0])
+        first_layer(0, round_first_tile(), [bank(s, "u0_%d" % s, [P, P])[:] for s in range(4)])
+
         for block in range(T // P):
             tiles = (0, 1, 2) if block < 2 else (0, 1)
             sums_in(bank(block, "sums%d" % block, [P, len(tiles) * P])[:], block, tiles)
-
-        spread_gate(0, pair("spread0", [4, P])[:, 0])
-        spread_gate(1, bank(4, "spread1", [P, 4, P])[:])
-        first_layer(0, round_first_tile(), pair("u0", [T])[:, 0])
 
         rounded = round_later_tile(1, "bias0")
         negate_loaded_gates("w1_raw1_0")
         gathers(0, 0, T, (0,), terms_tile("terms0a", T))
         gathers(0, 0, half, (1,), terms_tile("terms0b", half))
-        first_layer(1, rounded, bank(4, "u1", [P, T])[:])
+        first_layer(1, rounded, [bank(4, "u1", [P, T])[:]])
         gathers(0, half, half, (1,), terms_tile("terms0c", half, "w1_raw1_1"))
         gathers(0, 0, T, (2, 3), terms_tile("terms0d", 2 * T))
 
         rounded = round_later_tile(2, "bias1")
         gathers(1, 0, T, (0,), terms_tile("terms1a", T))
-        first_layer(2, rounded, bank(5, "u2", [P, T])[:])
+        first_layer(2, rounded, [bank(5, "u2", [P, T])[:]])
         gathers(1, 0, T, (1,), terms_tile("terms1b", T, "w1_raw2_1"))
-        first_layer(3, round_later_tile(3, "w1_raw2_0"), bank(4, "u3", [P, T])[:])
+        first_layer(3, round_later_tile(3, "w1_raw2_0"), [bank(4, "u3", [P, T])[:]])
         gathers(1, 0, T, (2, 3), terms_tile("terms1c", 2 * T, "w1_raw3_1"))
         w2_bf = round_w2("w1_codes3")
 
         gathers(2, 0, half, every, terms_tile("terms2a", D * half))
-        last_sums = pair("last_sums", [T])
         for block in range(2):
-            sums_in(last_sums[:, block, :P], block, (LAST,))
-        gathers(LAST, 0, half, every, terms_tile("terms3a", D * half))
+            sums_in(bank(6 + block, "last_sums%d" % block, [P, P])[:], block, (LAST,))
+        terms = terms_tile("terms3a", D * half)
+        gathers(LAST, 0, half, every[:-1], terms[:, : (D - 1) * half])
+        for block in range(2):
+            at = (D - 1) * half + block * P
+            gathers(LAST, block * P, P, every[-1:], terms[:, at : at + P])
         z_first = turn_back(0, (0, 1))
 
         for block in range(2, 4):
@@ -304,7 +309,7 @@ def tile_picked_wlapl_gelu_lo_kernel(tc, x_words, x_scales, w1, w2, gate, pos1, 
             gathers(2, half, half, (d,), rest[d])
         w2_codes = sb("w2_codes", [P, H], U32, "terms3a")
         nc.vector.quantize_mx(out=w2_codes[:].bitcast(FP8X4), scales=w2_sc[:], in_=w2_bf[:].rearrange("p t m j -> p (t m j)"))
-        y_first = second_layer(0, w2_codes, z_first, in_pair, (on_scalar, on_scalar))
+        y_first = second_layer(0, w2_codes, z_first, in_banks(6, 7), (on_scalar, on_scalar))
         gathers(2, half, half, (D - 1,), rest[D - 1])
 
         last_terms = terms_tile("terms3b", 2 * D * P, "z_bf0")

@@ -11,7 +11,7 @@ TILES = H // P
 LAST = TILES - 1
 BANK = 2048
 SPARE = 16
-SPREAD = 2
+SPREAD = 3
 
 CHUNKS = ((0, 256), (256, 128), (384, 128))
 
@@ -35,6 +35,7 @@ def tile_picked_wlapl_gelu_lo_kernel(tc, x_words, x_scales, w1, w2, gate, pos1, 
     with ExitStack() as ctx:
         keep = ctx.enter_context(tc.tile_pool(name="keep", bufs=1))
         w2_room = ctx.enter_context(tc.tile_pool(name="w2_room", bufs=1))
+        w1_room = ctx.enter_context(tc.tile_pool(name="w1_room", bufs=1))
         psum = ctx.enter_context(tc.psum_pool(name="psum", bufs=1))
 
         def sb(name, shape, dtype, room=None):
@@ -42,6 +43,9 @@ def tile_picked_wlapl_gelu_lo_kernel(tc, x_words, x_scales, w1, w2, gate, pos1, 
 
         def in_w2_room(name, shape, dtype, at):
             return w2_room.tile(shape, dtype, name=name, offset=at, align_bytes=64)
+
+        def in_w1_room(name, shape, dtype, at):
+            return w1_room.tile(shape, dtype, name=name, offset=at * 1024, align_bytes=64)
 
         def bank(number, name, shape):
             return psum.tile(shape, F32, name=name, offset=number * BANK)
@@ -54,11 +58,13 @@ def tile_picked_wlapl_gelu_lo_kernel(tc, x_words, x_scales, w1, w2, gate, pos1, 
 
         w1_raw = {}
 
-        def load_w1(t):
-            for g in range(PASSES):
-                w1_raw[t, g] = sb("w1_raw%d_%d" % (t, g), [P, PACK, P], F32)
+        def load_w1(t, passes=range(PASSES)):
+            for g in passes:
+                name = "w1_raw%d_%d" % (t, g)
+                raw = in_w1_room(name, [P, PACK, P], F32, (7, 1)[g]) if t == 1 else sb(name, [P, PACK, P], F32)
+                w1_raw[t, g] = raw[:]
                 rows = w1[g * P * PACK : (g + 1) * P * PACK, t * P : (t + 1) * P]
-                nc.sync.dma_start(out=w1_raw[t, g][:], in_=rows.rearrange("(p j) c -> p j c", j=PACK))
+                nc.sync.dma_start(out=raw[:], in_=rows.rearrange("(p j) c -> p j c", j=PACK))
 
         pos = (pos1, pos2, pos3, pos4)
         gate_cols = sb("gate_cols", [P, SPREAD, 4], F32)
@@ -80,8 +86,11 @@ def tile_picked_wlapl_gelu_lo_kernel(tc, x_words, x_scales, w1, w2, gate, pos1, 
         nc.sync.dma_start(out=gate_raw[:], in_=gate[SPREAD:].rearrange("d p v -> p d v"))
         for d in range(2, D):
             nc.sync.dma_start(out=lists[d][:], in_=pos[d])
-        load_w1(2)
-        load_w1(3)
+        both = sb("w1_raw23_0", [P, PACK, 2 * P], F32)
+        nc.sync.dma_start(out=both[:], in_=w1[: P * PACK, 2 * P :].rearrange("(p j) c -> p j c", j=PACK))
+        for t in (2, 3):
+            w1_raw[t, 0] = both[:, :, (t - 2) * P : (t - 1) * P]
+            load_w1(t, (1,))
         w2_raw = in_w2_room("w2_raw", [P, PACK, H], F32, 0)
         nc.sync.dma_start(out=w2_raw[:], in_=w2.rearrange("(p j) m -> p j m", j=PACK))
 
@@ -101,13 +110,13 @@ def tile_picked_wlapl_gelu_lo_kernel(tc, x_words, x_scales, w1, w2, gate, pos1, 
                 scale=-1.0,
             )
 
-        def negate_loaded_gates(room):
-            negated = sb("later_gates", [P, (D - SPREAD) * T], F32, room)
+        def negate_loaded_gates(negated):
             for s in range(D - SPREAD):
                 neg_gate[SPREAD + s] = negated[:, s * T : (s + 1) * T]
                 nc.scalar.activation(out=neg_gate[SPREAD + s], in_=gate_raw[:, s, :], func=ACT.Copy, scale=-1.0)
 
         w1_codes = [sb("w1_codes%d" % t, [P, PASSES * P], U32) for t in range(TILES)]
+        w1_sc = [sb("w1_sc%d" % t, [P, PASSES * P], U8) for t in range(TILES)]
         h = {}
 
         def round_pass(copy, raw, rounded):
@@ -118,37 +127,40 @@ def tile_picked_wlapl_gelu_lo_kernel(tc, x_words, x_scales, w1, w2, gate, pos1, 
 
         def round_first_tile():
             pieces = [sb("w1_bf0_0", [P, P * PACK], BF16)]
-            round_pass(on_vector, w1_raw[0, 0][:], pieces[0][:])
+            round_pass(on_vector, w1_raw[0, 0], pieces[0][:])
             for s in range(2):
                 pieces.append(sb("w1_bf0_1%d" % s, [P, P * PACK // 2], BF16))
                 round_pass(on_vector, w1_raw[0, 1][:, :, s * P // 2 : (s + 1) * P // 2], pieces[-1][:])
             return pieces
 
-        def round_later_tile(t, room):
-            rounded = sb("w1_bf%d" % t, [P, PASSES * P * PACK], BF16, room)
-            for g in range(PASSES):
-                round_pass(on_scalar, w1_raw[t, g][:], rounded[:, g * P * PACK : (g + 1) * P * PACK])
+        def round_later(t, passes, rounded):
+            for s, g in enumerate(passes):
+                round_pass(on_scalar, w1_raw[t, g], rounded[:, s * P * PACK : (s + 1) * P * PACK])
             return [rounded]
 
-        def first_layer(t, pieces, us):
-            scales = sb("w1_sc%d" % t, [P, PASSES * P], U8)
-            at = 0
+        def quantise_w1(t, first, pieces):
+            at = first * P
             for piece in pieces:
                 cols = slice(at, at + piece.shape[1] // PACK)
-                nc.vector.quantize_mx(out=w1_codes[t][:, cols].bitcast(FP8X4), scales=scales[:, cols], in_=piece[:])
+                nc.vector.quantize_mx(out=w1_codes[t][:, cols].bitcast(FP8X4), scales=w1_sc[t][:, cols], in_=piece[:, :])
                 at = cols.stop
+
+        def multiply(t, passes, us):
             n = T // len(us)
-            for g in range(PASSES):
-                for s, u in enumerate(us):
+            for s, u in enumerate(us):
+                for g in passes:
                     nc.tensor.matmul_mx(
                         out=u,
                         lhsT=w1_codes[t][:, g * P : (g + 1) * P].bitcast(FP8X4),
-                        lhsT_scale=scales[:, g * P : (g + 1) * P],
+                        lhsT_scale=w1_sc[t][:, g * P : (g + 1) * P],
                         rhs=x_w[:, g, 2 * s * n : 2 * (s + 1) * n].bitcast(FP4X4),
                         rhs_scale=x_sc[:, g * T + s * n : g * T + (s + 1) * n],
                         start=(g == 0),
                         stop=(g == PASSES - 1),
                     )
+
+        def make_h(t, us):
+            n = T // len(us)
             whole = t < 2
             h[t] = sb("h%d" % t, [P, T + (SPARE if whole else 0)], F32)
             if whole:
@@ -158,56 +170,60 @@ def tile_picked_wlapl_gelu_lo_kernel(tc, x_words, x_scales, w1, w2, gate, pos1, 
                     out=h[t][:, s * n : (s + 1) * n], in_=u, func=ACT.Gelu_apprx_tanh, bias=bias[t][:] if whole else 0.0
                 )
 
-        zT = [sb("zT%d" % c, [P, n // P, 2, 2 * P], BF16) for c, (v0, n) in enumerate(CHUNKS)]
-        home = {}
-        closes = {}
+        def first_layer(t, pieces, us):
+            quantise_w1(t, 0, pieces)
+            multiply(t, range(PASSES), us)
+            make_h(t, us)
 
-        def sums_in(columns, block, tiles):
-            for s, t in enumerate(tiles):
-                home[t, block] = columns[:, s * P : (s + 1) * P]
-            closes[tiles[-1], block] = (tiles[0], columns)
+        zT = sb("zT", [P, T // P, 2, 2 * P], BF16)
+        home = {}
+
+        def sums_in(columns, t, blocks):
+            for block in blocks:
+                home[t, block] = (columns, blocks)
 
         def add_term(t, block, d, term):
+            columns, blocks = home[t, block]
+            mine = columns[:, (block - blocks[0]) * P : (block - blocks[0] + 1) * P]
             if d == 0:
                 own = h[t][:, block * P : (block + 1) * P]
-                nc.tensor.matmul(home[t, block], lhsT=own, rhs=ident[:], start=True, stop=False, is_transpose=True)
-            nc.tensor.matmul(home[t, block], lhsT=term, rhs=ident[:], start=False, stop=(d == D - 1), is_transpose=True)
-
-        def round_z(block, first, columns):
-            c = max(block - 1, 0)
-            words = slice(64 * first, 64 * (first + columns.shape[1] // P))
-            nc.scalar.copy(
-                out=zT[c][:, block - CHUNKS[c][0] // P, :, words].rearrange("p u (q e) -> p u q e", e=2),
-                in_=columns.rearrange("p (q u e) -> p u q e", u=2, e=2),
-            )
+                nc.tensor.matmul(mine, lhsT=own, rhs=ident[:], start=(block == blocks[0]), stop=False, is_transpose=True)
+            last = d == D - 1 and block == blocks[-1]
+            nc.tensor.matmul(mine, lhsT=term, rhs=ident[:], start=False, stop=last, is_transpose=True)
+            if last:
+                nc.scalar.copy(
+                    out=zT[:, blocks[0] : block + 1, :, 64 * t : 64 * (t + 1)].rearrange("p b u (q e) -> p b u q e", e=2),
+                    in_=columns.rearrange("p (b q u e) -> p b u q e", q=32, u=2, e=2),
+                )
 
         def terms_tile(name, columns, room=None):
             return sb(name, [P, columns], F32, room)[:]
 
+        def gather(t, v0, d, terms):
+            n = terms.shape[1]
+            nc.vector.tensor_tensor(
+                out=terms,
+                in0=h[t][:].indirect(lists[d][:, v0 // 16 : (v0 + n) // 16]),
+                in1=neg_gate[d][:, v0 : v0 + n],
+                op=ALU.mult,
+            )
+
+        def add_terms(t, v0, d, terms):
+            for at in range(0, terms.shape[1], P):
+                add_term(t, (v0 + at) // P, d, terms[:, at : at + P])
+
         def gathers(t, v0, n, ds, terms):
-            mine = range(v0 // P, (v0 + n) // P)
             for s, d in enumerate(ds):
-                nc.vector.tensor_tensor(
-                    out=terms[:, s * n : (s + 1) * n],
-                    in0=h[t][:].indirect(lists[d][:, v0 // 16 : (v0 + n) // 16]),
-                    in1=neg_gate[d][:, v0 : v0 + n],
-                    op=ALU.mult,
-                )
-                for block in mine:
-                    at = s * n + block * P - v0
-                    add_term(t, block, d, terms[:, at : at + P])
-            if ds[-1] == D - 1:
-                for block in mine:
-                    if (t, block) in closes:
-                        round_z(block, *closes[t, block])
+                gather(t, v0, d, terms[:, s * n : (s + 1) * n])
+                add_terms(t, v0, d, terms[:, s * n : (s + 1) * n])
 
         def turn_back(c, numbers):
-            words = zT[c][:].bitcast(F32)
+            words = zT[:].bitcast(F32)
             z_bf = sb("z_bf%d" % c, [P, CHUNKS[c][1] * PACK], BF16)
             for b, number in enumerate(numbers):
                 back = bank(number, "back%d_%d" % (c, b), [P, 2, P])
                 for u in range(2):
-                    nc.tensor.transpose(back[:, u, :], words[:, b, u, :], ident[:])
+                    nc.tensor.transpose(back[:, u, :], words[:, CHUNKS[c][0] // P + b, u, :], ident[:])
                 nc.scalar.copy(
                     out=z_bf[:, b * P * PACK : (b + 1) * P * PACK].bitcast(F32).rearrange("p (v u) -> p v u", u=2),
                     in_=back[:].rearrange("p u v -> p v u"),
@@ -269,60 +285,72 @@ def tile_picked_wlapl_gelu_lo_kernel(tc, x_words, x_scales, w1, w2, gate, pos1, 
         every = tuple(range(D))
         half = T // 2
         for d in range(SPREAD):
-            spread_gate(d, bank(2 * d, "spread%d" % d, [P, 2, 4, P])[:, 0])
+            spread_gate(d, bank(d, "spread%d" % d, [P, 2 if d == SPREAD - 1 else 1, 4, P])[:, 0])
         first_layer(0, round_first_tile(), [bank(s, "u0_%d" % s, [P, P])[:] for s in range(4)])
 
-        for block in range(T // P):
-            tiles = (0, 1, 2) if block < 2 else (0, 1)
-            sums_in(bank(block, "sums%d" % block, [P, len(tiles) * P])[:], block, tiles)
+        shared = [bank(4 + 2 * t, "shared%d" % t, [P, 2, T]) for t in range(2)]
+        for t in range(2):
+            sums_in(shared[t][:, 0, :], t, (0, 1, 2, 3))
 
-        rounded = round_later_tile(1, "bias0")
-        negate_loaded_gates("w1_raw1_0")
+        rounded = [
+            round_later(1, (0,), sb("w1_bf1_0", [P, P * PACK], BF16, "bias0")),
+            round_later(1, (1,), in_w1_room("w1_bf1_1", [P, P * PACK], BF16, 7)),
+        ]
+        negate_loaded_gates(in_w1_room("later_gates", [P, (D - SPREAD) * T], F32, 0))
+        u1 = [shared[0][:, 1, :]]
         gathers(0, 0, T, (0,), terms_tile("terms0a", T))
-        gathers(0, 0, half, (1,), terms_tile("terms0b", half))
-        first_layer(1, rounded, [bank(4, "u1", [P, T])[:]])
-        gathers(0, half, half, (1,), terms_tile("terms0c", half, "w1_raw1_1"))
-        gathers(0, 0, T, (2, 3), terms_tile("terms0d", 2 * T))
+        quantise_w1(1, 0, rounded[0])
+        multiply(1, (0,), u1)
+        terms = in_w1_room("terms0b", [P, half], F32, 8)[:]
+        gather(0, 0, 1, terms)
+        quantise_w1(1, 1, rounded[1])
+        multiply(1, (1,), u1)
+        make_h(1, u1)
+        add_terms(0, 0, 1, terms)
+        terms = in_w1_room("terms0c", [P, half + 2 * T], F32, 2)
+        gathers(0, half, half, (1,), terms[:, :half])
+        gathers(0, 0, T, (2, 3), terms[:, half:])
 
-        rounded = round_later_tile(2, "bias1")
+        later = sb("w1_bf23", [P, 2 * PASSES * P * PACK], BF16, "bias1")
+        rounded = [round_later(t, range(PASSES), later[:, (t - 2) * K : (t - 1) * K]) for t in (2, 3)]
         gathers(1, 0, T, (0,), terms_tile("terms1a", T))
-        first_layer(2, rounded, [bank(5, "u2", [P, T])[:]])
+        first_layer(2, rounded[0], [shared[1][:, 1, :]])
         gathers(1, 0, T, (1,), terms_tile("terms1b", T, "w1_raw2_1"))
-        first_layer(3, round_later_tile(3, "w1_raw2_0"), [bank(4, "u3", [P, T])[:]])
+        first_layer(3, rounded[1], [bank(0, "u3", [P, T])[:]])
         gathers(1, 0, T, (2, 3), terms_tile("terms1c", 2 * T, "w1_raw3_1"))
         w2_bf = round_w2("w1_codes3")
 
+        sums_in(bank(1, "sums2a", [P, half])[:], 2, (0, 1))
         gathers(2, 0, half, every, terms_tile("terms2a", D * half))
         for block in range(2):
-            sums_in(bank(6 + block, "last_sums%d" % block, [P, P])[:], block, (LAST,))
+            sums_in(bank(2 + block, "last_sums%d" % block, [P, P])[:], LAST, (block,))
         terms = terms_tile("terms3a", D * half)
         gathers(LAST, 0, half, every[:-1], terms[:, : (D - 1) * half])
         for block in range(2):
             at = (D - 1) * half + block * P
             gathers(LAST, block * P, P, every[-1:], terms[:, at : at + P])
-        z_first = turn_back(0, (0, 1))
+        z_first = turn_back(0, (4, 5))
 
-        for block in range(2, 4):
-            sums_in(bank(block, "sums_rest%d" % block, [P, P])[:], block, (2,))
+        sums_in(bank(6, "sums2b", [P, half])[:], 2, (2, 3))
         rest = [in_w2_room("terms2b_%d" % d, [P, half], F32, d * half * 4)[:] for d in range(D)]
         for d in range(D - 1):
             gathers(2, half, half, (d,), rest[d])
         w2_codes = sb("w2_codes", [P, H], U32, "terms3a")
         nc.vector.quantize_mx(out=w2_codes[:].bitcast(FP8X4), scales=w2_sc[:], in_=w2_bf[:].rearrange("p t m j -> p (t m j)"))
-        y_first = second_layer(0, w2_codes, z_first, in_banks(6, 7), (on_scalar, on_scalar))
+        y_first = second_layer(0, w2_codes, z_first, in_banks(0, 1), (on_scalar, on_scalar))
         gathers(2, half, half, (D - 1,), rest[D - 1])
 
         last_terms = terms_tile("terms3b", 2 * D * P, "z_bf0")
-        sums_in(bank(5, "sums_second", [P, P])[:], 2, (LAST,))
+        sums_in(bank(7, "sums_second", [P, P])[:], LAST, (2,))
         gathers(LAST, CHUNKS[1][0], P, every, last_terms[:, : D * P])
-        z_second = turn_back(1, (2,))
-        sums_in(bank(4, "sums_third", [P, P])[:], 3, (LAST,))
+        z_second = turn_back(1, (3,))
+        sums_in(bank(2, "sums_third", [P, P])[:], LAST, (3,))
         gathers(LAST, CHUNKS[2][0], P, every, last_terms[:, D * P :])
-        z_third = turn_back(2, (5,))
+        z_third = turn_back(2, (7,))
 
         hand_on(0, y_first)
-        hand_on(1, second_layer(1, w2_codes, z_second, in_banks(4), (on_scalar,)))
-        hand_on(2, second_layer(2, w2_codes, z_third, in_banks(3, 2), (on_scalar, on_vector)))
+        hand_on(1, second_layer(1, w2_codes, z_second, in_banks(2), (on_scalar,)))
+        hand_on(2, second_layer(2, w2_codes, z_third, in_banks(4, 5), (on_scalar, on_vector)))
 
         for q in range(4):
             queue = nc.scalar if q % 2 else nc.sync

@@ -10,6 +10,7 @@ PASSES = K // (P * PACK)
 TILES = H // P
 LAST = TILES - 1
 BANK = 2048
+RAW1_AT = (11 * 1024, 3 * 1024)
 SPARE = 16
 SPREAD = 3
 
@@ -45,7 +46,7 @@ def tile_picked_wlapl_gelu_lo_kernel(tc, x_words, x_scales, w1, w2, gate, pos1, 
             return w2_room.tile(shape, dtype, name=name, offset=at, align_bytes=64)
 
         def in_w1_room(name, shape, dtype, at):
-            return w1_room.tile(shape, dtype, name=name, offset=at * 1024, align_bytes=64)
+            return w1_room.tile(shape, dtype, name=name, offset=at, align_bytes=64)
 
         def bank(number, name, shape):
             return psum.tile(shape, F32, name=name, offset=number * BANK)
@@ -61,7 +62,7 @@ def tile_picked_wlapl_gelu_lo_kernel(tc, x_words, x_scales, w1, w2, gate, pos1, 
         def load_w1(t, passes=range(PASSES)):
             for g in passes:
                 name = "w1_raw%d_%d" % (t, g)
-                raw = in_w1_room(name, [P, PACK, P], F32, (7, 1)[g]) if t == 1 else sb(name, [P, PACK, P], F32)
+                raw = in_w1_room(name, [P, PACK, P], F32, RAW1_AT[g]) if t == 1 else sb(name, [P, PACK, P], F32)
                 w1_raw[t, g] = raw[:]
                 rows = w1[g * P * PACK : (g + 1) * P * PACK, t * P : (t + 1) * P]
                 nc.sync.dma_start(out=raw[:], in_=rows.rearrange("(p j) c -> p j c", j=PACK))
@@ -99,23 +100,22 @@ def tile_picked_wlapl_gelu_lo_kernel(tc, x_words, x_scales, w1, w2, gate, pos1, 
 
         neg_gate = {}
 
-        def spread_gate(d, spread):
-            neg_gate[d] = sb("neg_gate%d" % d, [P, T], F32)[:]
+        def negate_columns(name, ds, room=None):
+            negated = sb(name, [P, len(ds), 4], F32, room)
+            nc.vector.tensor_scalar_mul(negated[:], gate_cols[:, ds[0] : ds[-1] + 1, :], -1.0)
+            return negated
+
+        def spread_gate(columns, number):
+            spread = bank(number, "spread%d_%d" % (number, len(neg_gate)), [P, 4, P])
             for m in range(4):
-                nc.tensor.transpose(spread[:, m, :], gate_cols[:, d, m : m + 1].to_broadcast([P, P]), ident[:])
-            nc.scalar.activation(
-                out=neg_gate[d].rearrange("p (n m) -> p n m", m=4),
-                in_=spread.rearrange("p m n -> p n m"),
-                func=ACT.Copy,
-                scale=-1.0,
-            )
+                nc.tensor.transpose(spread[:, m, :], columns[:, m : m + 1].to_broadcast([P, P]), ident[:])
+            return spread
 
-        def negate_loaded_gates(negated):
-            for s in range(D - SPREAD):
-                neg_gate[SPREAD + s] = negated[:, s * T : (s + 1) * T]
-                nc.scalar.activation(out=neg_gate[SPREAD + s], in_=gate_raw[:, s, :], func=ACT.Copy, scale=-1.0)
+        def fetch_gate(d, spread, place):
+            neg_gate[d] = place
+            nc.scalar.copy(out=place.rearrange("p (n m) -> p n m", m=4), in_=spread[:].rearrange("p m n -> p n m"))
 
-        w1_codes = [sb("w1_codes%d" % t, [P, PASSES * P], U32) for t in range(TILES)]
+        w1_codes = {t: sb("w1_codes%d" % t, [P, PASSES * P], U32) for t in range(1, TILES)}
         w1_sc = [sb("w1_sc%d" % t, [P, PASSES * P], U8) for t in range(TILES)]
         h = {}
 
@@ -185,11 +185,13 @@ def tile_picked_wlapl_gelu_lo_kernel(tc, x_words, x_scales, w1, w2, gate, pos1, 
         def add_term(t, block, d, term):
             columns, blocks = home[t, block]
             mine = columns[:, (block - blocks[0]) * P : (block - blocks[0] + 1) * P]
-            if d == 0:
-                own = h[t][:, block * P : (block + 1) * P]
-                nc.tensor.matmul(mine, lhsT=own, rhs=ident[:], start=(block == blocks[0]), stop=False, is_transpose=True)
+            summands = [term]
+            if d == (1 if t == 0 else 0):
+                summands.insert(0, h[t][:, block * P : (block + 1) * P])
             last = d == D - 1 and block == blocks[-1]
-            nc.tensor.matmul(mine, lhsT=term, rhs=ident[:], start=False, stop=last, is_transpose=True)
+            for s, summand in enumerate(summands):
+                first = d == 0 and s == 0 and block == blocks[0]
+                nc.tensor.matmul(mine, lhsT=summand, rhs=ident[:], start=first, stop=last, is_transpose=True)
             if last:
                 nc.scalar.copy(
                     out=zT[:, blocks[0] : block + 1, :, 64 * t : 64 * (t + 1)].rearrange("p b u (q e) -> p b u q e", e=2),
@@ -284,30 +286,34 @@ def tile_picked_wlapl_gelu_lo_kernel(tc, x_words, x_scales, w1, w2, gate, pos1, 
 
         every = tuple(range(D))
         half = T // 2
-        for d in range(SPREAD):
-            spread_gate(d, bank(d, "spread%d" % d, [P, 2 if d == SPREAD - 1 else 1, 4, P])[:, 0])
+        fetch_gate(0, spread_gate(negate_columns("columns0", (0,))[:, 0, :], 6), sb("neg_gate0", [P, T], F32)[:])
+        w1_codes[0] = sb("w1_codes0", [P, PASSES * P], U32, "columns0")
         first_layer(0, round_first_tile(), [bank(s, "u0_%d" % s, [P, P])[:] for s in range(4)])
+        columns = negate_columns("columns12", (1, 2), "w1_bf0_11")
+        spreads = [spread_gate(columns[:, s, :], 7 - s) for s in range(2)]
 
         shared = [bank(4 + 2 * t, "shared%d" % t, [P, 2, T]) for t in range(2)]
         for t in range(2):
             sums_in(shared[t][:, 0, :], t, (0, 1, 2, 3))
 
-        rounded = [
-            round_later(1, (0,), sb("w1_bf1_0", [P, P * PACK], BF16, "bias0")),
-            round_later(1, (1,), in_w1_room("w1_bf1_1", [P, P * PACK], BF16, 7)),
-        ]
-        negate_loaded_gates(in_w1_room("later_gates", [P, (D - SPREAD) * T], F32, 0))
+        rounded = [round_later(1, (0,), sb("w1_bf1_0", [P, P * PACK], BF16, "bias0"))]
+        fetch_gate(1, spreads[0], in_w1_room("neg_gate1", [P, T], F32, RAW1_AT[0] - 1536)[:])
+        rounded.append(round_later(1, (1,), in_w1_room("w1_bf1_1", [P, P * PACK], BF16, RAW1_AT[0] + 512)))
+        later_gates = in_w1_room("later_gates", [P, 2, T], F32, RAW1_AT[1] - 3072)
+        fetch_gate(2, spreads[1], later_gates[:, 0, :])
+        neg_gate[3] = later_gates[:, 1, :]
+        nc.scalar.activation(out=neg_gate[3], in_=gate_raw[:, 0, :], func=ACT.Copy, scale=-1.0)
         u1 = [shared[0][:, 1, :]]
         gathers(0, 0, T, (0,), terms_tile("terms0a", T))
         quantise_w1(1, 0, rounded[0])
         multiply(1, (0,), u1)
-        terms = in_w1_room("terms0b", [P, half], F32, 8)[:]
+        terms = in_w1_room("terms0b", [P, half], F32, RAW1_AT[0] + 1536)[:]
         gather(0, 0, 1, terms)
         quantise_w1(1, 1, rounded[1])
         multiply(1, (1,), u1)
         make_h(1, u1)
         add_terms(0, 0, 1, terms)
-        terms = in_w1_room("terms0c", [P, half + 2 * T], F32, 2)
+        terms = in_w1_room("terms0c", [P, half + 2 * T], F32, RAW1_AT[1] + 1024)
         gathers(0, half, half, (1,), terms[:, :half])
         gathers(0, 0, T, (2, 3), terms[:, half:])
 

@@ -12,7 +12,6 @@ LAST = TILES - 1
 BANK = 2048
 RAW1_AT = (11 * 1024, 3 * 1024)
 SPARE = 16
-SPREAD = 3
 
 CHUNKS = ((0, 256), (256, 128), (384, 128))
 
@@ -68,24 +67,23 @@ def tile_picked_wlapl_gelu_lo_kernel(tc, x_words, x_scales, w1, w2, gate, pos1, 
                 nc.sync.dma_start(out=raw[:], in_=rows.rearrange("(p j) c -> p j c", j=PACK))
 
         pos = (pos1, pos2, pos3, pos4)
-        gate_cols = sb("gate_cols", [P, SPREAD, 4], F32)
-        nc.sync.dma_start(out=gate_cols[:], in_=gate[:SPREAD, 0, :].rearrange("d (n m) -> n d m", m=4))
         load_w1(0)
-        x_w = sb("x_w", [P, PASSES, 2 * T], U8)
-        nc.sync.dma_start(out=x_w[:].bitcast(I32), in_=x_words.bitcast(I32).rearrange("g p c -> p g c"))
         x_sc_rows = x_sc[:].bitcast(I32).rearrange("p (g c) -> p g c", g=PASSES)
         for q in range(4):
-            nc.scalar.dma_start(
+            nc.sync.dma_start(
                 out=x_sc_rows[32 * q : 32 * q + 4],
                 in_=x_scales.bitcast(I32)[:, 4 * q : 4 * q + 4, :].rearrange("g r c -> r g c"),
             )
+        x_w = sb("x_w", [P, PASSES, 2 * T], U8)
+        nc.sync.dma_start(out=x_w[:].bitcast(I32), in_=x_words.bitcast(I32).rearrange("g p c -> p g c"))
         nc.scalar.activation(out=bias[1][:], in_=bias[0][:], func=ACT.Gelu_apprx_tanh)
+        gate_raw = sb("gate_raw", [P, T], F32)
+        nc.sync.dma_start(out=gate_raw[:], in_=gate[0])
+        gate_cols = sb("gate_cols", [P, D - 1, 4], F32)
+        nc.sync.dma_start(out=gate_cols[:], in_=gate[1:, 0, :].rearrange("d (n m) -> n d m", m=4))
         nc.sync.dma_start(out=lists[0][:], in_=pos[0])
         load_w1(1)
-        nc.sync.dma_start(out=lists[1][:], in_=pos[1])
-        gate_raw = sb("gate_raw", [P, D - SPREAD, T], F32)
-        nc.sync.dma_start(out=gate_raw[:], in_=gate[SPREAD:].rearrange("d p v -> p d v"))
-        for d in range(2, D):
+        for d in range(1, D):
             nc.sync.dma_start(out=lists[d][:], in_=pos[d])
         both = sb("w1_raw23_0", [P, PACK, 2 * P], F32)
         nc.sync.dma_start(out=both[:], in_=w1[: P * PACK, 2 * P :].rearrange("(p j) c -> p j c", j=PACK))
@@ -100,13 +98,8 @@ def tile_picked_wlapl_gelu_lo_kernel(tc, x_words, x_scales, w1, w2, gate, pos1, 
 
         neg_gate = {}
 
-        def negate_columns(name, ds, room=None):
-            negated = sb(name, [P, len(ds), 4], F32, room)
-            nc.vector.tensor_scalar_mul(negated[:], gate_cols[:, ds[0] : ds[-1] + 1, :], -1.0)
-            return negated
-
         def spread_gate(columns, number):
-            spread = bank(number, "spread%d_%d" % (number, len(neg_gate)), [P, 4, P])
+            spread = bank(number, "spread%d" % number, [P, 4, P])
             for m in range(4):
                 nc.tensor.transpose(spread[:, m, :], columns[:, m : m + 1].to_broadcast([P, P]), ident[:])
             return spread
@@ -115,7 +108,7 @@ def tile_picked_wlapl_gelu_lo_kernel(tc, x_words, x_scales, w1, w2, gate, pos1, 
             neg_gate[d] = place
             nc.scalar.copy(out=place.rearrange("p (n m) -> p n m", m=4), in_=spread[:].rearrange("p m n -> p n m"))
 
-        w1_codes = {t: sb("w1_codes%d" % t, [P, PASSES * P], U32) for t in range(1, TILES)}
+        w1_codes = [sb("w1_codes%d" % t, [P, PASSES * P], U32) for t in range(TILES)]
         w1_sc = [sb("w1_sc%d" % t, [P, PASSES * P], U8) for t in range(TILES)]
         h = {}
 
@@ -147,8 +140,8 @@ def tile_picked_wlapl_gelu_lo_kernel(tc, x_words, x_scales, w1, w2, gate, pos1, 
 
         def multiply(t, passes, us):
             n = T // len(us)
-            for s, u in enumerate(us):
-                for g in passes:
+            for g in passes:
+                for s, u in enumerate(us):
                     nc.tensor.matmul_mx(
                         out=u,
                         lhsT=w1_codes[t][:, g * P : (g + 1) * P].bitcast(FP8X4),
@@ -286,11 +279,12 @@ def tile_picked_wlapl_gelu_lo_kernel(tc, x_words, x_scales, w1, w2, gate, pos1, 
 
         every = tuple(range(D))
         half = T // 2
-        fetch_gate(0, spread_gate(negate_columns("columns0", (0,))[:, 0, :], 6), sb("neg_gate0", [P, T], F32)[:])
-        w1_codes[0] = sb("w1_codes0", [P, PASSES * P], U32, "columns0")
         first_layer(0, round_first_tile(), [bank(s, "u0_%d" % s, [P, P])[:] for s in range(4)])
-        columns = negate_columns("columns12", (1, 2), "w1_bf0_11")
-        spreads = [spread_gate(columns[:, s, :], 7 - s) for s in range(2)]
+        columns = sb("columns", [P, D - 1, 4], F32, "w1_bf0_11")
+        nc.vector.tensor_scalar_mul(columns[:], gate_cols[:], -1.0)
+        neg_gate[0] = sb("neg_gate0", [P, T], F32)[:]
+        nc.vector.tensor_scalar_mul(neg_gate[0], gate_raw[:], -1.0)
+        spreads = [spread_gate(columns[:, s, :], number) for s, number in enumerate((7, 6, 0))]
 
         shared = [bank(4 + 2 * t, "shared%d" % t, [P, 2, T]) for t in range(2)]
         for t in range(2):
@@ -300,9 +294,8 @@ def tile_picked_wlapl_gelu_lo_kernel(tc, x_words, x_scales, w1, w2, gate, pos1, 
         fetch_gate(1, spreads[0], in_w1_room("neg_gate1", [P, T], F32, RAW1_AT[0] - 1536)[:])
         rounded.append(round_later(1, (1,), in_w1_room("w1_bf1_1", [P, P * PACK], BF16, RAW1_AT[0] + 512)))
         later_gates = in_w1_room("later_gates", [P, 2, T], F32, RAW1_AT[1] - 3072)
-        fetch_gate(2, spreads[1], later_gates[:, 0, :])
-        neg_gate[3] = later_gates[:, 1, :]
-        nc.scalar.activation(out=neg_gate[3], in_=gate_raw[:, 0, :], func=ACT.Copy, scale=-1.0)
+        for s in range(2):
+            fetch_gate(2 + s, spreads[1 + s], later_gates[:, s, :])
         u1 = [shared[0][:, 1, :]]
         gathers(0, 0, T, (0,), terms_tile("terms0a", T))
         quantise_w1(1, 0, rounded[0])

@@ -11,6 +11,7 @@ TILES = H // P
 LAST = TILES - 1
 BANK = 2048
 RAW1_AT = (11 * 1024, 3 * 1024)
+BIAS_AT = 16 * 1024
 SPARE = 16
 
 CHUNKS = ((0, 256), (256, 128), (384, 128))
@@ -53,8 +54,8 @@ def tile_picked_wlapl_gelu_lo_kernel(tc, x_words, x_scales, w1, w2, gate, pos1, 
         lists = [keep.tile([P, T // 16], U16, name="list%d" % d) for d in range(D)]
         x_sc = sb("x_sc", [P, PASSES * T], U8)
         nc.gpsimd.memset(x_sc[:].bitcast(I32), 0)
-        bias = [sb("bias%d" % t, [P, 1], F32) for t in range(2)]
-        nc.gpsimd.memset(bias[0][:], 0.0)
+        bias = [in_w1_room("bias0", [P, 32], F32, BIAS_AT)[:, :1], sb("bias1", [P, 1], F32)[:]]
+        nc.gpsimd.memset(bias[0], 0.0)
 
         w1_raw = {}
 
@@ -76,7 +77,7 @@ def tile_picked_wlapl_gelu_lo_kernel(tc, x_words, x_scales, w1, w2, gate, pos1, 
             )
         x_w = sb("x_w", [P, PASSES, 2 * T], U8)
         nc.sync.dma_start(out=x_w[:].bitcast(I32), in_=x_words.bitcast(I32).rearrange("g p c -> p g c"))
-        nc.scalar.activation(out=bias[1][:], in_=bias[0][:], func=ACT.Gelu_apprx_tanh)
+        nc.scalar.activation(out=bias[1], in_=bias[0], func=ACT.Gelu_apprx_tanh)
         gate_raw = sb("gate_raw", [P, T], F32)
         nc.sync.dma_start(out=gate_raw[:], in_=gate[0])
         gate_cols = sb("gate_cols", [P, D - 1, 4], F32)
@@ -121,9 +122,10 @@ def tile_picked_wlapl_gelu_lo_kernel(tc, x_words, x_scales, w1, w2, gate, pos1, 
         def round_first_tile():
             pieces = [sb("w1_bf0_0", [P, P * PACK], BF16)]
             round_pass(on_vector, w1_raw[0, 0], pieces[0][:])
+            pieces.append(sb("w1_bf0_10", [P, P * PACK // 2], BF16))
+            pieces.append(in_w1_room("w1_bf0_11", [P, P * PACK // 2], BF16, BIAS_AT + 832))
             for s in range(2):
-                pieces.append(sb("w1_bf0_1%d" % s, [P, P * PACK // 2], BF16))
-                round_pass(on_vector, w1_raw[0, 1][:, :, s * P // 2 : (s + 1) * P // 2], pieces[-1][:])
+                round_pass(on_vector, w1_raw[0, 1][:, :, s * P // 2 : (s + 1) * P // 2], pieces[1 + s][:])
             return pieces
 
         def round_later(t, passes, rounded):
@@ -160,7 +162,7 @@ def tile_picked_wlapl_gelu_lo_kernel(tc, x_words, x_scales, w1, w2, gate, pos1, 
                 nc.gpsimd.memset(h[t][:, T:], 0.0)
             for s, u in enumerate(us):
                 nc.scalar.activation(
-                    out=h[t][:, s * n : (s + 1) * n], in_=u, func=ACT.Gelu_apprx_tanh, bias=bias[t][:] if whole else 0.0
+                    out=h[t][:, s * n : (s + 1) * n], in_=u, func=ACT.Gelu_apprx_tanh, bias=bias[t] if whole else 0.0
                 )
 
         def first_layer(t, pieces, us):
@@ -280,35 +282,36 @@ def tile_picked_wlapl_gelu_lo_kernel(tc, x_words, x_scales, w1, w2, gate, pos1, 
         every = tuple(range(D))
         half = T // 2
         first_layer(0, round_first_tile(), [bank(s, "u0_%d" % s, [P, P])[:] for s in range(4)])
-        columns = sb("columns", [P, D - 1, 4], F32, "w1_bf0_11")
-        nc.vector.tensor_scalar_mul(columns[:], gate_cols[:], -1.0)
+        columns = [
+            in_w1_room("columns1", [P, 1, 4], F32, BIAS_AT + 832),
+            in_w1_room("columns23", [P, 2, 4], F32, BIAS_AT + 1152),
+        ]
+        nc.vector.tensor_scalar_mul(columns[0][:], gate_cols[:, :1, :], -1.0)
+        nc.vector.tensor_scalar_mul(columns[1][:], gate_cols[:, 1:, :], -1.0)
         neg_gate[0] = sb("neg_gate0", [P, T], F32)[:]
         nc.vector.tensor_scalar_mul(neg_gate[0], gate_raw[:], -1.0)
-        spreads = [spread_gate(columns[:, s, :], number) for s, number in enumerate((7, 6, 0))]
+        spreads = [spread_gate(columns[0][:, 0, :], 7), spread_gate(columns[1][:, 0, :], 6), spread_gate(columns[1][:, 1, :], 0)]
 
         shared = [bank(4 + 2 * t, "shared%d" % t, [P, 2, T]) for t in range(2)]
         for t in range(2):
             sums_in(shared[t][:, 0, :], t, (0, 1, 2, 3))
 
-        rounded = [round_later(1, (0,), sb("w1_bf1_0", [P, P * PACK], BF16, "bias0"))]
-        fetch_gate(1, spreads[0], in_w1_room("neg_gate1", [P, T], F32, RAW1_AT[0] - 1536)[:])
+        fetch_gate(1, spreads[0], in_w1_room("neg_gate1", [P, T], F32, BIAS_AT + 64 - 2048)[:])
+        rounded = [round_later(1, (0,), in_w1_room("w1_bf1_0", [P, P * PACK], BF16, BIAS_AT + 64))]
+        fetch_gate(2, spreads[1], in_w1_room("neg_gate2", [P, T], F32, RAW1_AT[0] - 1536)[:])
         rounded.append(round_later(1, (1,), in_w1_room("w1_bf1_1", [P, P * PACK], BF16, RAW1_AT[0] + 512)))
-        later_gates = in_w1_room("later_gates", [P, 2, T], F32, RAW1_AT[1] - 3072)
-        for s in range(2):
-            fetch_gate(2 + s, spreads[1 + s], later_gates[:, s, :])
+        fetch_gate(3, spreads[2], in_w1_room("neg_gate3", [P, T], F32, RAW1_AT[1] - 1024)[:])
         u1 = [shared[0][:, 1, :]]
         gathers(0, 0, T, (0,), terms_tile("terms0a", T))
-        quantise_w1(1, 0, rounded[0])
-        multiply(1, (0,), u1)
-        terms = in_w1_room("terms0b", [P, half], F32, RAW1_AT[0] + 1536)[:]
-        gather(0, 0, 1, terms)
-        quantise_w1(1, 1, rounded[1])
-        multiply(1, (1,), u1)
+        second = [terms_tile("terms0b", half), in_w1_room("terms0c", [P, half], F32, RAW1_AT[0] + 1536)[:]]
+        for g in range(PASSES):
+            gather(0, g * half, 1, second[g])
+            quantise_w1(1, g, rounded[g])
+            multiply(1, (g,), u1)
         make_h(1, u1)
-        add_terms(0, 0, 1, terms)
-        terms = in_w1_room("terms0c", [P, half + 2 * T], F32, RAW1_AT[1] + 1024)
-        gathers(0, half, half, (1,), terms[:, :half])
-        gathers(0, 0, T, (2, 3), terms[:, half:])
+        for g in range(PASSES):
+            add_terms(0, g * half, 1, second[g])
+        gathers(0, 0, T, (2, 3), in_w1_room("terms0d", [P, 2 * T], F32, RAW1_AT[1] + 1024)[:])
 
         later = sb("w1_bf23", [P, 2 * PASSES * P * PACK], BF16, "bias1")
         rounded = [round_later(t, range(PASSES), later[:, (t - 2) * K : (t - 1) * K]) for t in (2, 3)]

@@ -9,11 +9,10 @@ PACK = 4
 PASSES = K // (P * PACK)
 TILES = H // P
 LAST = TILES - 1
+HALF = T // 2
 BANK = 2048
-RAW1_AT = (11 * 1024, 3 * 1024)
-BIAS_AT = 16 * 1024
+LAP = 64
 SPARE = 16
-
 CHUNKS = ((0, 256), (256, 128), (384, 128))
 
 FLOPS = 2 * K * H * T + 2 * H * H * T
@@ -28,6 +27,7 @@ FP8X4 = mybir.dt.float8_e4m3fn_x4
 FP4X4 = mybir.dt.float4_e2m1fn_x4
 ACT = mybir.ActivationFunctionType
 ALU = mybir.AluOpType
+BYTES_OF = {F32: 4, BF16: 2, U32: 4, U8: 1}
 
 
 def tile_picked_wlapl_gelu_lo_kernel(tc, x_words, x_scales, w1, w2, gate, pos1, pos2, pos3, pos4, out_0, out_1, out_2):
@@ -35,18 +35,33 @@ def tile_picked_wlapl_gelu_lo_kernel(tc, x_words, x_scales, w1, w2, gate, pos1, 
     on_vector, on_scalar = nc.vector.tensor_copy, nc.scalar.copy
     with ExitStack() as ctx:
         keep = ctx.enter_context(tc.tile_pool(name="keep", bufs=1))
-        w2_room = ctx.enter_context(tc.tile_pool(name="w2_room", bufs=1))
-        w1_room = ctx.enter_context(tc.tile_pool(name="w1_room", bufs=1))
+        rooms = ctx.enter_context(tc.tile_pool(name="rooms", bufs=1))
         psum = ctx.enter_context(tc.psum_pool(name="psum", bufs=1))
+        span = {}
 
-        def sb(name, shape, dtype, room=None):
-            return keep.tile(shape, dtype, name=name, tag=room or name, align_bytes=64)
+        def sb(name, shape, dtype):
+            return keep.tile(shape, dtype, name=name, align_bytes=64)
 
-        def in_w2_room(name, shape, dtype, at):
-            return w2_room.tile(shape, dtype, name=name, offset=at, align_bytes=64)
+        def size(shape, dtype):
+            count = BYTES_OF[dtype]
+            for n in shape[1:]:
+                count = count * n
+            return count
 
-        def in_w1_room(name, shape, dtype, at):
-            return w1_room.tile(shape, dtype, name=name, offset=at, align_bytes=64)
+        def place(name, shape, dtype, at):
+            span[name] = (at, at + size(shape, dtype))
+            return rooms.tile(shape, dtype, name=name, offset=at, align_bytes=64)
+
+        def host(name, shape, dtype, below=0, above=0):
+            at = max([0] + [end for (start, end) in span.values()]) + below
+            span[name + "_free"] = (at, at + size(shape, dtype) + above)
+            return place(name, shape, dtype, at)
+
+        def under(earlier, name, shape, dtype):
+            return place(name, shape, dtype, span[earlier][0] + LAP - size(shape, dtype))
+
+        def over(earlier, name, shape, dtype):
+            return place(name, shape, dtype, span[earlier][1] - LAP)
 
         def bank(number, name, shape):
             return psum.tile(shape, F32, name=name, offset=number * BANK)
@@ -54,21 +69,21 @@ def tile_picked_wlapl_gelu_lo_kernel(tc, x_words, x_scales, w1, w2, gate, pos1, 
         lists = [keep.tile([P, T // 16], U16, name="list%d" % d) for d in range(D)]
         x_sc = sb("x_sc", [P, PASSES * T], U8)
         nc.gpsimd.memset(x_sc[:].bitcast(I32), 0)
-        bias = [in_w1_room("bias0", [P, 32], F32, BIAS_AT)[:, :1], sb("bias1", [P, 1], F32)[:]]
-        nc.gpsimd.memset(bias[0], 0.0)
+        zero = sb("zero", [P, 1], F32)
+        nc.gpsimd.memset(zero[:], 0.0)
+        bias0 = host("bias0", [P, 32], F32, below=2048, above=1024)
 
         w1_raw = {}
 
-        def load_w1(t, passes=range(PASSES)):
-            for g in passes:
-                name = "w1_raw%d_%d" % (t, g)
-                raw = in_w1_room(name, [P, PACK, P], F32, RAW1_AT[g]) if t == 1 else sb(name, [P, PACK, P], F32)
-                w1_raw[t, g] = raw[:]
-                rows = w1[g * P * PACK : (g + 1) * P * PACK, t * P : (t + 1) * P]
-                nc.sync.dma_start(out=raw[:], in_=rows.rearrange("(p j) c -> p j c", j=PACK))
+        def load_w1(raw, t, g):
+            rows = w1[g * P * PACK : (g + 1) * P * PACK, t * P : t * P + raw.shape[2]]
+            nc.sync.dma_start(out=raw[:], in_=rows.rearrange("(p j) c -> p j c", j=PACK))
+            for s in range(raw.shape[2] // P):
+                w1_raw[t + s, g] = raw[:, :, s * P : (s + 1) * P]
 
         pos = (pos1, pos2, pos3, pos4)
-        load_w1(0)
+        for g in range(PASSES):
+            load_w1(sb("w1_raw0_%d" % g, [P, PACK, P], F32), 0, g)
         x_sc_rows = x_sc[:].bitcast(I32).rearrange("p (g c) -> p g c", g=PASSES)
         for q in range(4):
             nc.sync.dma_start(
@@ -77,37 +92,40 @@ def tile_picked_wlapl_gelu_lo_kernel(tc, x_words, x_scales, w1, w2, gate, pos1, 
             )
         x_w = sb("x_w", [P, PASSES, 2 * T], U8)
         nc.sync.dma_start(out=x_w[:].bitcast(I32), in_=x_words.bitcast(I32).rearrange("g p c -> p g c"))
-        nc.scalar.activation(out=bias[1], in_=bias[0], func=ACT.Gelu_apprx_tanh)
-        gate_raw = sb("gate_raw", [P, T], F32)
-        nc.sync.dma_start(out=gate_raw[:], in_=gate[0])
-        gate_cols = sb("gate_cols", [P, D - 1, 4], F32)
-        nc.sync.dma_start(out=gate_cols[:], in_=gate[1:, 0, :].rearrange("d (n m) -> n d m", m=4))
-        nc.sync.dma_start(out=lists[0][:], in_=pos[0])
-        load_w1(1)
-        for d in range(1, D):
+        gates = [sb("gate%d" % d, [P, T], F32) for d in range(D)]
+        nc.sync.dma_start(out=gates[0][:], in_=gate[0])
+        nc.scalar.activation(out=bias0[:, :1], in_=zero[:], func=ACT.Gelu_apprx_tanh)
+        def load_list(d):
             nc.sync.dma_start(out=lists[d][:], in_=pos[d])
-        both = sb("w1_raw23_0", [P, PACK, 2 * P], F32)
-        nc.sync.dma_start(out=both[:], in_=w1[: P * PACK, 2 * P :].rearrange("(p j) c -> p j c", j=PACK))
-        for t in (2, 3):
-            w1_raw[t, 0] = both[:, :, (t - 2) * P : (t - 1) * P]
-            load_w1(t, (1,))
-        w2_raw = in_w2_room("w2_raw", [P, PACK, H], F32, 0)
-        nc.sync.dma_start(out=w2_raw[:], in_=w2.rearrange("(p j) m -> p j m", j=PACK))
+
+        def load_gate(d):
+            nc.sync.dma_start(out=gates[d][:], in_=gate[d])
+
+        load_list(0)
+        load_list(3)
+        load_w1(host("w1_raw1_0", [P, PACK, P], F32, below=1024), 1, 0)
+        load_gate(1)
+        load_list(1)
+        load_w1(host("w1_raw1_1", [P, PACK, P], F32, below=1024, above=5120), 1, 1)
+        load_gate(3)
+        load_list(2)
+        load_gate(2)
+        load_w1(sb("w1_raw2_0", [P, PACK, P], F32), 2, 0)
+        load_w1(host("w1_raw2_1", [P, PACK, P], F32, below=2176, above=3072), 2, 1)
+        load_w1(host("w1_raw3_0", [P, PACK, P], F32, below=5120, above=2048), 3, 0)
+        load_w1(host("w1_raw3_1", [P, PACK, P], F32, below=2048, above=6144), 3, 1)
+        w2_raw = [host("w2_raw%d" % s, [P, PACK, H // 2], F32, below=2048, above=5120) for s in range(2)]
+        for s in range(2):
+            nc.sync.dma_start(out=w2_raw[s][:], in_=w2[:, s * H // 2 : (s + 1) * H // 2].rearrange("(p j) m -> p j m", j=PACK))
 
         ident = sb("ident", [P, P], F32)
         make_identity(nc, ident[:])
 
         neg_gate = {}
 
-        def spread_gate(columns, number):
-            spread = bank(number, "spread%d" % number, [P, 4, P])
-            for m in range(4):
-                nc.tensor.transpose(spread[:, m, :], columns[:, m : m + 1].to_broadcast([P, P]), ident[:])
-            return spread
-
-        def fetch_gate(d, spread, place):
-            neg_gate[d] = place
-            nc.scalar.copy(out=place.rearrange("p (n m) -> p n m", m=4), in_=spread[:].rearrange("p m n -> p n m"))
+        def negate_gate(d, negated):
+            neg_gate[d] = negated
+            nc.vector.tensor_scalar_mul(neg_gate[d], gates[d][:], -1.0)
 
         w1_codes = [sb("w1_codes%d" % t, [P, PASSES * P], U32) for t in range(TILES)]
         w1_sc = [sb("w1_sc%d" % t, [P, PASSES * P], U8) for t in range(TILES)]
@@ -119,26 +137,9 @@ def tile_picked_wlapl_gelu_lo_kernel(tc, x_words, x_scales, w1, w2, gate, pos1, 
                 in_=raw.rearrange("p j (c i) -> p c j i", i=4),
             )
 
-        def round_first_tile():
-            pieces = [sb("w1_bf0_0", [P, P * PACK], BF16)]
-            round_pass(on_vector, w1_raw[0, 0], pieces[0][:])
-            pieces.append(sb("w1_bf0_10", [P, P * PACK // 2], BF16))
-            pieces.append(in_w1_room("w1_bf0_11", [P, P * PACK // 2], BF16, BIAS_AT + 832))
-            for s in range(2):
-                round_pass(on_vector, w1_raw[0, 1][:, :, s * P // 2 : (s + 1) * P // 2], pieces[1 + s][:])
-            return pieces
-
-        def round_later(t, passes, rounded):
-            for s, g in enumerate(passes):
-                round_pass(on_scalar, w1_raw[t, g], rounded[:, s * P * PACK : (s + 1) * P * PACK])
-            return [rounded]
-
-        def quantise_w1(t, first, pieces):
-            at = first * P
-            for piece in pieces:
-                cols = slice(at, at + piece.shape[1] // PACK)
-                nc.vector.quantize_mx(out=w1_codes[t][:, cols].bitcast(FP8X4), scales=w1_sc[t][:, cols], in_=piece[:, :])
-                at = cols.stop
+        def quantise_w1(t, first, piece):
+            cols = slice(first, first + piece.shape[1] // PACK)
+            nc.vector.quantize_mx(out=w1_codes[t][:, cols].bitcast(FP8X4), scales=w1_sc[t][:, cols], in_=piece)
 
         def multiply(t, passes, us):
             n = T // len(us)
@@ -154,73 +155,89 @@ def tile_picked_wlapl_gelu_lo_kernel(tc, x_words, x_scales, w1, w2, gate, pos1, 
                         stop=(g == PASSES - 1),
                     )
 
-        def make_h(t, us):
+        def make_h(t, us, bias=0.0):
             n = T // len(us)
             whole = t < 2
-            h[t] = sb("h%d" % t, [P, T + (SPARE if whole else 0)], F32)
+            shape = [P, T + (SPARE if whole else 0)]
+            if t == LAST:
+                h[t] = place("h3", shape, F32, span["w2_raw0"][0] + 1024)
+            else:
+                h[t] = under(("", "w1_raw2_1", "w2_raw0")[t], "h%d" % t, shape, F32) if t else sb("h0", shape, F32)
             if whole:
                 nc.gpsimd.memset(h[t][:, T:], 0.0)
             for s, u in enumerate(us):
-                nc.scalar.activation(
-                    out=h[t][:, s * n : (s + 1) * n], in_=u, func=ACT.Gelu_apprx_tanh, bias=bias[t] if whole else 0.0
-                )
+                nc.scalar.activation(out=h[t][:, s * n : (s + 1) * n], in_=u, func=ACT.Gelu_apprx_tanh, bias=bias)
 
-        def first_layer(t, pieces, us):
-            quantise_w1(t, 0, pieces)
-            multiply(t, range(PASSES), us)
-            make_h(t, us)
+        def round_tile(t):
+            rounded = sb("w1_bf%d" % t, [P, K], BF16)
+            for g in range(PASSES):
+                round_pass(on_scalar, w1_raw[t, g], rounded[:, g * P * PACK : (g + 1) * P * PACK])
+            return rounded[:]
 
-        zT = sb("zT", [P, T // P, 2, 2 * P], BF16)
+        zT = {}
         home = {}
+        added = {}
 
-        def sums_in(columns, t, blocks):
+        def sums_in(number, t, blocks):
+            columns = bank(number, "sums%d_%d" % (t, blocks[0]), [P, len(blocks) * P])[:]
+            added[t, blocks] = 0
             for block in blocks:
                 home[t, block] = (columns, blocks)
 
-        def add_term(t, block, d, term):
-            columns, blocks = home[t, block]
-            mine = columns[:, (block - blocks[0]) * P : (block - blocks[0] + 1) * P]
-            summands = [term]
-            if d == (1 if t == 0 else 0):
-                summands.insert(0, h[t][:, block * P : (block + 1) * P])
-            last = d == D - 1 and block == blocks[-1]
-            for s, summand in enumerate(summands):
-                first = d == 0 and s == 0 and block == blocks[0]
-                nc.tensor.matmul(mine, lhsT=summand, rhs=ident[:], start=first, stop=last, is_transpose=True)
-            if last:
-                nc.scalar.copy(
-                    out=zT[:, blocks[0] : block + 1, :, 64 * t : 64 * (t + 1)].rearrange("p b u (q e) -> p b u q e", e=2),
-                    in_=columns.rearrange("p (b q u e) -> p b u q e", q=32, u=2, e=2),
-                )
+        def add(t, v0, summand):
+            for at in range(0, summand.shape[1], P):
+                block = (v0 + at) // P
+                columns, blocks = home[t, block]
+                mine = columns[:, (block - blocks[0]) * P : (block - blocks[0] + 1) * P]
+                count = added[t, blocks]
+                added[t, blocks] = count + 1
+                last = count + 1 == (D + 1) * len(blocks)
+                nc.tensor.matmul(mine, lhsT=summand[:, at : at + P], rhs=ident[:], start=count == 0, stop=last, is_transpose=True)
 
-        def terms_tile(name, columns, room=None):
-            return sb(name, [P, columns], F32, room)[:]
+        def add_own(t, v0, n):
+            add(t, v0, h[t][:, v0 : v0 + n])
+
+        def round_z(t, first, count):
+            columns, blocks = home[t, first]
+            sums = columns[:, (first - blocks[0]) * P : (first - blocks[0] + count) * P]
+            place_z = zT[first // 2][:, first % 2 : first % 2 + count, :, 64 * t : 64 * (t + 1)]
+            nc.scalar.copy(
+                out=place_z.rearrange("p b u (q e) -> p b u q e", e=2),
+                in_=sums.rearrange("p (b q u e) -> p b u q e", q=32, u=2, e=2),
+            )
+
+        def looked_up(t, v0, d, n):
+            return h[t][:].indirect(lists[d][:, v0 // 16 : (v0 + n) // 16])
 
         def gather(t, v0, d, terms):
             n = terms.shape[1]
-            nc.vector.tensor_tensor(
-                out=terms,
-                in0=h[t][:].indirect(lists[d][:, v0 // 16 : (v0 + n) // 16]),
-                in1=neg_gate[d][:, v0 : v0 + n],
-                op=ALU.mult,
-            )
+            nc.vector.tensor_tensor(out=terms, in0=looked_up(t, v0, d, n), in1=neg_gate[d][:, v0 : v0 + n], op=ALU.mult)
 
-        def add_terms(t, v0, d, terms):
-            for at in range(0, terms.shape[1], P):
-                add_term(t, (v0 + at) // P, d, terms[:, at : at + P])
+        def gather_add(t, v0, d, terms):
+            gather(t, v0, d, terms)
+            add(t, v0, terms)
 
-        def gathers(t, v0, n, ds, terms):
-            for s, d in enumerate(ds):
-                gather(t, v0, d, terms[:, s * n : (s + 1) * n])
-                add_terms(t, v0, d, terms[:, s * n : (s + 1) * n])
+        def pick(t, v0, d, picked):
+            nc.scalar.activation(out=picked, in_=looked_up(t, v0, d, picked.shape[1]), func=ACT.Copy, scale=-1.0)
+            return picked
 
-        def turn_back(c, numbers):
-            words = zT[:].bitcast(F32)
-            z_bf = sb("z_bf%d" % c, [P, CHUNKS[c][1] * PACK], BF16)
+        def weigh_add(t, v0, d, picked, terms=None):
+            n = picked.shape[1]
+            if terms is None:
+                terms = sb("weighed%d_%d_%d" % (t, v0, d), [P, n], F32)[:]
+            nc.vector.tensor_tensor(out=terms, in0=picked, in1=gates[d][:, v0 : v0 + n], op=ALU.mult)
+            add(t, v0, terms)
+
+        def fresh(name, n):
+            return sb(name, [P, n], F32)[:]
+
+        def turn_back(c, numbers, z_bf):
             for b, number in enumerate(numbers):
+                block = CHUNKS[c][0] // P + b
+                words = zT[block // 2][:].bitcast(F32)
                 back = bank(number, "back%d_%d" % (c, b), [P, 2, P])
                 for u in range(2):
-                    nc.tensor.transpose(back[:, u, :], words[:, CHUNKS[c][0] // P + b, u, :], ident[:])
+                    nc.tensor.transpose(back[:, u, :], words[:, block % 2, u, :], ident[:])
                 nc.scalar.copy(
                     out=z_bf[:, b * P * PACK : (b + 1) * P * PACK].bitcast(F32).rearrange("p (v u) -> p v u", u=2),
                     in_=back[:].rearrange("p u v -> p v u"),
@@ -229,27 +246,24 @@ def tile_picked_wlapl_gelu_lo_kernel(tc, x_words, x_scales, w1, w2, gate, pos1, 
 
         w2_sc = sb("w2_sc", [P, H], U8)
 
-        def round_w2(room):
-            w2_bf = sb("w2_bf", [P, TILES, P, PACK], BF16, room)
-            for m0 in range(0, P, P // 2):
-                nc.scalar.copy(
-                    out=w2_bf[:, :, m0 : m0 + P // 2, :].rearrange("p t m j -> p m t j"),
-                    in_=w2_raw[:, :, TILES * m0 : TILES * (m0 + P // 2)].rearrange("p j (m t) -> p m t j", t=TILES),
-                )
-            return w2_bf
+        def round_w2(w2_bf, s):
+            nc.scalar.copy(
+                out=w2_bf[:, :, s * P // 2 : (s + 1) * P // 2, :].rearrange("p t m j -> p m t j"),
+                in_=w2_raw[s][:].rearrange("p j (m t) -> p m t j", t=TILES),
+            )
 
         y_codes = sb("y_codes", [P, T], U32)
         y_sc = sb("y_sc", [P, T], U8)
         out_rows = out_0.rearrange("(p t) v -> p t v", t=TILES)
         out_words = out_1[0].rearrange("p v r -> p (v r)").bitcast(I32)
 
-        def second_layer(c, w2_codes, z_bf, make_accs, copies):
-            v0, n = CHUNKS[c]
-            z_codes = sb("z_codes%d" % c, [P, n], U32) if c else in_w2_room("z_codes0", [P, n], U32, 0)
+        def second_layer(c, w2_codes, z_bf, numbers):
+            n = CHUNKS[c][1]
+            z_codes = sb("z_codes%d" % c, [P, n], U32)
             z_sc = sb("z_sc%d" % c, [P, n], U8)
             nc.vector.quantize_mx(out=z_codes[:].bitcast(FP8X4), scales=z_sc[:], in_=z_bf[:])
-            per_bank = TILES // len(copies)
-            accs = make_accs([per_bank, n])
+            per_bank = TILES // len(numbers)
+            accs = [bank(number, "acc%d_%d" % (c, number), [P, per_bank, n])[:] for number in numbers]
             for t in range(TILES):
                 nc.tensor.matmul_mx(
                     out=accs[t // per_bank][:, t % per_bank, :],
@@ -260,14 +274,16 @@ def tile_picked_wlapl_gelu_lo_kernel(tc, x_words, x_scales, w1, w2, gate, pos1, 
                     start=True,
                     stop=True,
                 )
+            return accs
+
+        def store_y(c, accs, copies):
+            v0, n = CHUNKS[c]
+            per_bank = TILES // len(accs)
             y = sb("y%d" % c, [P, TILES, n], F32)
             for s, copy in enumerate(copies):
                 copy(out=y[:, per_bank * s : per_bank * (s + 1), :], in_=accs[s])
             nc.sync.dma_start(out=out_rows[:, :, v0 : v0 + n], in_=y[:])
             return y
-
-        def in_banks(*numbers):
-            return lambda shape: [bank(number, "acc%d_%d" % (number, shape[1]), [P] + shape)[:] for number in numbers]
 
         def hand_on(c, y):
             v0, n = CHUNKS[c]
@@ -279,80 +295,127 @@ def tile_picked_wlapl_gelu_lo_kernel(tc, x_words, x_scales, w1, w2, gate, pos1, 
             nc.vector.quantize_mx(out=y_codes[:, v0 : v0 + n].bitcast(FP8X4), scales=y_sc[:, v0 : v0 + n], in_=y_bf[:])
             nc.sync.dma_start(out=out_words[:, v0 : v0 + n], in_=y_codes[:, v0 : v0 + n].bitcast(I32))
 
-        every = tuple(range(D))
-        half = T // 2
-        first_layer(0, round_first_tile(), [bank(s, "u0_%d" % s, [P, P])[:] for s in range(4)])
-        columns = [
-            in_w1_room("columns1", [P, 1, 4], F32, BIAS_AT + 832),
-            in_w1_room("columns23", [P, 2, 4], F32, BIAS_AT + 1152),
-        ]
-        nc.vector.tensor_scalar_mul(columns[0][:], gate_cols[:, :1, :], -1.0)
-        nc.vector.tensor_scalar_mul(columns[1][:], gate_cols[:, 1:, :], -1.0)
-        neg_gate[0] = sb("neg_gate0", [P, T], F32)[:]
-        nc.vector.tensor_scalar_mul(neg_gate[0], gate_raw[:], -1.0)
-        spreads = [spread_gate(columns[0][:, 0, :], 7), spread_gate(columns[1][:, 0, :], 6), spread_gate(columns[1][:, 1, :], 0)]
+        pieces = [sb("w1_bf0_0", [P, P * PACK], BF16)[:], sb("w1_bf0_1", [P, P * PACK // 2], BF16)[:]]
+        pieces.append(sb("w1_bf0_2", [P, P * PACK // 2], BF16)[:])
+        round_pass(on_vector, w1_raw[0, 0], pieces[0])
+        for s in range(2):
+            round_pass(on_vector, w1_raw[0, 1][:, :, s * P // 2 : (s + 1) * P // 2], pieces[1 + s])
+        for first, piece in zip((0, P, P + P // 2), pieces):
+            quantise_w1(0, first, piece)
+        u0 = [bank(s, "u0_%d" % s, [P, P])[:] for s in range(4)]
+        multiply(0, range(PASSES), u0)
+        make_h(0, u0, bias0[:, :1])
+        negate_gate(0, fresh("neg_gate0", T))
 
-        shared = [bank(4 + 2 * t, "shared%d" % t, [P, 2, T]) for t in range(2)]
-        for t in range(2):
-            sums_in(shared[t][:, 0, :], t, (0, 1, 2, 3))
-
-        fetch_gate(1, spreads[0], in_w1_room("neg_gate1", [P, T], F32, BIAS_AT + 64 - 2048)[:])
-        rounded = [round_later(1, (0,), in_w1_room("w1_bf1_0", [P, P * PACK], BF16, BIAS_AT + 64))]
-        fetch_gate(2, spreads[1], in_w1_room("neg_gate2", [P, T], F32, RAW1_AT[0] - 1536)[:])
-        rounded.append(round_later(1, (1,), in_w1_room("w1_bf1_1", [P, P * PACK], BF16, RAW1_AT[0] + 512)))
-        fetch_gate(3, spreads[2], in_w1_room("neg_gate3", [P, T], F32, RAW1_AT[1] - 1024)[:])
-        u1 = [shared[0][:, 1, :]]
-        gathers(0, 0, T, (0,), terms_tile("terms0a", T))
-        second = [terms_tile("terms0b", half), in_w1_room("terms0c", [P, half], F32, RAW1_AT[0] + 1536)[:]]
+        sums_in(4, 0, (0, 1, 2, 3))
+        add_own(0, 0, T)
+        picked = [pick(0, 0, 3, fresh("picked0_3", T))]
+        rounded = [over("bias0", "w1_bf1_0", [P, P * PACK], BF16)[:], sb("w1_bf1_1", [P, P * PACK], BF16)[:]]
         for g in range(PASSES):
-            gather(0, g * half, 1, second[g])
-            quantise_w1(1, g, rounded[g])
+            round_pass(on_scalar, w1_raw[1, g], rounded[g])
+        picked.append(pick(0, HALF, 2, under("w1_raw1_1", "picked0_2", [P, HALF], F32)[:]))
+        terms = fresh("terms0_0", T)
+        gather_add(0, 0, 0, terms[:, :HALF])
+        negate_gate(1, fresh("neg_gate1", T))
+        gather_add(0, HALF, 0, terms[:, HALF:])
+        second = [fresh("terms0_1a", HALF), under("w1_raw1_0", "terms0_1b", [P, HALF], F32)[:]]
+        u1 = [bank(5, "u1", [P, T])[:]]
+        for g in range(PASSES):
+            gather(0, g * HALF, 1, second[g])
+            quantise_w1(1, g * P, rounded[g])
             multiply(1, (g,), u1)
+        rounded = [round_tile(2)]
         make_h(1, u1)
         for g in range(PASSES):
-            add_terms(0, g * half, 1, second[g])
-        gathers(0, 0, T, (2, 3), in_w1_room("terms0d", [P, 2 * T], F32, RAW1_AT[1] + 1024)[:])
+            add(0, g * HALF, second[g])
+        held = over("w1_raw1_1", "held0", [P, 2 * T + HALF], F32)
+        negate_gate(2, held[:, T : 2 * T])
+        weigh_add(0, 0, 3, picked[0], held[:, :T])
+        rounded.append(round_tile(3))
+        gather_add(0, 0, 2, held[:, 2 * T :])
+        weigh_add(0, HALF, 2, picked[1])
 
-        later = sb("w1_bf23", [P, 2 * PASSES * P * PACK], BF16, "bias1")
-        rounded = [round_later(t, range(PASSES), later[:, (t - 2) * K : (t - 1) * K]) for t in (2, 3)]
-        gathers(1, 0, T, (0,), terms_tile("terms1a", T))
-        first_layer(2, rounded[0], [shared[1][:, 1, :]])
-        gathers(1, 0, T, (1,), terms_tile("terms1b", T, "w1_raw2_1"))
-        first_layer(3, rounded[1], [bank(0, "u3", [P, T])[:]])
-        gathers(1, 0, T, (2, 3), terms_tile("terms1c", 2 * T, "w1_raw3_1"))
-        w2_bf = round_w2("w1_codes3")
+        sums_in(6, 1, (0, 1, 2, 3))
+        add_own(1, 0, T)
+        quantise_w1(2, 0, rounded[0])
+        u2 = [bank(0, "u2", [P, T])[:]]
+        multiply(2, range(PASSES), u2)
+        gather_add(1, 0, 0, fresh("terms1_0", T))
+        quantise_w1(3, 0, rounded[1])
+        u3 = [bank(1, "u3", [P, T])[:]]
+        multiply(3, range(PASSES), u3)
+        zT[0] = under("w1_raw3_0", "zT0", [P, 2, 2, 2 * P], BF16)
+        zT[1] = over("w1_raw3_0", "zT1", [P, 2, 2, 2 * P], BF16)
+        round_z(0, 0, 2)
+        round_z(0, 2, 2)
+        w2_bf = sb("w2_bf", [P, TILES, P, PACK], BF16)
+        round_w2(w2_bf, 0)
+        make_h(2, u2)
+        terms = over("w1_raw3_1", "terms1", [P, 3, T], F32)
+        gather_add(1, 0, 1, terms[:, 0, :])
+        picks = over("w2_raw0", "picks", [P, 5 * HALF], F32)
+        picked = [pick(1, 0, 3, picks[:, :T])]
+        make_h(3, u3)
+        gather_add(1, 0, 2, terms[:, 1, :])
 
-        sums_in(bank(1, "sums2a", [P, half])[:], 2, (0, 1))
-        gathers(2, 0, half, every, terms_tile("terms2a", D * half))
+        sums_in(2, 2, (0, 1))
+        picked.append(pick(2, 0, 3, picks[:, T : T + HALF]))
+        add_own(2, 0, HALF)
+        for d in range(2):
+            gather_add(2, 0, d, terms[:, 2, d * HALF : (d + 1) * HALF])
+        weigh_add(1, 0, 3, picked[0])
+        terms = over("h1", "terms3a", [P, 3, HALF], F32)
+        gather_add(2, 0, 2, terms[:, 2, :])
+        weigh_add(2, 0, 3, picked[1])
+        picked = [pick(LAST, 0, d, picks[:, (6 - d) * HALF : (7 - d) * HALF]) for d in (3, 2)]
+        round_z(1, 0, 2)
+        round_z(1, 2, 2)
+        round_w2(w2_bf, 1)
+        round_z(2, 0, 2)
+        sums_in(3, LAST, (0,))
+        sums_in(7, LAST, (1,))
+        add_own(LAST, 0, HALF)
+        gather_add(LAST, 0, 0, terms[:, 0, :])
+        weigh_add(LAST, 0, 3, picked[0])
+        weigh_add(LAST, 0, 2, picked[1])
         for block in range(2):
-            sums_in(bank(2 + block, "last_sums%d" % block, [P, P])[:], LAST, (block,))
-        terms = terms_tile("terms3a", D * half)
-        gathers(LAST, 0, half, every[:-1], terms[:, : (D - 1) * half])
-        for block in range(2):
-            at = (D - 1) * half + block * P
-            gathers(LAST, block * P, P, every[-1:], terms[:, at : at + P])
-        z_first = turn_back(0, (4, 5))
+            gather_add(LAST, block * P, 1, terms[:, 1, block * P : (block + 1) * P])
+            round_z(LAST, block, 1)
+        picked = pick(2, HALF, 3, fresh("picked2b_3", HALF))
+        z_first = turn_back(0, (4, 5), host("z_bf0", [P, HALF * PACK], BF16, above=3072))
 
-        sums_in(bank(6, "sums2b", [P, half])[:], 2, (2, 3))
-        rest = [in_w2_room("terms2b_%d" % d, [P, half], F32, d * half * 4)[:] for d in range(D)]
-        for d in range(D - 1):
-            gathers(2, half, half, (d,), rest[d])
-        w2_codes = sb("w2_codes", [P, H], U32, "terms3a")
+        sums_in(7, 2, (2, 3))
+        add_own(2, HALF, HALF)
+        w2_codes = over("terms3a", "w2_codes", [P, H], U32)
         nc.vector.quantize_mx(out=w2_codes[:].bitcast(FP8X4), scales=w2_sc[:], in_=w2_bf[:].rearrange("p t m j -> p (t m j)"))
-        y_first = second_layer(0, w2_codes, z_first, in_banks(0, 1), (on_scalar, on_scalar))
-        gathers(2, half, half, (D - 1,), rest[D - 1])
-
-        last_terms = terms_tile("terms3b", 2 * D * P, "z_bf0")
-        sums_in(bank(7, "sums_second", [P, P])[:], LAST, (2,))
-        gathers(LAST, CHUNKS[1][0], P, every, last_terms[:, : D * P])
-        z_second = turn_back(1, (3,))
-        sums_in(bank(2, "sums_third", [P, P])[:], LAST, (3,))
-        gathers(LAST, CHUNKS[2][0], P, every, last_terms[:, D * P :])
-        z_third = turn_back(2, (7,))
+        terms = over("w2_raw1", "terms2b", [P, 2, HALF], F32)
+        for d in range(2):
+            gather_add(2, HALF, d, terms[:, d, :])
+        weigh_add(2, HALF, 3, picked)
+        late = place("picked_late", [P, 2, HALF], F32, span["zT0"][0] + LAP - 2048)
+        picked = [pick(2, HALF, 2, late[:, 0, :]), pick(LAST, HALF, 3, late[:, 1, :])]
+        acc_first = second_layer(0, w2_codes, z_first, (1, 2))
+        weigh_add(2, HALF, 2, picked[0])
+        round_z(2, 2, 2)
+        y_first = store_y(0, acc_first, (on_scalar, on_scalar))
+        sums_in(3, LAST, (2,))
+        sums_in(0, LAST, (3,))
+        add_own(LAST, HALF, HALF)
+        terms = over("z_bf0", "terms3b", [P, 3, HALF], F32)
+        for d in range(2):
+            gather_add(LAST, 2 * P, d, terms[:, d, :P])
+        weigh_add(LAST, HALF, 3, picked[1])
+        gather_add(LAST, 2 * P, 2, terms[:, 2, :P])
+        round_z(LAST, 2, 1)
+        z_second = turn_back(1, (6,), sb("z_bf1", [P, P * PACK], BF16))
+        for d in range(3):
+            gather_add(LAST, 3 * P, d, terms[:, d, P:])
+        round_z(LAST, 3, 1)
+        z_third = turn_back(2, (3,), sb("z_bf2", [P, P * PACK], BF16))
 
         hand_on(0, y_first)
-        hand_on(1, second_layer(1, w2_codes, z_second, in_banks(2), (on_scalar,)))
-        hand_on(2, second_layer(2, w2_codes, z_third, in_banks(4, 5), (on_scalar, on_vector)))
+        hand_on(1, store_y(1, second_layer(1, w2_codes, z_second, (0,)), (on_scalar,)))
+        hand_on(2, store_y(2, second_layer(2, w2_codes, z_third, (4, 5)), (on_scalar, on_vector)))
 
         for q in range(4):
             queue = nc.scalar if q % 2 else nc.sync

@@ -92,24 +92,23 @@ def tile_picked_wlapl_gelu_lo_kernel(tc, x_words, x_scales, w1, w2, gate, pos1, 
             )
         x_w = sb("x_w", [P, PASSES, 2 * T], U8)
         nc.sync.dma_start(out=x_w[:].bitcast(I32), in_=x_words.bitcast(I32).rearrange("g p c -> p g c"))
-        gates = [sb("gate%d" % d, [P, T], F32) for d in range(D)]
-        nc.sync.dma_start(out=gates[0][:], in_=gate[0])
         nc.scalar.activation(out=bias0[:, :1], in_=zero[:], func=ACT.Gelu_apprx_tanh)
         def load_list(d):
             nc.sync.dma_start(out=lists[d][:], in_=pos[d])
 
-        def load_gate(d):
-            nc.sync.dma_start(out=gates[d][:], in_=gate[d])
+        def load_gates(pair, first):
+            nc.sync.dma_start(out=pair[:], in_=gate[first : first + 2].rearrange("d p v -> p d v"))
 
+        gate_pairs = [host("gates01", [P, 2, T], F32, above=2048), sb("gates23", [P, 2, T], F32)]
         load_list(0)
-        load_list(3)
+        load_gates(gate_pairs[0], 0)
         load_w1(host("w1_raw1_0", [P, PACK, P], F32, below=1024), 1, 0)
-        load_gate(1)
-        load_list(1)
+        load_list(3)
         load_w1(host("w1_raw1_1", [P, PACK, P], F32, below=1024, above=5120), 1, 1)
-        load_gate(3)
+        load_list(1)
+        load_gates(gate_pairs[1], 2)
         load_list(2)
-        load_gate(2)
+        gates = {d: gate_pairs[1][:, d - 2, :] for d in (2, 3)}
         load_w1(sb("w1_raw2_0", [P, PACK, P], F32), 2, 0)
         load_w1(host("w1_raw2_1", [P, PACK, P], F32, below=2176, above=3072), 2, 1)
         load_w1(host("w1_raw3_0", [P, PACK, P], F32, below=5120, above=2048), 3, 0)
@@ -125,7 +124,7 @@ def tile_picked_wlapl_gelu_lo_kernel(tc, x_words, x_scales, w1, w2, gate, pos1, 
 
         def negate_gate(d, negated):
             neg_gate[d] = negated
-            nc.vector.tensor_scalar_mul(neg_gate[d], gates[d][:], -1.0)
+            nc.vector.tensor_scalar_mul(neg_gate[d], gates[d], -1.0)
 
         w1_codes = [sb("w1_codes%d" % t, [P, PASSES * P], U32) for t in range(TILES)]
         w1_sc = [sb("w1_sc%d" % t, [P, PASSES * P], U8) for t in range(TILES)]
@@ -248,8 +247,8 @@ def tile_picked_wlapl_gelu_lo_kernel(tc, x_words, x_scales, w1, w2, gate, pos1, 
 
         def round_w2(w2_bf, s):
             nc.scalar.copy(
-                out=w2_bf[:, :, s * P // 2 : (s + 1) * P // 2, :].rearrange("p t m j -> p m t j"),
-                in_=w2_raw[s][:].rearrange("p j (m t) -> p m t j", t=TILES),
+                out=w2_bf[:, :, s * P // 2 : (s + 1) * P // 2, :].rearrange("p t m j -> p m j t"),
+                in_=w2_raw[s][:].rearrange("p j (m t) -> p m j t", t=TILES),
             )
 
         y_codes = sb("y_codes", [P, T], U32)
@@ -305,7 +304,10 @@ def tile_picked_wlapl_gelu_lo_kernel(tc, x_words, x_scales, w1, w2, gate, pos1, 
         u0 = [bank(s, "u0_%d" % s, [P, P])[:] for s in range(4)]
         multiply(0, range(PASSES), u0)
         make_h(0, u0, bias0[:, :1])
-        negate_gate(0, fresh("neg_gate0", T))
+        negated = sb("neg_gates01", [P, 2, T], F32)
+        nc.vector.tensor_scalar_mul(negated[:], gate_pairs[0][:], -1.0)
+        for d in range(2):
+            neg_gate[d] = negated[:, d, :]
 
         sums_in(4, 0, (0, 1, 2, 3))
         add_own(0, 0, T)
@@ -314,10 +316,7 @@ def tile_picked_wlapl_gelu_lo_kernel(tc, x_words, x_scales, w1, w2, gate, pos1, 
         for g in range(PASSES):
             round_pass(on_scalar, w1_raw[1, g], rounded[g])
         picked.append(pick(0, HALF, 2, under("w1_raw1_1", "picked0_2", [P, HALF], F32)[:]))
-        terms = fresh("terms0_0", T)
-        gather_add(0, 0, 0, terms[:, :HALF])
-        negate_gate(1, fresh("neg_gate1", T))
-        gather_add(0, HALF, 0, terms[:, HALF:])
+        gather_add(0, 0, 0, over("gates01", "terms0_0", [P, T], F32)[:])
         second = [fresh("terms0_1a", HALF), under("w1_raw1_0", "terms0_1b", [P, HALF], F32)[:]]
         u1 = [bank(5, "u1", [P, T])[:]]
         for g in range(PASSES):

@@ -71,7 +71,7 @@ def tile_picked_wlapl_gelu_lo_kernel(tc, x_words, x_scales, w1, w2, gate, pos1, 
         nc.gpsimd.memset(x_sc[:].bitcast(I32), 0)
         zero = sb("zero", [P, 1], F32)
         nc.gpsimd.memset(zero[:], 0.0)
-        bias0 = host("bias0", [P, 32], F32, below=2048, above=1024)
+        bias0 = host("bias0", [P, 32], F32, below=8192, above=1024)
 
         w1_raw = {}
 
@@ -82,6 +82,8 @@ def tile_picked_wlapl_gelu_lo_kernel(tc, x_words, x_scales, w1, w2, gate, pos1, 
                 w1_raw[t + s, g] = raw[:, :, s * P : (s + 1) * P]
 
         pos = (pos1, pos2, pos3, pos4)
+        gate_cols = sb("gate_cols", [P, D, 4], F32)
+        nc.sync.dma_start(out=gate_cols[:], in_=gate[:, 0, :].rearrange("d (n m) -> n d m", m=4))
         for g in range(PASSES):
             load_w1(sb("w1_raw0_%d" % g, [P, PACK, P], F32), 0, g)
         x_sc_rows = x_sc[:].bitcast(I32).rearrange("p (g c) -> p g c", g=PASSES)
@@ -96,21 +98,13 @@ def tile_picked_wlapl_gelu_lo_kernel(tc, x_words, x_scales, w1, w2, gate, pos1, 
         def load_list(d):
             nc.sync.dma_start(out=lists[d][:], in_=pos[d])
 
-        def load_gates(pair, first):
-            nc.sync.dma_start(out=pair[:], in_=gate[first : first + 2].rearrange("d p v -> p d v"))
-
-        gate_pairs = [host("gates01", [P, 2, T], F32, above=2048), sb("gates23", [P, 2, T], F32)]
+        load_w1(host("w1_raw1_0", [P, PACK, P], F32, above=2048), 1, 0)
         load_list(0)
-        load_gates(gate_pairs[0], 0)
-        load_w1(host("w1_raw1_0", [P, PACK, P], F32, below=1024), 1, 0)
-        load_list(3)
-        load_w1(host("w1_raw1_1", [P, PACK, P], F32, below=1024, above=5120), 1, 1)
-        load_list(1)
-        load_gates(gate_pairs[1], 2)
-        load_list(2)
-        gates = {d: gate_pairs[1][:, d - 2, :] for d in (2, 3)}
-        load_w1(sb("w1_raw2_0", [P, PACK, P], F32), 2, 0)
-        load_w1(host("w1_raw2_1", [P, PACK, P], F32, below=2176, above=3072), 2, 1)
+        load_w1(host("w1_raw1_1", [P, PACK, P], F32, below=1024, above=4096), 1, 1)
+        for d in (3, 1, 2):
+            load_list(d)
+        for g in range(PASSES):
+            load_w1(sb("w1_raw2_%d" % g, [P, PACK, P], F32), 2, g)
         load_w1(host("w1_raw3_0", [P, PACK, P], F32, below=5120, above=2048), 3, 0)
         load_w1(host("w1_raw3_1", [P, PACK, P], F32, below=2048, above=6144), 3, 1)
         w2_raw = [host("w2_raw%d" % s, [P, PACK, H // 2], F32, below=2048, above=5120) for s in range(2)]
@@ -122,9 +116,13 @@ def tile_picked_wlapl_gelu_lo_kernel(tc, x_words, x_scales, w1, w2, gate, pos1, 
 
         neg_gate = {}
 
-        def negate_gate(d, negated):
-            neg_gate[d] = negated
-            nc.vector.tensor_scalar_mul(neg_gate[d], gates[d], -1.0)
+        def spread_gate(d, spread):
+            for m in range(4):
+                nc.tensor.transpose(spread[:, m * P : (m + 1) * P], gate_cols[:, d, m : m + 1].to_broadcast([P, P]), ident[:])
+            return spread.rearrange("p (m n) -> p n m", m=4)
+
+        def by_four(columns):
+            return columns.rearrange("p (n m) -> p n m", m=4)
 
         w1_codes = [sb("w1_codes%d" % t, [P, PASSES * P], U32) for t in range(TILES)]
         w1_sc = [sb("w1_sc%d" % t, [P, PASSES * P], U8) for t in range(TILES)]
@@ -140,38 +138,46 @@ def tile_picked_wlapl_gelu_lo_kernel(tc, x_words, x_scales, w1, w2, gate, pos1, 
             cols = slice(first, first + piece.shape[1] // PACK)
             nc.vector.quantize_mx(out=w1_codes[t][:, cols].bitcast(FP8X4), scales=w1_sc[t][:, cols], in_=piece)
 
+        def parts(us):
+            first = 0
+            for s, u in enumerate(us):
+                us[s] = (first, u.shape[1], u)
+                first = first + u.shape[1]
+            return us
+
         def multiply(t, passes, us):
-            n = T // len(us)
             for g in passes:
-                for s, u in enumerate(us):
+                for first, n, u in parts(list(us)):
                     nc.tensor.matmul_mx(
                         out=u,
                         lhsT=w1_codes[t][:, g * P : (g + 1) * P].bitcast(FP8X4),
                         lhsT_scale=w1_sc[t][:, g * P : (g + 1) * P],
-                        rhs=x_w[:, g, 2 * s * n : 2 * (s + 1) * n].bitcast(FP4X4),
-                        rhs_scale=x_sc[:, g * T + s * n : g * T + (s + 1) * n],
+                        rhs=x_w[:, g, 2 * first : 2 * (first + n)].bitcast(FP4X4),
+                        rhs_scale=x_sc[:, g * T + first : g * T + first + n],
                         start=(g == 0),
                         stop=(g == PASSES - 1),
                     )
 
         def make_h(t, us, bias=0.0):
-            n = T // len(us)
             whole = t < 2
             shape = [P, T + (SPARE if whole else 0)]
             if t == LAST:
                 h[t] = place("h3", shape, F32, span["w2_raw0"][0] + 1024)
+            elif t == 2:
+                h[t] = under("w2_raw0", "h2", shape, F32)
+            elif t == 1:
+                h[t] = host("h1", shape, F32, above=5120)
             else:
-                h[t] = under(("", "w1_raw2_1", "w2_raw0")[t], "h%d" % t, shape, F32) if t else sb("h0", shape, F32)
+                h[t] = sb("h0", shape, F32)
             if whole:
                 nc.gpsimd.memset(h[t][:, T:], 0.0)
-            for s, u in enumerate(us):
-                nc.scalar.activation(out=h[t][:, s * n : (s + 1) * n], in_=u, func=ACT.Gelu_apprx_tanh, bias=bias)
+            for first, n, u in parts(list(us)):
+                nc.scalar.activation(out=h[t][:, first : first + n], in_=u, func=ACT.Gelu_apprx_tanh, bias=bias)
 
-        def round_tile(t):
-            rounded = sb("w1_bf%d" % t, [P, K], BF16)
+        def round_tile(t, rounded):
             for g in range(PASSES):
                 round_pass(on_scalar, w1_raw[t, g], rounded[:, g * P * PACK : (g + 1) * P * PACK])
-            return rounded[:]
+            return rounded
 
         zT = {}
         home = {}
@@ -217,14 +223,17 @@ def tile_picked_wlapl_gelu_lo_kernel(tc, x_words, x_scales, w1, w2, gate, pos1, 
             add(t, v0, terms)
 
         def pick(t, v0, d, picked):
-            nc.scalar.activation(out=picked, in_=looked_up(t, v0, d, picked.shape[1]), func=ACT.Copy, scale=-1.0)
+            nc.scalar.activation(out=picked, in_=looked_up(t, v0, d, picked.shape[1]), func=ACT.Copy, scale=-1.0 if d == LAST else 1.0)
             return picked
 
         def weigh_add(t, v0, d, picked, terms=None):
             n = picked.shape[1]
             if terms is None:
                 terms = sb("weighed%d_%d_%d" % (t, v0, d), [P, n], F32)[:]
-            nc.vector.tensor_tensor(out=terms, in0=picked, in1=gates[d][:, v0 : v0 + n], op=ALU.mult)
+            if d == LAST:
+                nc.vector.tensor_tensor(out=by_four(terms), in0=by_four(picked), in1=last_gate[:, v0 // 4 : (v0 + n) // 4, :], op=ALU.mult)
+            else:
+                nc.vector.tensor_tensor(out=terms, in0=picked, in1=neg_gate[d][:, v0 : v0 + n], op=ALU.mult)
             add(t, v0, terms)
 
         def fresh(name, n):
@@ -294,6 +303,9 @@ def tile_picked_wlapl_gelu_lo_kernel(tc, x_words, x_scales, w1, w2, gate, pos1, 
             nc.vector.quantize_mx(out=y_codes[:, v0 : v0 + n].bitcast(FP8X4), scales=y_sc[:, v0 : v0 + n], in_=y_bf[:])
             nc.sync.dma_start(out=out_words[:, v0 : v0 + n], in_=y_codes[:, v0 : v0 + n].bitcast(I32))
 
+        for d in range(3):
+            neg_gate[d] = fresh("neg_gate%d" % d, T)
+            nc.scalar.mul(by_four(neg_gate[d]), spread_gate(d, bank(d, "spread%d" % d, [P, T])[:]), -1.0)
         pieces = [sb("w1_bf0_0", [P, P * PACK], BF16)[:], sb("w1_bf0_1", [P, P * PACK // 2], BF16)[:]]
         pieces.append(sb("w1_bf0_2", [P, P * PACK // 2], BF16)[:])
         round_pass(on_vector, w1_raw[0, 0], pieces[0])
@@ -301,53 +313,50 @@ def tile_picked_wlapl_gelu_lo_kernel(tc, x_words, x_scales, w1, w2, gate, pos1, 
             round_pass(on_vector, w1_raw[0, 1][:, :, s * P // 2 : (s + 1) * P // 2], pieces[1 + s])
         for first, piece in zip((0, P, P + P // 2), pieces):
             quantise_w1(0, first, piece)
-        u0 = [bank(s, "u0_%d" % s, [P, P])[:] for s in range(4)]
+        u0 = [bank(s, "u0_%d" % s, [P, n])[:] for s, n in enumerate((HALF, P, P))]
         multiply(0, range(PASSES), u0)
         make_h(0, u0, bias0[:, :1])
-        negated = sb("neg_gates01", [P, 2, T], F32)
-        nc.vector.tensor_scalar_mul(negated[:], gate_pairs[0][:], -1.0)
-        for d in range(2):
-            neg_gate[d] = negated[:, d, :]
+        last_gate = spread_gate(3, bank(0, "spread3", [P, T])[:])
 
-        sums_in(4, 0, (0, 1, 2, 3))
+        sums_in(3, 0, (0, 1, 2, 3))
         add_own(0, 0, T)
+        u1 = [bank(2, "u1", [P, T])[:]]
+        rounded = [sb("w1_bf1_0", [P, P * PACK], BF16)[:], over("bias0", "w1_bf1_1", [P, P * PACK], BF16)[:]]
+        round_pass(on_vector, w1_raw[1, 0], rounded[0])
+        quantise_w1(1, 0, rounded[0])
+        multiply(1, (0,), u1)
         picked = [pick(0, 0, 3, fresh("picked0_3", T))]
-        rounded = [over("bias0", "w1_bf1_0", [P, P * PACK], BF16)[:], sb("w1_bf1_1", [P, P * PACK], BF16)[:]]
-        for g in range(PASSES):
-            round_pass(on_scalar, w1_raw[1, g], rounded[g])
+        round_pass(on_scalar, w1_raw[1, 1], rounded[1])
         picked.append(pick(0, HALF, 2, under("w1_raw1_1", "picked0_2", [P, HALF], F32)[:]))
-        gather_add(0, 0, 0, over("gates01", "terms0_0", [P, T], F32)[:])
-        second = [fresh("terms0_1a", HALF), under("w1_raw1_0", "terms0_1b", [P, HALF], F32)[:]]
-        u1 = [bank(5, "u1", [P, T])[:]]
-        for g in range(PASSES):
-            gather(0, g * HALF, 1, second[g])
-            quantise_w1(1, g * P, rounded[g])
-            multiply(1, (g,), u1)
-        rounded = [round_tile(2)]
+        gather_add(0, 0, 0, over("w1_raw1_0", "terms0_0", [P, T], F32)[:])
+        second = fresh("terms0_1a", HALF)
+        gather(0, 0, 1, second)
+        quantise_w1(1, P, rounded[1])
+        multiply(1, (1,), u1)
         make_h(1, u1)
-        for g in range(PASSES):
-            add(0, g * HALF, second[g])
-        held = over("w1_raw1_1", "held0", [P, 2 * T + HALF], F32)
-        negate_gate(2, held[:, T : 2 * T])
-        weigh_add(0, 0, 3, picked[0], held[:, :T])
-        rounded.append(round_tile(3))
-        gather_add(0, 0, 2, held[:, 2 * T :])
+        add(0, 0, second)
+        held = over("w1_raw1_1", "held0", [P, 2 * T], F32)
+        gather_add(0, HALF, 1, held[:, :HALF])
+        weigh_add(0, 0, 3, picked[0], held[:, T:])
+        later = under("bias0", "later_bf", [P, 4 * K], BF16)
+        rounded = [round_tile(t, later[:, (t - 2) * K : (t - 1) * K]) for t in (2, 3)]
+        gather_add(0, 0, 2, held[:, HALF:T])
         weigh_add(0, HALF, 2, picked[1])
 
-        sums_in(6, 1, (0, 1, 2, 3))
+        sums_in(5, 1, (0, 1, 2, 3))
         add_own(1, 0, T)
-        quantise_w1(2, 0, rounded[0])
-        u2 = [bank(0, "u2", [P, T])[:]]
-        multiply(2, range(PASSES), u2)
         gather_add(1, 0, 0, fresh("terms1_0", T))
+        quantise_w1(2, 0, rounded[0])
+        u2 = [bank(6, "u2", [P, T])[:]]
+        multiply(2, range(PASSES), u2)
         quantise_w1(3, 0, rounded[1])
-        u3 = [bank(1, "u3", [P, T])[:]]
+        u3 = [bank(7, "u3", [P, T])[:]]
         multiply(3, range(PASSES), u3)
         zT[0] = under("w1_raw3_0", "zT0", [P, 2, 2, 2 * P], BF16)
         zT[1] = over("w1_raw3_0", "zT1", [P, 2, 2, 2 * P], BF16)
         round_z(0, 0, 2)
         round_z(0, 2, 2)
-        w2_bf = sb("w2_bf", [P, TILES, P, PACK], BF16)
+        w2_bf = later[:, 2 * K :].rearrange("p (t m j) -> p t m j", t=TILES, j=PACK)
         round_w2(w2_bf, 0)
         make_h(2, u2)
         terms = over("w1_raw3_1", "terms1", [P, 3, T], F32)
@@ -357,7 +366,7 @@ def tile_picked_wlapl_gelu_lo_kernel(tc, x_words, x_scales, w1, w2, gate, pos1, 
         make_h(3, u3)
         gather_add(1, 0, 2, terms[:, 1, :])
 
-        sums_in(2, 2, (0, 1))
+        sums_in(1, 2, (0, 1))
         picked.append(pick(2, 0, 3, picks[:, T : T + HALF]))
         add_own(2, 0, HALF)
         for d in range(2):
@@ -371,8 +380,8 @@ def tile_picked_wlapl_gelu_lo_kernel(tc, x_words, x_scales, w1, w2, gate, pos1, 
         round_z(1, 2, 2)
         round_w2(w2_bf, 1)
         round_z(2, 0, 2)
-        sums_in(3, LAST, (0,))
-        sums_in(7, LAST, (1,))
+        sums_in(2, LAST, (0,))
+        sums_in(4, LAST, (1,))
         add_own(LAST, 0, HALF)
         gather_add(LAST, 0, 0, terms[:, 0, :])
         weigh_add(LAST, 0, 3, picked[0])
@@ -381,12 +390,12 @@ def tile_picked_wlapl_gelu_lo_kernel(tc, x_words, x_scales, w1, w2, gate, pos1, 
             gather_add(LAST, block * P, 1, terms[:, 1, block * P : (block + 1) * P])
             round_z(LAST, block, 1)
         picked = pick(2, HALF, 3, fresh("picked2b_3", HALF))
-        z_first = turn_back(0, (4, 5), host("z_bf0", [P, HALF * PACK], BF16, above=3072))
+        z_first = turn_back(0, (3, 5), host("z_bf0", [P, HALF * PACK], BF16, above=3072))
 
-        sums_in(7, 2, (2, 3))
+        sums_in(4, 2, (2, 3))
         add_own(2, HALF, HALF)
         w2_codes = over("terms3a", "w2_codes", [P, H], U32)
-        nc.vector.quantize_mx(out=w2_codes[:].bitcast(FP8X4), scales=w2_sc[:], in_=w2_bf[:].rearrange("p t m j -> p (t m j)"))
+        nc.vector.quantize_mx(out=w2_codes[:].bitcast(FP8X4), scales=w2_sc[:], in_=later[:, 2 * K :])
         terms = over("w2_raw1", "terms2b", [P, 2, HALF], F32)
         for d in range(2):
             gather_add(2, HALF, d, terms[:, d, :])
@@ -395,10 +404,10 @@ def tile_picked_wlapl_gelu_lo_kernel(tc, x_words, x_scales, w1, w2, gate, pos1, 
         picked = [pick(2, HALF, 2, late[:, 0, :]), pick(LAST, HALF, 3, late[:, 1, :])]
         acc_first = second_layer(0, w2_codes, z_first, (1, 2))
         weigh_add(2, HALF, 2, picked[0])
-        round_z(2, 2, 2)
         y_first = store_y(0, acc_first, (on_scalar, on_scalar))
-        sums_in(3, LAST, (2,))
-        sums_in(0, LAST, (3,))
+        round_z(2, 2, 2)
+        sums_in(6, LAST, (2,))
+        sums_in(7, LAST, (3,))
         add_own(LAST, HALF, HALF)
         terms = over("z_bf0", "terms3b", [P, 3, HALF], F32)
         for d in range(2):
@@ -406,15 +415,15 @@ def tile_picked_wlapl_gelu_lo_kernel(tc, x_words, x_scales, w1, w2, gate, pos1, 
         weigh_add(LAST, HALF, 3, picked[1])
         gather_add(LAST, 2 * P, 2, terms[:, 2, :P])
         round_z(LAST, 2, 1)
-        z_second = turn_back(1, (6,), sb("z_bf1", [P, P * PACK], BF16))
+        z_second = turn_back(1, (3,), sb("z_bf1", [P, P * PACK], BF16))
         for d in range(3):
             gather_add(LAST, 3 * P, d, terms[:, d, P:])
         round_z(LAST, 3, 1)
-        z_third = turn_back(2, (3,), sb("z_bf2", [P, P * PACK], BF16))
+        z_third = turn_back(2, (5,), sb("z_bf2", [P, P * PACK], BF16))
 
         hand_on(0, y_first)
-        hand_on(1, store_y(1, second_layer(1, w2_codes, z_second, (0,)), (on_scalar,)))
-        hand_on(2, store_y(2, second_layer(2, w2_codes, z_third, (4, 5)), (on_scalar, on_vector)))
+        hand_on(1, store_y(1, second_layer(1, w2_codes, z_second, (7,)), (on_scalar,)))
+        hand_on(2, store_y(2, second_layer(2, w2_codes, z_third, (1, 4)), (on_scalar, on_vector)))
 
         for q in range(4):
             queue = nc.scalar if q % 2 else nc.sync

@@ -98,9 +98,9 @@ def tile_picked_wlapl_gelu_lo_kernel(tc, x_words, x_scales, w1, w2, gate, pos1, 
         def load_list(d):
             nc.sync.dma_start(out=lists[d][:], in_=pos[d])
 
-        load_w1(host("w1_raw1_0", [P, PACK, P], F32, above=2048), 1, 0)
+        load_w1(sb("w1_raw1_0", [P, PACK, P], F32), 1, 0)
         load_list(0)
-        load_w1(host("w1_raw1_1", [P, PACK, P], F32, below=1024, above=4096), 1, 1)
+        load_w1(host("w1_raw1_1", [P, PACK, P], F32, above=2048), 1, 1)
         for d in (3, 1, 2):
             load_list(d)
         for g in range(PASSES):
@@ -166,7 +166,7 @@ def tile_picked_wlapl_gelu_lo_kernel(tc, x_words, x_scales, w1, w2, gate, pos1, 
             elif t == 2:
                 h[t] = under("w2_raw0", "h2", shape, F32)
             elif t == 1:
-                h[t] = host("h1", shape, F32, above=5120)
+                h[t] = host("h1", shape, F32, above=6144)
             else:
                 h[t] = sb("h0", shape, F32)
             if whole:
@@ -321,27 +321,21 @@ def tile_picked_wlapl_gelu_lo_kernel(tc, x_words, x_scales, w1, w2, gate, pos1, 
         sums_in(3, 0, (0, 1, 2, 3))
         add_own(0, 0, T)
         u1 = [bank(2, "u1", [P, T])[:]]
-        rounded = [sb("w1_bf1_0", [P, P * PACK], BF16)[:], over("bias0", "w1_bf1_1", [P, P * PACK], BF16)[:]]
+        rounded = [sb("w1_bf1_%d" % g, [P, P * PACK], BF16)[:] for g in range(PASSES)]
         round_pass(on_vector, w1_raw[1, 0], rounded[0])
         quantise_w1(1, 0, rounded[0])
         multiply(1, (0,), u1)
-        picked = [pick(0, 0, 3, fresh("picked0_3", T))]
-        round_pass(on_scalar, w1_raw[1, 1], rounded[1])
-        picked.append(pick(0, HALF, 2, under("w1_raw1_1", "picked0_2", [P, HALF], F32)[:]))
-        gather_add(0, 0, 0, over("w1_raw1_0", "terms0_0", [P, T], F32)[:])
-        second = fresh("terms0_1a", HALF)
-        gather(0, 0, 1, second)
+        round_pass(on_vector, w1_raw[1, 1], rounded[1])
+        picked = [pick(0, 0, d, fresh("picked0_%d" % d, T)) for d in (3, 2)]
+        gather_add(0, 0, 0, over("w1_raw1_1", "terms0_0", [P, T], F32)[:])
         quantise_w1(1, P, rounded[1])
         multiply(1, (1,), u1)
         make_h(1, u1)
-        add(0, 0, second)
-        held = over("w1_raw1_1", "held0", [P, 2 * T], F32)
-        gather_add(0, HALF, 1, held[:, :HALF])
-        weigh_add(0, 0, 3, picked[0], held[:, T:])
+        gather_add(0, 0, 1, fresh("terms0_1", T))
+        weigh_add(0, 0, 3, picked[0])
         later = under("bias0", "later_bf", [P, 4 * K], BF16)
         rounded = [round_tile(t, later[:, (t - 2) * K : (t - 1) * K]) for t in (2, 3)]
-        gather_add(0, 0, 2, held[:, HALF:T])
-        weigh_add(0, HALF, 2, picked[1])
+        weigh_add(0, 0, 2, picked[1])
 
         sums_in(5, 1, (0, 1, 2, 3))
         add_own(1, 0, T)
@@ -361,7 +355,7 @@ def tile_picked_wlapl_gelu_lo_kernel(tc, x_words, x_scales, w1, w2, gate, pos1, 
         make_h(2, u2)
         terms = over("w1_raw3_1", "terms1", [P, 3, T], F32)
         gather_add(1, 0, 1, terms[:, 0, :])
-        picks = over("w2_raw0", "picks", [P, 5 * HALF], F32)
+        picks = over("w2_raw0", "picks", [P, 2 * T], F32)
         picked = [pick(1, 0, 3, picks[:, :T])]
         make_h(3, u3)
         gather_add(1, 0, 2, terms[:, 1, :])
@@ -372,10 +366,10 @@ def tile_picked_wlapl_gelu_lo_kernel(tc, x_words, x_scales, w1, w2, gate, pos1, 
         for d in range(2):
             gather_add(2, 0, d, terms[:, 2, d * HALF : (d + 1) * HALF])
         weigh_add(1, 0, 3, picked[0])
-        terms = over("h1", "terms3a", [P, 3, HALF], F32)
+        terms = over("h1", "terms3a", [P, 4, HALF], F32)
         gather_add(2, 0, 2, terms[:, 2, :])
         weigh_add(2, 0, 3, picked[1])
-        picked = [pick(LAST, 0, d, picks[:, (6 - d) * HALF : (7 - d) * HALF]) for d in (3, 2)]
+        picked = pick(LAST, 0, 3, picks[:, T + HALF :])
         round_z(1, 0, 2)
         round_z(1, 2, 2)
         round_w2(w2_bf, 1)
@@ -384,8 +378,8 @@ def tile_picked_wlapl_gelu_lo_kernel(tc, x_words, x_scales, w1, w2, gate, pos1, 
         sums_in(4, LAST, (1,))
         add_own(LAST, 0, HALF)
         gather_add(LAST, 0, 0, terms[:, 0, :])
-        weigh_add(LAST, 0, 3, picked[0])
-        weigh_add(LAST, 0, 2, picked[1])
+        weigh_add(LAST, 0, 3, picked)
+        gather_add(LAST, 0, 2, terms[:, 3, :])
         for block in range(2):
             gather_add(LAST, block * P, 1, terms[:, 1, block * P : (block + 1) * P])
             round_z(LAST, block, 1)

@@ -99,9 +99,8 @@ def tile_picked_wlapl_gelu_lo_kernel(tc, x_words, x_scales, w1, w2, gate, pos1, 
             nc.sync.dma_start(out=lists[d][:], in_=pos[d])
 
         load_w1(sb("w1_raw1_0", [P, PACK, P], F32), 1, 0)
-        load_list(0)
         load_w1(host("w1_raw1_1", [P, PACK, P], F32, above=2048), 1, 1)
-        for d in (3, 1, 2):
+        for d in (0, 3, 1, 2):
             load_list(d)
         for g in range(PASSES):
             load_w1(sb("w1_raw2_%d" % g, [P, PACK, P], F32), 2, g)
@@ -394,23 +393,26 @@ def tile_picked_wlapl_gelu_lo_kernel(tc, x_words, x_scales, w1, w2, gate, pos1, 
         for d in range(2):
             gather_add(2, HALF, d, terms[:, d, :])
         weigh_add(2, HALF, 3, picked)
-        late = place("picked_late", [P, 2, HALF], F32, span["zT0"][0] + LAP - 2048)
-        picked = [pick(2, HALF, 2, late[:, 0, :]), pick(LAST, HALF, 3, late[:, 1, :])]
+        late = place("picked_late", [P, 3, HALF], F32, span["zT0"][0] + LAP - 3072)
+        picked = [pick(2, HALF, 2, late[:, 0, :]), pick(LAST, HALF, 3, late[:, 1, :]), pick(LAST, HALF, 2, late[:, 2, :])]
         acc_first = second_layer(0, w2_codes, z_first, (1, 2))
         weigh_add(2, HALF, 2, picked[0])
-        y_first = store_y(0, acc_first, (on_scalar, on_scalar))
         round_z(2, 2, 2)
+        y_first = sb("y0", [P, TILES, HALF], F32)
+        on_scalar(out=y_first[:, :2, :], in_=acc_first[0])
         sums_in(6, LAST, (2,))
         sums_in(7, LAST, (3,))
         add_own(LAST, HALF, HALF)
-        terms = over("z_bf0", "terms3b", [P, 3, HALF], F32)
+        terms = over("z_bf0", "terms3b", [P, 2, HALF], F32)
         for d in range(2):
             gather_add(LAST, 2 * P, d, terms[:, d, :P])
         weigh_add(LAST, HALF, 3, picked[1])
-        gather_add(LAST, 2 * P, 2, terms[:, 2, :P])
+        weigh_add(LAST, HALF, 2, picked[2])
         round_z(LAST, 2, 1)
+        on_scalar(out=y_first[:, 2:, :], in_=acc_first[1])
+        nc.sync.dma_start(out=out_rows[:, :, :HALF], in_=y_first[:])
         z_second = turn_back(1, (3,), sb("z_bf1", [P, P * PACK], BF16))
-        for d in range(3):
+        for d in range(2):
             gather_add(LAST, 3 * P, d, terms[:, d, P:])
         round_z(LAST, 3, 1)
         z_third = turn_back(2, (5,), sb("z_bf2", [P, P * PACK], BF16))

@@ -283,13 +283,15 @@ def tile_picked_wlapl_gelu_lo_kernel(tc, x_words, x_scales, w1, w2, gate, pos1, 
                 )
             return accs
 
-        def store_y(c, accs, copies):
+        def store_y(c, accs, copies, stores):
             v0, n = CHUNKS[c]
             per_bank = TILES // len(accs)
             y = sb("y%d" % c, [P, TILES, n], F32)
             for s, copy in enumerate(copies):
                 copy(out=y[:, per_bank * s : per_bank * (s + 1), :], in_=accs[s])
-            nc.sync.dma_start(out=out_rows[:, :, v0 : v0 + n], in_=y[:])
+            for first in range(0, TILES, TILES // stores):
+                rows = slice(first, first + TILES // stores)
+                nc.sync.dma_start(out=out_rows[:, rows, v0 : v0 + n], in_=y[:, rows, :])
             return y
 
         def hand_on(c, y):
@@ -300,7 +302,9 @@ def tile_picked_wlapl_gelu_lo_kernel(tc, x_words, x_scales, w1, w2, gate, pos1, 
                 in_=y[:].rearrange("p t (c i) -> p c t i", i=4),
             )
             nc.vector.quantize_mx(out=y_codes[:, v0 : v0 + n].bitcast(FP8X4), scales=y_sc[:, v0 : v0 + n], in_=y_bf[:])
-            nc.sync.dma_start(out=out_words[:, v0 : v0 + n], in_=y_codes[:, v0 : v0 + n].bitcast(I32))
+
+        def store_codes(v0):
+            nc.sync.dma_start(out=out_words[:, v0 : v0 + HALF], in_=y_codes[:, v0 : v0 + HALF].bitcast(I32))
 
         for d in range(3):
             neg_gate[d] = fresh("neg_gate%d" % d, T)
@@ -400,6 +404,7 @@ def tile_picked_wlapl_gelu_lo_kernel(tc, x_words, x_scales, w1, w2, gate, pos1, 
         round_z(2, 2, 2)
         y_first = sb("y0", [P, TILES, HALF], F32)
         on_scalar(out=y_first[:, :2, :], in_=acc_first[0])
+        nc.sync.dma_start(out=out_rows[:, :2, :HALF], in_=y_first[:, :2, :])
         sums_in(6, LAST, (2,))
         sums_in(7, LAST, (3,))
         add_own(LAST, HALF, HALF)
@@ -410,7 +415,7 @@ def tile_picked_wlapl_gelu_lo_kernel(tc, x_words, x_scales, w1, w2, gate, pos1, 
         weigh_add(LAST, HALF, 2, picked[2])
         round_z(LAST, 2, 1)
         on_scalar(out=y_first[:, 2:, :], in_=acc_first[1])
-        nc.sync.dma_start(out=out_rows[:, :, :HALF], in_=y_first[:])
+        nc.sync.dma_start(out=out_rows[:, 2:, :HALF], in_=y_first[:, 2:, :])
         z_second = turn_back(1, (3,), sb("z_bf1", [P, P * PACK], BF16))
         for d in range(2):
             gather_add(LAST, 3 * P, d, terms[:, d, P:])
@@ -418,8 +423,10 @@ def tile_picked_wlapl_gelu_lo_kernel(tc, x_words, x_scales, w1, w2, gate, pos1, 
         z_third = turn_back(2, (5,), sb("z_bf2", [P, P * PACK], BF16))
 
         hand_on(0, y_first)
-        hand_on(1, store_y(1, second_layer(1, w2_codes, z_second, (7,)), (on_scalar,)))
-        hand_on(2, store_y(2, second_layer(2, w2_codes, z_third, (1, 4)), (on_scalar, on_vector)))
+        store_codes(0)
+        hand_on(1, store_y(1, second_layer(1, w2_codes, z_second, (7, 6)), (on_scalar, on_scalar), 2))
+        hand_on(2, store_y(2, second_layer(2, w2_codes, z_third, (1, 4)), (on_scalar, on_vector), 1))
+        store_codes(HALF)
 
         for q in range(4):
             queue = nc.scalar if q % 2 else nc.sync

@@ -13,6 +13,7 @@ HALF = T // 2
 BANK = 2048
 LAP = 64
 SPARE = 16
+RUN = 16
 CHUNKS = ((0, 256), (256, 128), (384, 128))
 
 FLOPS = 2 * K * H * T + 2 * H * H * T
@@ -63,6 +64,9 @@ def tile_picked_wlapl_gelu_lo_kernel(tc, x_words, x_scales, w1, w2, gate, pos1, 
         def over(earlier, name, shape, dtype):
             return place(name, shape, dtype, span[earlier][1] - LAP)
 
+        def inside(earlier, name, shape, dtype, skip=0):
+            return place(name, shape, dtype, span[earlier][0] + 2 * LAP + skip)
+
         def bank(number, name, shape):
             return psum.tile(shape, F32, name=name, offset=number * BANK)
 
@@ -71,122 +75,95 @@ def tile_picked_wlapl_gelu_lo_kernel(tc, x_words, x_scales, w1, w2, gate, pos1, 
         nc.gpsimd.memset(x_sc[:].bitcast(I32), 0)
         zero = sb("zero", [P, 1], F32)
         nc.gpsimd.memset(zero[:], 0.0)
-        bias0 = host("bias0", [P, 32], F32, below=8192, above=1024)
+        bias0 = host("bias0", [P, 32], F32, above=1024)
 
         w1_raw = {}
 
-        def load_w1(raw, t, g):
-            rows = w1[g * P * PACK : (g + 1) * P * PACK, t * P : t * P + raw.shape[2]]
+        def load_w1(t, g, below=0, above=0):
+            raw = host("w1_raw%d_%d" % (t, g), [P, PACK, P], F32, below, above)
+            rows = w1[g * P * PACK : (g + 1) * P * PACK, t * P : (t + 1) * P]
             nc.sync.dma_start(out=raw[:], in_=rows.rearrange("(p j) c -> p j c", j=PACK))
-            for s in range(raw.shape[2] // P):
-                w1_raw[t + s, g] = raw[:, :, s * P : (s + 1) * P]
+            w1_raw[t, g] = raw[:]
 
-        pos = (pos1, pos2, pos3, pos4)
-        gate_cols = sb("gate_cols", [P, D, 4], F32)
-        nc.sync.dma_start(out=gate_cols[:], in_=gate[:, 0, :].rearrange("d (n m) -> n d m", m=4))
+        def load_list(d):
+            nc.sync.dma_start(out=lists[d][:], in_=(pos1, pos2, pos3, pos4)[d])
+
+        gate_runs = sb("gate_runs", [P, RUN], F32)
+        runs = gate.rearrange("d p (r m) -> (d p r) m", m=RUN)
+        nc.sync.dma_start(out=gate_runs[:], in_=runs[0 : runs.shape[0] : P + 1])
         for g in range(PASSES):
-            load_w1(sb("w1_raw0_%d" % g, [P, PACK, P], F32), 0, g)
+            load_w1(0, g)
         x_sc_rows = x_sc[:].bitcast(I32).rearrange("p (g c) -> p g c", g=PASSES)
         for q in range(4):
             nc.sync.dma_start(
                 out=x_sc_rows[32 * q : 32 * q + 4],
                 in_=x_scales.bitcast(I32)[:, 4 * q : 4 * q + 4, :].rearrange("g r c -> r g c"),
             )
-        x_w = sb("x_w", [P, PASSES, 2 * T], U8)
-        nc.sync.dma_start(out=x_w[:].bitcast(I32), in_=x_words.bitcast(I32).rearrange("g p c -> p g c"))
-        nc.scalar.activation(out=bias0[:, :1], in_=zero[:], func=ACT.Gelu_apprx_tanh)
-        def load_list(d):
-            nc.sync.dma_start(out=lists[d][:], in_=pos[d])
-
-        load_w1(sb("w1_raw1_0", [P, PACK, P], F32), 1, 0)
-        load_w1(host("w1_raw1_1", [P, PACK, P], F32, above=2048), 1, 1)
-        for d in (0, 3, 1, 2):
-            load_list(d)
+        x_w = [sb("x_w%d" % g, [P, 2 * T], U8) for g in range(PASSES)]
         for g in range(PASSES):
-            load_w1(sb("w1_raw2_%d" % g, [P, PACK, P], F32), 2, g)
-        load_w1(host("w1_raw3_0", [P, PACK, P], F32, below=5120, above=2048), 3, 0)
-        load_w1(host("w1_raw3_1", [P, PACK, P], F32, below=2048, above=6144), 3, 1)
-        w2_raw = [host("w2_raw%d" % s, [P, PACK, H // 2], F32, below=2048, above=5120) for s in range(2)]
+            nc.sync.dma_start(out=x_w[g][:].bitcast(I32), in_=x_words[g].bitcast(I32))
+        nc.scalar.activation(out=bias0[:, :1], in_=zero[:], func=ACT.Gelu_apprx_tanh)
+        load_w1(1, 0)
+        load_list(0)
+        load_list(3)
+        load_w1(1, 1, 2048, 4096)
+        load_list(1)
+        load_list(2)
+        load_w1(2, 0)
+        load_w1(2, 1, 2048, 4096)
+        load_w1(3, 0)
+        load_w1(3, 1, 2048, 4096)
+        w2_raw = [host("w2_raw%d" % s, [P, PACK, H // 2], F32, above=2048) for s in range(2)]
         for s in range(2):
             nc.sync.dma_start(out=w2_raw[s][:], in_=w2[:, s * H // 2 : (s + 1) * H // 2].rearrange("(p j) m -> p j m", j=PACK))
 
         ident = sb("ident", [P, P], F32)
         make_identity(nc, ident[:])
 
-        neg_gate = {}
-
-        def spread_gate(d, spread):
-            for m in range(4):
-                nc.tensor.transpose(spread[:, m * P : (m + 1) * P], gate_cols[:, d, m : m + 1].to_broadcast([P, P]), ident[:])
-            return spread.rearrange("p (m n) -> p n m", m=4)
-
-        def by_four(columns):
-            return columns.rearrange("p (n m) -> p n m", m=4)
-
-        w1_codes = [sb("w1_codes%d" % t, [P, PASSES * P], U32) for t in range(TILES)]
-        w1_sc = [sb("w1_sc%d" % t, [P, PASSES * P], U8) for t in range(TILES)]
+        w1_codes = [sb("w1_codes0", [P, PASSES * P], U32)]
+        for t in (1, 2):
+            w1_codes.append(place("w1_codes%d" % t, [P, PASSES * P], U32, span["w1_raw%d_1" % (t + 1)][1] + 4 * HALF - 2 * LAP))
+        w1_codes.append(host("w1_codes3", [P, PASSES * P], U32, above=4096))
+        w1_sc = [host("w1_sc%d" % t, [P, PASSES * P], U8, 8192 if t == 1 else 0, 2048 if t == 1 else 0) for t in range(TILES)]
         h = {}
 
-        def round_pass(copy, raw, rounded):
+        def interleave(copy, rounded, rows):
             copy(
                 out=rounded.rearrange("p (c i j) -> p c j i", i=4, j=PACK),
-                in_=raw.rearrange("p j (c i) -> p c j i", i=4),
+                in_=rows.rearrange("p j (c i) -> p c j i", i=4),
             )
+            return rounded
 
         def quantise_w1(t, first, piece):
             cols = slice(first, first + piece.shape[1] // PACK)
             nc.vector.quantize_mx(out=w1_codes[t][:, cols].bitcast(FP8X4), scales=w1_sc[t][:, cols], in_=piece)
 
         def parts(us):
-            first = 0
-            for s, u in enumerate(us):
-                us[s] = (first, u.shape[1], u)
-                first = first + u.shape[1]
-            return us
+            firsts = [sum(u.shape[1] for u in us[:s]) for s in range(len(us))]
+            return [(first, u.shape[1], u) for first, u in zip(firsts, us)]
 
         def multiply(t, passes, us):
             for g in passes:
-                for first, n, u in parts(list(us)):
+                for first, n, u in parts(us):
                     nc.tensor.matmul_mx(
                         out=u,
                         lhsT=w1_codes[t][:, g * P : (g + 1) * P].bitcast(FP8X4),
                         lhsT_scale=w1_sc[t][:, g * P : (g + 1) * P],
-                        rhs=x_w[:, g, 2 * first : 2 * (first + n)].bitcast(FP4X4),
+                        rhs=x_w[g][:, 2 * first : 2 * (first + n)].bitcast(FP4X4),
                         rhs_scale=x_sc[:, g * T + first : g * T + first + n],
                         start=(g == 0),
                         stop=(g == PASSES - 1),
                     )
 
-        def make_h(t, us, bias=0.0):
-            whole = t < 2
-            shape = [P, T + (SPARE if whole else 0)]
-            if t == LAST:
-                h[t] = place("h3", shape, F32, span["w2_raw0"][0] + 1024)
-            elif t == 2:
-                h[t] = under("w2_raw0", "h2", shape, F32)
-            elif t == 1:
-                h[t] = host("h1", shape, F32, above=6144)
-            else:
-                h[t] = sb("h0", shape, F32)
-            if whole:
-                nc.gpsimd.memset(h[t][:, T:], 0.0)
-            for first, n, u in parts(list(us)):
+        def make_h(t, us, tile, bias=0.0):
+            h[t] = tile
+            for first, n, u in parts(us):
                 nc.scalar.activation(out=h[t][:, first : first + n], in_=u, func=ACT.Gelu_apprx_tanh, bias=bias)
-
-        def round_tile(t, rounded):
-            for g in range(PASSES):
-                round_pass(on_scalar, w1_raw[t, g], rounded[:, g * P * PACK : (g + 1) * P * PACK])
-            return rounded
 
         zT = {}
         home = {}
+        across = {}
         added = {}
-
-        def sums_in(number, t, blocks):
-            columns = bank(number, "sums%d_%d" % (t, blocks[0]), [P, len(blocks) * P])[:]
-            added[t, blocks] = 0
-            for block in blocks:
-                home[t, block] = (columns, blocks)
 
         def add(t, v0, summand):
             for at in range(0, summand.shape[1], P):
@@ -197,6 +174,34 @@ def tile_picked_wlapl_gelu_lo_kernel(tc, x_words, x_scales, w1, w2, gate, pos1, 
                 added[t, blocks] = count + 1
                 last = count + 1 == (D + 1) * len(blocks)
                 nc.tensor.matmul(mine, lhsT=summand[:, at : at + P], rhs=ident[:], start=count == 0, stop=last, is_transpose=True)
+
+        def sums_in(number, t, blocks):
+            columns = bank(number, "sums%d_%d" % (t, blocks[0]), [P, len(blocks) * P])[:]
+            added[t, blocks] = 0
+            for block in blocks:
+                home[t, block] = (columns, blocks)
+
+        def sums_across(number, block, tiles):
+            columns = bank(number, "sums_of_block%d_%d" % (block, tiles[0]), [P, len(tiles) * P])[:]
+            added[block, tiles, "across"] = 0
+            for t in tiles:
+                across[t, block] = (columns, tiles)
+
+        def add_across(t, block, summand):
+            columns, tiles = across[t, block]
+            mine = columns[:, (t - tiles[0]) * P : (t - tiles[0] + 1) * P]
+            count = added[block, tiles, "across"]
+            added[block, tiles, "across"] = count + 1
+            last = count + 1 == (D + 1) * len(tiles)
+            nc.tensor.matmul(mine, lhsT=summand, rhs=ident[:], start=count == 0, stop=last, is_transpose=True)
+
+        def round_across(t, block):
+            columns, tiles = across[t, block]
+            place_z = zT[block // 2][:, block % 2, :, 64 * tiles[0] : 64 * (tiles[-1] + 1)]
+            nc.scalar.copy(
+                out=place_z.rearrange("p u (q e) -> p u q e", e=2),
+                in_=columns.rearrange("p (q u e) -> p u q e", u=2, e=2),
+            )
 
         def add_own(t, v0, n):
             add(t, v0, h[t][:, v0 : v0 + n])
@@ -213,221 +218,261 @@ def tile_picked_wlapl_gelu_lo_kernel(tc, x_words, x_scales, w1, w2, gate, pos1, 
         def looked_up(t, v0, d, n):
             return h[t][:].indirect(lists[d][:, v0 // 16 : (v0 + n) // 16])
 
-        def gather(t, v0, d, terms):
-            n = terms.shape[1]
-            nc.vector.tensor_tensor(out=terms, in0=looked_up(t, v0, d, n), in1=neg_gate[d][:, v0 : v0 + n], op=ALU.mult)
+        def fresh(name, n, dtype=F32):
+            return sb(name, [P, n], dtype)[:]
 
-        def gather_add(t, v0, d, terms):
-            gather(t, v0, d, terms)
-            add(t, v0, terms)
+        def gather(t, v0, d, n, terms=None):
+            if terms is None:
+                terms = fresh("terms%d_%d_%d" % (t, d, v0), n)
+            nc.vector.tensor_tensor(out=terms, in0=looked_up(t, v0, d, n), in1=neg_gate[:, d, v0 : v0 + n], op=ALU.mult)
+            return terms
 
-        def pick(t, v0, d, picked):
-            nc.scalar.activation(out=picked, in_=looked_up(t, v0, d, picked.shape[1]), func=ACT.Copy, scale=-1.0 if d == LAST else 1.0)
+        def pick(t, v0, d, n, picked=None):
+            if picked is None:
+                picked = fresh("picked%d_%d_%d" % (t, d, v0), n)
+            nc.scalar.activation(out=picked, in_=looked_up(t, v0, d, n), func=ACT.Copy)
             return picked
 
-        def weigh_add(t, v0, d, picked, terms=None):
+        def weigh(t, v0, d, picked, terms=None):
             n = picked.shape[1]
             if terms is None:
-                terms = sb("weighed%d_%d_%d" % (t, v0, d), [P, n], F32)[:]
-            if d == LAST:
-                nc.vector.tensor_tensor(out=by_four(terms), in0=by_four(picked), in1=last_gate[:, v0 // 4 : (v0 + n) // 4, :], op=ALU.mult)
-            else:
-                nc.vector.tensor_tensor(out=terms, in0=picked, in1=neg_gate[d][:, v0 : v0 + n], op=ALU.mult)
-            add(t, v0, terms)
+                terms = fresh("weighed%d_%d_%d" % (t, d, v0), n)
+            nc.vector.tensor_tensor(out=terms, in0=picked, in1=neg_gate[:, d, v0 : v0 + n], op=ALU.mult)
+            return terms
 
-        def fresh(name, n):
-            return sb(name, [P, n], F32)[:]
+        def gather_add(t, v0, d, n, terms=None):
+            add(t, v0, gather(t, v0, d, n, terms))
 
-        def turn_back(c, numbers, z_bf):
-            for b, number in enumerate(numbers):
-                block = CHUNKS[c][0] // P + b
-                words = zT[block // 2][:].bitcast(F32)
-                back = bank(number, "back%d_%d" % (c, b), [P, 2, P])
-                for u in range(2):
-                    nc.tensor.transpose(back[:, u, :], words[:, block % 2, u, :], ident[:])
-                nc.scalar.copy(
-                    out=z_bf[:, b * P * PACK : (b + 1) * P * PACK].bitcast(F32).rearrange("p (v u) -> p v u", u=2),
-                    in_=back[:].rearrange("p u v -> p v u"),
-                )
-            return z_bf
+        def weigh_add(t, v0, d, picked, terms=None):
+            add(t, v0, weigh(t, v0, d, picked, terms))
 
+        def turn_back(block, number):
+            words = zT[block // 2][:].bitcast(F32)
+            back = bank(number, "back%d" % block, [P, 2, P])
+            for u in range(2):
+                nc.tensor.transpose(back[:, u, :], words[:, block % 2, u, :], ident[:])
+            return back
+
+        def fetch_z(back, z_bf):
+            nc.scalar.copy(out=z_bf.bitcast(F32).rearrange("p (v u) -> p v u", u=2), in_=back[:].rearrange("p u v -> p v u"))
+
+        w2_codes = sb("w2_codes", [P, H], U32)
         w2_sc = sb("w2_sc", [P, H], U8)
-
-        def round_w2(w2_bf, s):
-            nc.scalar.copy(
-                out=w2_bf[:, :, s * P // 2 : (s + 1) * P // 2, :].rearrange("p t m j -> p m j t"),
-                in_=w2_raw[s][:].rearrange("p j (m t) -> p m j t", t=TILES),
-            )
-
         y_codes = sb("y_codes", [P, T], U32)
         y_sc = sb("y_sc", [P, T], U8)
         out_rows = out_0.rearrange("(p t) v -> p t v", t=TILES)
         out_words = out_1[0].rearrange("p v r -> p (v r)").bitcast(I32)
 
-        def second_layer(c, w2_codes, z_bf, numbers):
+        def round_w2(copy, w2_bf, s, count):
+            m = P // count
+            raw = w2_raw[s * 2 // count][:, :, (s * H // count) % HALF : (s * H // count) % HALF + H // count]
+            copy(
+                out=w2_bf[:, :, s * m : (s + 1) * m, :].rearrange("p t m j -> p m j t"),
+                in_=raw.rearrange("p j (m t) -> p m j t", t=TILES),
+            )
+
+        def quantise_z(c, z_bf):
             n = CHUNKS[c][1]
             z_codes = sb("z_codes%d" % c, [P, n], U32)
             z_sc = sb("z_sc%d" % c, [P, n], U8)
-            nc.vector.quantize_mx(out=z_codes[:].bitcast(FP8X4), scales=z_sc[:], in_=z_bf[:])
-            per_bank = TILES // len(numbers)
-            accs = [bank(number, "acc%d_%d" % (c, number), [P, per_bank, n])[:] for number in numbers]
+            nc.vector.quantize_mx(out=z_codes[:].bitcast(FP8X4), scales=z_sc[:], in_=z_bf)
+            return z_codes, z_sc
+
+        def second_layer(c, z, numbers):
+            n = CHUNKS[c][1]
+            accs = [bank(number, "acc%d_%d" % (c, number), [P, 2, n])[:] for number in numbers]
             for t in range(TILES):
                 nc.tensor.matmul_mx(
-                    out=accs[t // per_bank][:, t % per_bank, :],
+                    out=accs[t // 2][:, t % 2, :],
                     lhsT=w2_codes[:, t * P : (t + 1) * P].bitcast(FP8X4),
                     lhsT_scale=w2_sc[:, t * P : (t + 1) * P],
-                    rhs=z_codes[:].bitcast(FP8X4),
-                    rhs_scale=z_sc[:],
+                    rhs=z[0][:].bitcast(FP8X4),
+                    rhs_scale=z[1][:],
                     start=True,
                     stop=True,
                 )
             return accs
 
-        def store_y(c, accs, copies, stores):
-            v0, n = CHUNKS[c]
-            per_bank = TILES // len(accs)
-            y = sb("y%d" % c, [P, TILES, n], F32)
-            for s, copy in enumerate(copies):
-                copy(out=y[:, per_bank * s : per_bank * (s + 1), :], in_=accs[s])
-            for first in range(0, TILES, TILES // stores):
-                rows = slice(first, first + TILES // stores)
-                nc.sync.dma_start(out=out_rows[:, rows, v0 : v0 + n], in_=y[:, rows, :])
-            return y
+        y = [sb("y%d" % c, [P, TILES, n], F32) for c, (v0, n) in enumerate(CHUNKS)]
 
-        def hand_on(c, y):
+        def fetch_y(c, s, acc, copy, store):
             v0, n = CHUNKS[c]
-            y_bf = sb("y_bf%d" % c, [P, n * PACK], BF16)
-            nc.vector.tensor_copy(
-                out=y_bf[:].rearrange("p (c i t) -> p c t i", i=4, t=TILES),
-                in_=y[:].rearrange("p t (c i) -> p c t i", i=4),
-            )
-            nc.vector.quantize_mx(out=y_codes[:, v0 : v0 + n].bitcast(FP8X4), scales=y_sc[:, v0 : v0 + n], in_=y_bf[:])
+            copy(out=y[c][:, 2 * s : 2 * s + 2, :], in_=acc)
+            if store is not None:
+                nc.sync.dma_start(out=out_rows[:, store, v0 : v0 + n], in_=y[c][:, store, :])
+
+        def round_y(c):
+            return interleave(on_vector, fresh("y_bf%d" % c, CHUNKS[c][1] * PACK, BF16), y[c][:])
+
+        def quantise_y(c, y_bf):
+            v0, n = CHUNKS[c]
+            nc.vector.quantize_mx(out=y_codes[:, v0 : v0 + n].bitcast(FP8X4), scales=y_sc[:, v0 : v0 + n], in_=y_bf)
 
         def store_codes(v0):
             nc.sync.dma_start(out=out_words[:, v0 : v0 + HALF], in_=y_codes[:, v0 : v0 + HALF].bitcast(I32))
 
-        for d in range(3):
-            neg_gate[d] = fresh("neg_gate%d" % d, T)
-            nc.scalar.mul(by_four(neg_gate[d]), spread_gate(d, bank(d, "spread%d" % d, [P, T])[:]), -1.0)
-        pieces = [sb("w1_bf0_0", [P, P * PACK], BF16)[:], sb("w1_bf0_1", [P, P * PACK // 2], BF16)[:]]
-        pieces.append(sb("w1_bf0_2", [P, P * PACK // 2], BF16)[:])
-        round_pass(on_vector, w1_raw[0, 0], pieces[0])
+        neg_gate = sb("neg_gate", [P, D, T], F32)
+        for s in range(RUN // 4):
+            spread = bank(s, "spread%d" % s, [P, 4, P])
+            for m in range(4):
+                nc.tensor.transpose(spread[:, m, :], gate_runs[:, 4 * s + m : 4 * s + m + 1].to_broadcast([P, P]), ident[:])
+            nc.scalar.mul(
+                neg_gate[:].rearrange("p d (r m) -> p (d r) m", m=RUN)[:, :, 4 * s : 4 * s + 4],
+                spread[:].rearrange("p m n -> p n m"),
+                -1.0,
+            )
+        pieces = [fresh("w1_bf0_0", P * PACK, BF16), fresh("w1_bf0_1", P * PACK // 2, BF16), fresh("w1_bf0_2", P * PACK // 2, BF16)]
+        interleave(on_vector, pieces[0], w1_raw[0, 0])
+        quantise_w1(0, 0, pieces[0])
         for s in range(2):
-            round_pass(on_vector, w1_raw[0, 1][:, :, s * P // 2 : (s + 1) * P // 2], pieces[1 + s])
-        for first, piece in zip((0, P, P + P // 2), pieces):
-            quantise_w1(0, first, piece)
-        u0 = [bank(s, "u0_%d" % s, [P, n])[:] for s, n in enumerate((HALF, P, P))]
+            interleave(on_vector, pieces[1 + s], w1_raw[0, 1][:, :, s * P // 2 : (s + 1) * P // 2])
+        quantise_w1(0, P, pieces[1])
+        quantise_w1(0, P + P // 2, pieces[2])
+        u0 = [bank(s, "u0_%d" % s, [P, n])[:] for s, n in enumerate((HALF, HALF))]
         multiply(0, range(PASSES), u0)
-        make_h(0, u0, bias0[:, :1])
-        last_gate = spread_gate(3, bank(0, "spread3", [P, T])[:])
-
-        sums_in(3, 0, (0, 1, 2, 3))
-        add_own(0, 0, T)
-        u1 = [bank(2, "u1", [P, T])[:]]
-        rounded = [sb("w1_bf1_%d" % g, [P, P * PACK], BF16)[:] for g in range(PASSES)]
-        round_pass(on_vector, w1_raw[1, 0], rounded[0])
-        quantise_w1(1, 0, rounded[0])
+        h0 = sb("h0", [P, T + SPARE], F32)
+        nc.gpsimd.memset(h0[:, T:], 0.0)
+        make_h(0, u0, h0, bias0[:, :1])
+        u1 = [bank(3, "u1", [P, T])[:]]
+        quantise_w1(1, 0, interleave(on_vector, fresh("w1_bf1_0", P * PACK, BF16), w1_raw[1, 0]))
         multiply(1, (0,), u1)
-        round_pass(on_vector, w1_raw[1, 1], rounded[1])
-        picked = [pick(0, 0, d, fresh("picked0_%d" % d, T)) for d in (3, 2)]
-        gather_add(0, 0, 0, over("w1_raw1_1", "terms0_0", [P, T], F32)[:])
-        quantise_w1(1, P, rounded[1])
-        multiply(1, (1,), u1)
-        make_h(1, u1)
-        gather_add(0, 0, 1, fresh("terms0_1", T))
-        weigh_add(0, 0, 3, picked[0])
-        later = under("bias0", "later_bf", [P, 4 * K], BF16)
-        rounded = [round_tile(t, later[:, (t - 2) * K : (t - 1) * K]) for t in (2, 3)]
-        weigh_add(0, 0, 2, picked[1])
 
-        sums_in(5, 1, (0, 1, 2, 3))
-        add_own(1, 0, T)
-        gather_add(1, 0, 0, fresh("terms1_0", T))
-        quantise_w1(2, 0, rounded[0])
-        u2 = [bank(6, "u2", [P, T])[:]]
+        sums_in(4, 0, (0, 1, 2, 3))
+        add_own(0, 0, T)
+        p03 = pick(0, 0, 3, T)
+        p02 = [pick(0, 0, 2, HALF)]
+        gather_add(0, 0, 0, HALF)
+        rounded = interleave(on_vector, over("bias0", "w1_bf1_1", [P, P * PACK], BF16)[:], w1_raw[1, 1])
+        terms = gather(0, 0, 1, HALF)
+        quantise_w1(1, P, rounded)
+        add(0, 0, terms)
+        multiply(1, (1,), u1)
+        w1_bf2 = under("w1_raw1_1", "w1_bf2", [P, K], BF16)[:]
+        for g in range(PASSES):
+            interleave(on_scalar, w1_bf2[:, g * K // 2 : (g + 1) * K // 2], w1_raw[2, g])
+        make_h(1, u1, under("w1_raw2_1", "h1", [P, T], F32))
+        terms = over("w1_raw1_1", "terms0", [P, 2 * T], F32)
+        weigh_add(0, 0, 3, p03, terms[:, :T])
+        for d in range(2):
+            gather_add(0, HALF, d, HALF, terms[:, T + d * HALF : T + (d + 1) * HALF])
+        quantise_w1(2, 0, w1_bf2)
+        u2 = [bank(0, "u2", [P, T])[:]]
         multiply(2, range(PASSES), u2)
-        quantise_w1(3, 0, rounded[1])
-        u3 = [bank(7, "u3", [P, T])[:]]
+        weigh_add(0, 0, 2, p02[0], inside("w1_raw2_1", "weighed0_2", [P, HALF], F32)[:])
+        p02.append(pick(0, HALF, 2, HALF, over("w1_raw2_1", "picked0_2b", [P, HALF], F32)[:]))
+
+        sums_in(5, 1, (0, 1))
+        gather_add(1, 0, 0, HALF)
+        add_own(1, 0, HALF)
+        w1_bf3 = under("w1_sc1", "w1_bf3", [P, K], BF16)[:]
+        for g in range(PASSES):
+            interleave(on_scalar, w1_bf3[:, g * K // 2 : (g + 1) * K // 2], w1_raw[3, g])
+        make_h(2, u2, under("w1_raw3_1", "h2", [P, T], F32))
+        weigh_add(0, HALF, 2, p02[1])
+        gather_add(1, 0, 1, HALF)
+        quantise_w1(3, 0, w1_bf3)
+        u3 = [bank(1, "u3", [P, T])[:]]
         multiply(3, range(PASSES), u3)
-        zT[0] = under("w1_raw3_0", "zT0", [P, 2, 2, 2 * P], BF16)
-        zT[1] = over("w1_raw3_0", "zT1", [P, 2, 2, 2 * P], BF16)
+        gather_add(1, 0, 2, HALF, inside("w1_raw3_1", "terms1_2", [P, HALF], F32)[:])
+        p13 = pick(1, 0, 3, HALF, over("w1_raw3_1", "picked1_3", [P, HALF], F32)[:])
+        p23 = pick(2, 0, 3, HALF)
+        zT[0] = under("w1_bf3", "zT0", [P, 2, 2, 2 * P], BF16)
+        zT[1] = over("w1_bf3", "zT1", [P, 2, 2, 2 * P], BF16)
         round_z(0, 0, 2)
         round_z(0, 2, 2)
-        w2_bf = later[:, 2 * K :].rearrange("p (t m j) -> p t m j", t=TILES, j=PACK)
-        round_w2(w2_bf, 0)
-        make_h(2, u2)
-        terms = over("w1_raw3_1", "terms1", [P, 3, T], F32)
-        gather_add(1, 0, 1, terms[:, 0, :])
-        picks = over("w2_raw0", "picks", [P, 2 * T], F32)
-        picked = [pick(1, 0, 3, picks[:, :T])]
-        make_h(3, u3)
-        gather_add(1, 0, 2, terms[:, 1, :])
+        make_h(3, u3, sb("h3", [P, T], F32))
 
-        sums_in(1, 2, (0, 1))
-        picked.append(pick(2, 0, 3, picks[:, T : T + HALF]))
+        sums_in(2, 2, (0, 1))
+        gather_add(2, 0, 0, HALF)
         add_own(2, 0, HALF)
-        for d in range(2):
-            gather_add(2, 0, d, terms[:, 2, d * HALF : (d + 1) * HALF])
-        weigh_add(1, 0, 3, picked[0])
-        terms = over("h1", "terms3a", [P, 4, HALF], F32)
-        gather_add(2, 0, 2, terms[:, 2, :])
-        weigh_add(2, 0, 3, picked[1])
-        picked = pick(LAST, 0, 3, picks[:, T + HALF :])
+        weigh_add(1, 0, 3, p13)
+        gather_add(2, 0, 1, HALF)
+        gather_add(2, 0, 2, HALF)
+        weigh_add(2, 0, 3, p23)
+        w2_bf = over("w1_codes3", "w2_bf", [P, TILES, P, PACK], BF16)
+        round_w2(on_scalar, w2_bf, 0, 4)
+        p33 = pick(3, 0, 3, HALF, host("picked3_3", [P, HALF], F32, above=2048)[:])
+        round_w2(on_scalar, w2_bf, 1, 4)
         round_z(1, 0, 2)
-        round_z(1, 2, 2)
-        round_w2(w2_bf, 1)
         round_z(2, 0, 2)
-        sums_in(2, LAST, (0,))
-        sums_in(4, LAST, (1,))
-        add_own(LAST, 0, HALF)
-        gather_add(LAST, 0, 0, terms[:, 0, :])
-        weigh_add(LAST, 0, 3, picked)
-        gather_add(LAST, 0, 2, terms[:, 3, :])
+        round_w2(on_scalar, w2_bf, 1, 2)
+        sums_in(3, 3, (0, 1))
+        gather_add(3, 0, 0, HALF)
+        add_own(3, 0, HALF)
+        gather_add(3, 0, 2, HALF)
+        weigh_add(3, 0, 3, p33)
+        gather_add(3, 0, 1, HALF, host("terms3_1", [P, HALF], F32, above=1024)[:])
+        round_z(3, 0, 2)
+
+        sums_across(6, 2, (1, 2, 3))
+        sums_across(7, 3, (1, 2))
+        sums_across(0, 3, (3,))
+
+        def add_both(t, terms, blocks=(2, 3)):
+            for block in blocks:
+                add_across(t, block, terms[:, (block - 2) * P : (block - 1) * P])
+
+        late = {(1, 3): pick(1, HALF, 3, HALF, over("terms3_1", "picked1_3b", [P, HALF], F32)[:])}
+        terms = over("picked3_3", "terms1b", [P, 2, HALF], F32)
+        add_both(1, gather(1, HALF, 0, HALF, terms[:, 0, :]))
+        for t in (1, 2):
+            add_both(t, h[t][:, HALF:T])
+        backs = [turn_back(block, 4 + block) for block in range(2)]
+        z_bf = host("z_bf0", [P, HALF * PACK], BF16, above=1024)[:]
         for block in range(2):
-            gather_add(LAST, block * P, 1, terms[:, 1, block * P : (block + 1) * P])
-            round_z(LAST, block, 1)
-        picked = pick(2, HALF, 3, fresh("picked2b_3", HALF))
-        z_first = turn_back(0, (3, 5), host("z_bf0", [P, HALF * PACK], BF16, above=3072))
+            fetch_z(backs[block], z_bf[:, block * P * PACK : (block + 1) * P * PACK])
+        add_both(1, gather(1, HALF, 1, HALF, terms[:, 1, :]))
+        add_both(3, h[3][:, HALF:T], (2,))
+        nc.vector.quantize_mx(out=w2_codes[:].bitcast(FP8X4), scales=w2_sc[:], in_=w2_bf[:].rearrange("p t m j -> p (t m j)"))
+        terms = over("w2_raw1", "terms1c", [P, HALF + P], F32)
+        add_both(1, gather(1, HALF, 2, HALF, terms[:, :HALF]))
+        add_both(1, weigh(1, HALF, 3, late[1, 3]))
+        add_across(2, 2, gather(2, 2 * P, 0, P, terms[:, HALF:]))
+        z = quantise_z(0, z_bf)
+        accs = second_layer(0, z, (1, 2))
+        picks = under("zT0", "picked2b", [P, 2, HALF], F32)
+        for d in (3, 2):
+            late[2, d] = pick(2, HALF, d, HALF, picks[:, 3 - d, :])
+        late[3, 3] = pick(3, HALF, 3, HALF, inside("zT0", "picked3_3b", [P, HALF], F32)[:])
+        late[3, 2] = pick(3, HALF, 2, HALF, over("zT0", "picked3_2b", [P, HALF], F32)[:])
+        add_across(2, 2, gather(2, 2 * P, 1, P, inside("zT0", "terms2_1", [P, P], F32, 4 * HALF)[:]))
+        terms = over("z_bf0", "terms3b", [P, 2, P], F32)
+        for d in range(2):
+            add_across(3, 2, gather(3, 2 * P, d, P, terms[:, d, :]))
+        weighed = {key: weigh(key[0], HALF, key[1], late[key]) for key in ((2, 3), (2, 2), (3, 3))}
+        for block in (2, 3):
+            for t, d in weighed:
+                add_both(t, weighed[t, d], (block,))
+        add_both(3, h[3][:, HALF:T], (3,))
+        terms = gather(2, 3 * P, 0, P, under("picked2b", "terms2_0", [P, P], F32)[:])
+        add_both(3, weigh(3, HALF, 2, late[3, 2]))
+        add_across(2, 3, terms)
+        for s in range(2):
+            fetch_y(0, s, accs[s], on_scalar, slice(2 * s, 2 * s + 2))
+        round_across(1, 2)
+        terms = inside("zT0", "terms_last", [P, 3, P], F32)
+        for s, (t, d) in enumerate(((2, 1), (3, 0), (3, 1))):
+            add_across(t, 3, gather(t, 3 * P, d, P, terms[:, s, :]))
+        back = turn_back(2, 3)
+        z_bf = [fresh("z_bf1", P * PACK, BF16), fresh("z_bf2", P * PACK, BF16)]
+        round_across(1, 3)
+        round_across(3, 3)
+        fetch_z(back, z_bf[0])
+        back = turn_back(3, 4)
 
-        sums_in(4, 2, (2, 3))
-        add_own(2, HALF, HALF)
-        w2_codes = over("terms3a", "w2_codes", [P, H], U32)
-        nc.vector.quantize_mx(out=w2_codes[:].bitcast(FP8X4), scales=w2_sc[:], in_=later[:, 2 * K :])
-        terms = over("w2_raw1", "terms2b", [P, 2, HALF], F32)
-        for d in range(2):
-            gather_add(2, HALF, d, terms[:, d, :])
-        weigh_add(2, HALF, 3, picked)
-        late = place("picked_late", [P, 3, HALF], F32, span["zT0"][0] + LAP - 3072)
-        picked = [pick(2, HALF, 2, late[:, 0, :]), pick(LAST, HALF, 3, late[:, 1, :]), pick(LAST, HALF, 2, late[:, 2, :])]
-        acc_first = second_layer(0, w2_codes, z_first, (1, 2))
-        weigh_add(2, HALF, 2, picked[0])
-        round_z(2, 2, 2)
-        y_first = sb("y0", [P, TILES, HALF], F32)
-        on_scalar(out=y_first[:, :2, :], in_=acc_first[0])
-        nc.sync.dma_start(out=out_rows[:, :2, :HALF], in_=y_first[:, :2, :])
-        sums_in(6, LAST, (2,))
-        sums_in(7, LAST, (3,))
-        add_own(LAST, HALF, HALF)
-        terms = over("z_bf0", "terms3b", [P, 2, HALF], F32)
-        for d in range(2):
-            gather_add(LAST, 2 * P, d, terms[:, d, :P])
-        weigh_add(LAST, HALF, 3, picked[1])
-        weigh_add(LAST, HALF, 2, picked[2])
-        round_z(LAST, 2, 1)
-        on_scalar(out=y_first[:, 2:, :], in_=acc_first[1])
-        nc.sync.dma_start(out=out_rows[:, 2:, :HALF], in_=y_first[:, 2:, :])
-        z_second = turn_back(1, (3,), sb("z_bf1", [P, P * PACK], BF16))
-        for d in range(2):
-            gather_add(LAST, 3 * P, d, terms[:, d, P:])
-        round_z(LAST, 3, 1)
-        z_third = turn_back(2, (5,), sb("z_bf2", [P, P * PACK], BF16))
-
-        hand_on(0, y_first)
+        quantise_y(0, round_y(0))
         store_codes(0)
-        hand_on(1, store_y(1, second_layer(1, w2_codes, z_second, (7, 6)), (on_scalar, on_scalar), 2))
-        hand_on(2, store_y(2, second_layer(2, w2_codes, z_third, (1, 4)), (on_scalar, on_vector), 1))
+        accs = [second_layer(1, quantise_z(1, z_bf[0]), (5, 6))]
+        fetch_z(back, z_bf[1])
+        for s in range(2):
+            fetch_y(1, s, accs[0][s], on_scalar, slice(2 * s, 2 * s + 2))
+        accs.append(second_layer(2, quantise_z(2, z_bf[1]), (7, 0)))
+        fetch_y(2, 0, accs[1][0], on_scalar, None)
+        y_bf = round_y(1)
+        fetch_y(2, 1, accs[1][1], on_vector, slice(0, 4))
+        quantise_y(1, y_bf)
+        quantise_y(2, round_y(2))
         store_codes(HALF)
-
         for q in range(4):
             queue = nc.scalar if q % 2 else nc.sync
             queue.dma_start(

@@ -112,8 +112,8 @@ def tile_picked_wlapl_gelu_lo_kernel(tc, x_words, x_scales, w1, w2, gate, pos1, 
         load_w1(2, 0)
         load_w1(2, 1, 2048, 4096)
         load_w1(3, 0)
-        load_w1(3, 1, 2048, 4096)
-        w2_raw = [host("w2_raw%d" % s, [P, PACK, H // 2], F32, above=2048) for s in range(2)]
+        load_w1(3, 1, 2048, 5120)
+        w2_raw = [host("w2_raw%d" % s, [P, PACK, H // 2], F32, above=3072) for s in range(2)]
         for s in range(2):
             nc.sync.dma_start(out=w2_raw[s][:], in_=w2[:, s * H // 2 : (s + 1) * H // 2].rearrange("(p j) m -> p j m", j=PACK))
 
@@ -122,7 +122,7 @@ def tile_picked_wlapl_gelu_lo_kernel(tc, x_words, x_scales, w1, w2, gate, pos1, 
 
         w1_codes = [sb("w1_codes0", [P, PASSES * P], U32)]
         for t in (1, 2):
-            w1_codes.append(place("w1_codes%d" % t, [P, PASSES * P], U32, span["w1_raw%d_1" % (t + 1)][1] + 4 * HALF - 2 * LAP))
+            w1_codes.append(place("w1_codes%d" % t, [P, PASSES * P], U32, span["w1_raw%d_1" % (t + 1)][1] + 4 * HALF * (2 * t - 1) - 2 * LAP))
         w1_codes.append(host("w1_codes3", [P, PASSES * P], U32, above=4096))
         w1_sc = [host("w1_sc%d" % t, [P, PASSES * P], U8, 8192 if t == 1 else 0, 2048 if t == 1 else 0) for t in range(TILES)]
         h = {}
@@ -263,11 +263,10 @@ def tile_picked_wlapl_gelu_lo_kernel(tc, x_words, x_scales, w1, w2, gate, pos1, 
         out_rows = out_0.rearrange("(p t) v -> p t v", t=TILES)
         out_words = out_1[0].rearrange("p v r -> p (v r)").bitcast(I32)
 
-        def round_w2(copy, w2_bf, s, count):
-            m = P // count
-            raw = w2_raw[s * 2 // count][:, :, (s * H // count) % HALF : (s * H // count) % HALF + H // count]
+        def round_w2(copy, w2_bf, first, end):
+            raw = w2_raw[first // (P // 2)][:, :, TILES * first % HALF : TILES * first % HALF + TILES * (end - first)]
             copy(
-                out=w2_bf[:, :, s * m : (s + 1) * m, :].rearrange("p t m j -> p m j t"),
+                out=w2_bf[:, :, first:end, :].rearrange("p t m j -> p m j t"),
                 in_=raw.rearrange("p j (m t) -> p m j t", t=TILES),
             )
 
@@ -359,7 +358,6 @@ def tile_picked_wlapl_gelu_lo_kernel(tc, x_words, x_scales, w1, w2, gate, pos1, 
         u2 = [bank(0, "u2", [P, T])[:]]
         multiply(2, range(PASSES), u2)
         weigh_add(0, 0, 2, p02[0], inside("w1_raw2_1", "weighed0_2", [P, HALF], F32)[:])
-        p02.append(pick(0, HALF, 2, HALF, over("w1_raw2_1", "picked0_2b", [P, HALF], F32)[:]))
 
         sums_in(5, 1, (0, 1))
         gather_add(1, 0, 0, HALF)
@@ -367,93 +365,104 @@ def tile_picked_wlapl_gelu_lo_kernel(tc, x_words, x_scales, w1, w2, gate, pos1, 
         w1_bf3 = under("w1_sc1", "w1_bf3", [P, K], BF16)[:]
         for g in range(PASSES):
             interleave(on_scalar, w1_bf3[:, g * K // 2 : (g + 1) * K // 2], w1_raw[3, g])
+        p02.append(pick(0, HALF, 2, HALF, inside("w1_raw3_1", "picked0_2b", [P, HALF], F32)[:]))
         make_h(2, u2, under("w1_raw3_1", "h2", [P, T], F32))
-        weigh_add(0, HALF, 2, p02[1])
         gather_add(1, 0, 1, HALF)
         quantise_w1(3, 0, w1_bf3)
         u3 = [bank(1, "u3", [P, T])[:]]
         multiply(3, range(PASSES), u3)
-        gather_add(1, 0, 2, HALF, inside("w1_raw3_1", "terms1_2", [P, HALF], F32)[:])
-        p13 = pick(1, 0, 3, HALF, over("w1_raw3_1", "picked1_3", [P, HALF], F32)[:])
+        p13 = over("w1_raw3_1", "picked1_3", [P, T + HALF], F32)
+        gather_add(1, 0, 2, HALF, p13[:, T:])
+        weigh_add(0, HALF, 2, p02[1])
+        pick(1, 0, 3, HALF, p13[:, :HALF])
         p23 = pick(2, 0, 3, HALF)
-        zT[0] = under("w1_bf3", "zT0", [P, 2, 2, 2 * P], BF16)
-        zT[1] = over("w1_bf3", "zT1", [P, 2, 2, 2 * P], BF16)
-        round_z(0, 0, 2)
-        round_z(0, 2, 2)
+        pick(1, HALF, 3, HALF, p13[:, HALF:T])
         make_h(3, u3, sb("h3", [P, T], F32))
 
         sums_in(2, 2, (0, 1))
         gather_add(2, 0, 0, HALF)
         add_own(2, 0, HALF)
-        weigh_add(1, 0, 3, p13)
+        weigh_add(1, 0, 3, p13[:, :HALF])
         gather_add(2, 0, 1, HALF)
         gather_add(2, 0, 2, HALF)
         weigh_add(2, 0, 3, p23)
         w2_bf = over("w1_codes3", "w2_bf", [P, TILES, P, PACK], BF16)
-        round_w2(on_scalar, w2_bf, 0, 4)
-        p33 = pick(3, 0, 3, HALF, host("picked3_3", [P, HALF], F32, above=2048)[:])
-        round_w2(on_scalar, w2_bf, 1, 4)
+        round_w2(on_scalar, w2_bf, 0, 32)
+        p33 = pick(3, 0, 3, HALF, host("picked3_3", [P, HALF], F32, above=3072)[:])
+        zT[0] = under("w1_bf3", "zT0", [P, 2, 2, 2 * P], BF16)
+        round_z(0, 0, 2)
+        round_w2(on_scalar, w2_bf, 32, 64)
         round_z(1, 0, 2)
         round_z(2, 0, 2)
-        round_w2(on_scalar, w2_bf, 1, 2)
+        round_w2(on_scalar, w2_bf, 64, 96)
+        round_w2(on_vector, w2_bf, 96, 128)
         sums_in(3, 3, (0, 1))
         gather_add(3, 0, 0, HALF)
         add_own(3, 0, HALF)
         gather_add(3, 0, 2, HALF)
         weigh_add(3, 0, 3, p33)
-        gather_add(3, 0, 1, HALF, host("terms3_1", [P, HALF], F32, above=1024)[:])
+        sums_across(1, 3, (3,))
+        add_across(3, 3, h[3][:, 3 * P : T])
+        gather_add(3, 0, 1, HALF, host("terms3_1", [P, HALF], F32, 2048, 1024)[:])
+        zT[1] = under("terms3_1", "zT1", [P, 2, 2, 2 * P], BF16)
         round_z(3, 0, 2)
 
-        sums_across(6, 2, (1, 2, 3))
-        sums_across(7, 3, (1, 2))
-        sums_across(0, 3, (3,))
+        sums_across(5, 2, (1, 2))
+        sums_across(3, 2, (3,))
+        sums_across(2, 3, (1, 2))
 
         def add_both(t, terms, blocks=(2, 3)):
             for block in blocks:
                 add_across(t, block, terms[:, (block - 2) * P : (block - 1) * P])
 
-        late = {(1, 3): pick(1, HALF, 3, HALF, over("terms3_1", "picked1_3b", [P, HALF], F32)[:])}
+        late = {(2, 3): pick(2, HALF, 3, HALF, over("terms3_1", "picked2_3b", [P, HALF], F32)[:])}
         terms = over("picked3_3", "terms1b", [P, 2, HALF], F32)
-        add_both(1, gather(1, HALF, 0, HALF, terms[:, 0, :]))
         for t in (1, 2):
             add_both(t, h[t][:, HALF:T])
-        backs = [turn_back(block, 4 + block) for block in range(2)]
-        z_bf = host("z_bf0", [P, HALF * PACK], BF16, above=1024)[:]
+        first = gather(1, HALF, 0, HALF, terms[:, 0, :])
+        backs = [turn_back(0, 6), turn_back(1, 7)]
+        add_both(1, first)
+        z_bf = host("z_bf0", [P, HALF * PACK], BF16, above=3072)[:]
         for block in range(2):
             fetch_z(backs[block], z_bf[:, block * P * PACK : (block + 1) * P * PACK])
         add_both(1, gather(1, HALF, 1, HALF, terms[:, 1, :]))
         add_both(3, h[3][:, HALF:T], (2,))
         nc.vector.quantize_mx(out=w2_codes[:].bitcast(FP8X4), scales=w2_sc[:], in_=w2_bf[:].rearrange("p t m j -> p (t m j)"))
-        terms = over("w2_raw1", "terms1c", [P, HALF + P], F32)
+        terms = over("w2_raw1", "terms1c", [P, 5 * P], F32)
         add_both(1, gather(1, HALF, 2, HALF, terms[:, :HALF]))
-        add_both(1, weigh(1, HALF, 3, late[1, 3]))
-        add_across(2, 2, gather(2, 2 * P, 0, P, terms[:, HALF:]))
+        add_both(1, weigh(1, HALF, 3, p13[:, HALF:T], terms[:, HALF:T]))
+        add_across(2, 2, gather(2, 2 * P, 0, P, terms[:, T:]))
         z = quantise_z(0, z_bf)
-        accs = second_layer(0, z, (1, 2))
-        picks = under("zT0", "picked2b", [P, 2, HALF], F32)
+        accs = second_layer(0, z, (0, 6))
+        picks = under("zT0", "picked_late", [P, 2, HALF], F32)
+        late[2, 2] = pick(2, HALF, 2, HALF, picks[:, 0, :])
+        late[3, 3] = pick(3, HALF, 3, HALF, picks[:, 1, :])
+        late[3, 2] = pick(3, HALF, 2, HALF, inside("zT0", "picked3_2b", [P, HALF], F32)[:])
+        late[2, 1] = pick(2, HALF, 1, HALF, over("zT0", "picked2_1b", [P, HALF], F32)[:])
+        add_across(3, 2, gather(3, 2 * P, 0, P, inside("zT0", "terms3_0", [P, P], F32, 4 * HALF)[:]))
+        terms = over("z_bf0", "terms3b", [P, 3 * P], F32)
+        weighed = {(2, 3): weigh(2, HALF, 3, late[2, 3], terms[:, :HALF])}
+        add_both(2, weighed[2, 3], (2,))
+        add_across(3, 2, gather(3, 2 * P, 1, P, terms[:, HALF:]))
+        for t, d in ((2, 2), (3, 3), (3, 2)):
+            weighed[t, d] = weigh(t, HALF, d, late[t, d])
+            add_both(t, weighed[t, d], (2,))
+        terms = gather(2, 3 * P, 0, P, under("picked_late", "terms2_0b", [P, P], F32)[:])
         for d in (3, 2):
-            late[2, d] = pick(2, HALF, d, HALF, picks[:, 3 - d, :])
-        late[3, 3] = pick(3, HALF, 3, HALF, inside("zT0", "picked3_3b", [P, HALF], F32)[:])
-        late[3, 2] = pick(3, HALF, 2, HALF, over("zT0", "picked3_2b", [P, HALF], F32)[:])
-        add_across(2, 2, gather(2, 2 * P, 1, P, inside("zT0", "terms2_1", [P, P], F32, 4 * HALF)[:]))
-        terms = over("z_bf0", "terms3b", [P, 2, P], F32)
-        for d in range(2):
-            add_across(3, 2, gather(3, 2 * P, d, P, terms[:, d, :]))
-        weighed = {key: weigh(key[0], HALF, key[1], late[key]) for key in ((2, 3), (2, 2), (3, 3))}
-        for block in (2, 3):
-            for t, d in weighed:
-                add_both(t, weighed[t, d], (block,))
-        add_both(3, h[3][:, HALF:T], (3,))
-        terms = gather(2, 3 * P, 0, P, under("picked2b", "terms2_0", [P, P], F32)[:])
-        add_both(3, weigh(3, HALF, 2, late[3, 2]))
+            add_both(2, weighed[2, d], (3,))
+        add_both(2, weigh(2, HALF, 1, late[2, 1]))
         add_across(2, 3, terms)
+        for d in (3, 2):
+            add_both(3, weighed[3, d], (3,))
+        round_z(0, 2, 2)
         for s in range(2):
             fetch_y(0, s, accs[s], on_scalar, slice(2 * s, 2 * s + 2))
+        round_across(3, 2)
         round_across(1, 2)
-        terms = inside("zT0", "terms_last", [P, 3, P], F32)
-        for s, (t, d) in enumerate(((2, 1), (3, 0), (3, 1))):
-            add_across(t, 3, gather(t, 3 * P, d, P, terms[:, s, :]))
-        back = turn_back(2, 3)
+        terms = inside("zT0", "terms_last", [P, 2, P], F32)
+        for d in range(2):
+            add_across(3, 3, gather(3, 3 * P, d, P, terms[:, d, :]))
+        back = turn_back(2, 7)
         z_bf = [fresh("z_bf1", P * PACK, BF16), fresh("z_bf2", P * PACK, BF16)]
         round_across(1, 3)
         round_across(3, 3)
@@ -462,16 +471,16 @@ def tile_picked_wlapl_gelu_lo_kernel(tc, x_words, x_scales, w1, w2, gate, pos1, 
 
         quantise_y(0, round_y(0))
         store_codes(0)
-        accs = [second_layer(1, quantise_z(1, z_bf[0]), (5, 6))]
+        accs = [second_layer(1, quantise_z(1, z_bf[0]), (3, 5))]
         fetch_z(back, z_bf[1])
         for s in range(2):
             fetch_y(1, s, accs[0][s], on_scalar, slice(2 * s, 2 * s + 2))
-        accs.append(second_layer(2, quantise_z(2, z_bf[1]), (7, 0)))
+        accs.append(second_layer(2, quantise_z(2, z_bf[1]), (2, 1)))
         fetch_y(2, 0, accs[1][0], on_scalar, None)
-        y_bf = round_y(1)
         fetch_y(2, 1, accs[1][1], on_vector, slice(0, 4))
-        quantise_y(1, y_bf)
-        quantise_y(2, round_y(2))
+        y_bf = [round_y(1), round_y(2)]
+        quantise_y(1, y_bf[0])
+        quantise_y(2, y_bf[1])
         store_codes(HALF)
         for q in range(4):
             queue = nc.scalar if q % 2 else nc.sync

@@ -163,6 +163,7 @@ def tile_picked_wlapl_gelu_lo_kernel(tc, x_words, x_scales, w1, w2, gate, pos1, 
         zT = {}
         home = {}
         across = {}
+        total = {}
         added = {}
 
         def add(t, v0, summand):
@@ -172,18 +173,20 @@ def tile_picked_wlapl_gelu_lo_kernel(tc, x_words, x_scales, w1, w2, gate, pos1, 
                 mine = columns[:, (block - blocks[0]) * P : (block - blocks[0] + 1) * P]
                 count = added[t, blocks]
                 added[t, blocks] = count + 1
-                last = count + 1 == (D + 1) * len(blocks)
+                last = count + 1 == total[t, blocks]
                 nc.tensor.matmul(mine, lhsT=summand[:, at : at + P], rhs=ident[:], start=count == 0, stop=last, is_transpose=True)
 
-        def sums_in(number, t, blocks):
+        def sums_in(number, t, blocks, summands=D + 1):
             columns = bank(number, "sums%d_%d" % (t, blocks[0]), [P, len(blocks) * P])[:]
             added[t, blocks] = 0
+            total[t, blocks] = summands * len(blocks)
             for block in blocks:
                 home[t, block] = (columns, blocks)
 
-        def sums_across(number, block, tiles):
+        def sums_across(number, block, tiles, folded=0):
             columns = bank(number, "sums_of_block%d_%d" % (block, tiles[0]), [P, len(tiles) * P])[:]
             added[block, tiles, "across"] = 0
+            total[block, tiles, "across"] = (D + 1) * len(tiles) - folded
             for t in tiles:
                 across[t, block] = (columns, tiles)
 
@@ -192,7 +195,7 @@ def tile_picked_wlapl_gelu_lo_kernel(tc, x_words, x_scales, w1, w2, gate, pos1, 
             mine = columns[:, (t - tiles[0]) * P : (t - tiles[0] + 1) * P]
             count = added[block, tiles, "across"]
             added[block, tiles, "across"] = count + 1
-            last = count + 1 == (D + 1) * len(tiles)
+            last = count + 1 == total[block, tiles, "across"]
             nc.tensor.matmul(mine, lhsT=summand, rhs=ident[:], start=count == 0, stop=last, is_transpose=True)
 
         def round_across(t, block):
@@ -239,6 +242,14 @@ def tile_picked_wlapl_gelu_lo_kernel(tc, x_words, x_scales, w1, w2, gate, pos1, 
                 terms = fresh("weighed%d_%d_%d" % (t, d, v0), n)
             nc.vector.tensor_tensor(out=terms, in0=picked, in1=neg_gate[:, d, v0 : v0 + n], op=ALU.mult)
             return terms
+
+        def joined(name, first, second):
+            both = fresh(name, first.shape[1])
+            nc.vector.tensor_tensor(out=both, in0=first, in1=second, op=ALU.add)
+            return both
+
+        def with_own(t, v0, terms):
+            return joined("with_own%d_%d" % (t, v0), terms, h[t][:, v0 : v0 + terms.shape[1]])
 
         def gather_add(t, v0, d, n, terms=None):
             add(t, v0, gather(t, v0, d, n, terms))
@@ -339,7 +350,7 @@ def tile_picked_wlapl_gelu_lo_kernel(tc, x_words, x_scales, w1, w2, gate, pos1, 
         sums_in(4, 0, (0, 1, 2, 3))
         add_own(0, 0, T)
         p03 = pick(0, 0, 3, T)
-        p02 = [pick(0, 0, 2, HALF)]
+        p02 = []
         gather_add(0, 0, 0, HALF)
         rounded = interleave(on_vector, over("bias0", "w1_bf1_1", [P, P * PACK], BF16)[:], w1_raw[1, 1])
         terms = gather(0, 0, 1, HALF)
@@ -357,7 +368,7 @@ def tile_picked_wlapl_gelu_lo_kernel(tc, x_words, x_scales, w1, w2, gate, pos1, 
         quantise_w1(2, 0, w1_bf2)
         u2 = [bank(0, "u2", [P, T])[:]]
         multiply(2, range(PASSES), u2)
-        weigh_add(0, 0, 2, p02[0], inside("w1_raw2_1", "weighed0_2", [P, HALF], F32)[:])
+        gather_add(0, 0, 2, HALF, inside("w1_raw2_1", "weighed0_2", [P, HALF], F32)[:])
 
         sums_in(5, 1, (0, 1))
         gather_add(1, 0, 0, HALF)
@@ -373,7 +384,7 @@ def tile_picked_wlapl_gelu_lo_kernel(tc, x_words, x_scales, w1, w2, gate, pos1, 
         multiply(3, range(PASSES), u3)
         p13 = over("w1_raw3_1", "picked1_3", [P, T + HALF], F32)
         gather_add(1, 0, 2, HALF, p13[:, T:])
-        weigh_add(0, HALF, 2, p02[1])
+        weigh_add(0, HALF, 2, p02[0])
         pick(1, 0, 3, HALF, p13[:, :HALF])
         p23 = pick(2, 0, 3, HALF)
         pick(1, HALF, 3, HALF, p13[:, HALF:T])
@@ -438,30 +449,30 @@ def tile_picked_wlapl_gelu_lo_kernel(tc, x_words, x_scales, w1, w2, gate, pos1, 
         late[2, 2] = pick(2, HALF, 2, HALF, picks[:, 0, :])
         late[3, 3] = pick(3, HALF, 3, HALF, picks[:, 1, :])
         late[3, 2] = pick(3, HALF, 2, HALF, inside("zT0", "picked3_2b", [P, HALF], F32)[:])
-        late[2, 1] = pick(2, HALF, 1, HALF, over("zT0", "picked2_1b", [P, HALF], F32)[:])
         add_across(3, 2, gather(3, 2 * P, 0, P, inside("zT0", "terms3_0", [P, P], F32, 4 * HALF)[:]))
-        terms = over("z_bf0", "terms3b", [P, 3 * P], F32)
+        terms = over("z_bf0", "terms3b", [P, 4 * P], F32)
         weighed = {(2, 3): weigh(2, HALF, 3, late[2, 3], terms[:, :HALF])}
         add_both(2, weighed[2, 3], (2,))
-        add_across(3, 2, gather(3, 2 * P, 1, P, terms[:, HALF:]))
+        add_across(3, 2, gather(3, 2 * P, 1, P, terms[:, HALF : 3 * P]))
+        add_across(2, 2, gather(2, 2 * P, 1, P, terms[:, 3 * P :]))
         for t, d in ((2, 2), (3, 3), (3, 2)):
             weighed[t, d] = weigh(t, HALF, d, late[t, d])
             add_both(t, weighed[t, d], (2,))
         terms = gather(2, 3 * P, 0, P, under("picked_late", "terms2_0b", [P, P], F32)[:])
         for d in (3, 2):
             add_both(2, weighed[2, d], (3,))
-        add_both(2, weigh(2, HALF, 1, late[2, 1]))
+        last = inside("zT0", "terms_last", [P, 3, P], F32)
+        add_across(2, 3, gather(2, 3 * P, 1, P, last[:, 2, :]))
         add_across(2, 3, terms)
         for d in (3, 2):
             add_both(3, weighed[3, d], (3,))
         round_z(0, 2, 2)
         for s in range(2):
             fetch_y(0, s, accs[s], on_scalar, slice(2 * s, 2 * s + 2))
-        round_across(3, 2)
         round_across(1, 2)
-        terms = inside("zT0", "terms_last", [P, 2, P], F32)
+        round_across(3, 2)
         for d in range(2):
-            add_across(3, 3, gather(3, 3 * P, d, P, terms[:, d, :]))
+            add_across(3, 3, gather(3, 3 * P, d, P, last[:, d, :]))
         back = turn_back(2, 7)
         z_bf = [fresh("z_bf1", P * PACK, BF16), fresh("z_bf2", P * PACK, BF16)]
         round_across(1, 3)
@@ -476,8 +487,8 @@ def tile_picked_wlapl_gelu_lo_kernel(tc, x_words, x_scales, w1, w2, gate, pos1, 
         for s in range(2):
             fetch_y(1, s, accs[0][s], on_scalar, slice(2 * s, 2 * s + 2))
         accs.append(second_layer(2, quantise_z(2, z_bf[1]), (2, 1)))
-        fetch_y(2, 0, accs[1][0], on_scalar, None)
-        fetch_y(2, 1, accs[1][1], on_vector, slice(0, 4))
+        fetch_y(2, 0, accs[1][0], on_vector, None)
+        fetch_y(2, 1, accs[1][1], on_scalar, slice(0, 4))
         y_bf = [round_y(1), round_y(2)]
         quantise_y(1, y_bf[0])
         quantise_y(2, y_bf[1])

@@ -109,7 +109,7 @@ def tile_picked_wlapl_gelu_lo_kernel(tc, x_words, x_scales, w1, w2, gate, pos1, 
         load_w1(1, 1, 2048, 4096)
         load_list(1)
         load_list(2)
-        load_w1(2, 0)
+        load_w1(2, 0, 0, 1024)
         load_w1(2, 1, 2048, 4096)
         load_w1(3, 0)
         load_w1(3, 1, 2048, 5120)
@@ -360,6 +360,7 @@ def tile_picked_wlapl_gelu_lo_kernel(tc, x_words, x_scales, w1, w2, gate, pos1, 
         w1_bf2 = under("w1_raw1_1", "w1_bf2", [P, K], BF16)[:]
         for g in range(PASSES):
             interleave(on_scalar, w1_bf2[:, g * K // 2 : (g + 1) * K // 2], w1_raw[2, g])
+        quarter = pick(0, 0, 2, P, over("w1_raw2_0", "picked0_2a", [P, P], F32)[:])
         make_h(1, u1, under("w1_raw2_1", "h1", [P, T], F32))
         terms = over("w1_raw1_1", "terms0", [P, 2 * T], F32)
         weigh_add(0, 0, 3, p03, terms[:, :T])
@@ -368,7 +369,9 @@ def tile_picked_wlapl_gelu_lo_kernel(tc, x_words, x_scales, w1, w2, gate, pos1, 
         quantise_w1(2, 0, w1_bf2)
         u2 = [bank(0, "u2", [P, T])[:]]
         multiply(2, range(PASSES), u2)
-        gather_add(0, 0, 2, HALF, inside("w1_raw2_1", "weighed0_2", [P, HALF], F32)[:])
+        terms = inside("w1_raw2_1", "weighed0_2", [P, HALF], F32)
+        gather_add(0, P, 2, P, terms[:, P:])
+        weigh_add(0, 0, 2, quarter, terms[:, :P])
 
         sums_in(5, 1, (0, 1))
         gather_add(1, 0, 0, HALF)
@@ -449,6 +452,7 @@ def tile_picked_wlapl_gelu_lo_kernel(tc, x_words, x_scales, w1, w2, gate, pos1, 
         late[2, 2] = pick(2, HALF, 2, HALF, picks[:, 0, :])
         late[3, 3] = pick(3, HALF, 3, HALF, picks[:, 1, :])
         late[3, 2] = pick(3, HALF, 2, HALF, inside("zT0", "picked3_2b", [P, HALF], F32)[:])
+        late[2, 1] = pick(2, 3 * P, 1, P, over("zT0", "picked2_1b", [P, P], F32)[:])
         add_across(3, 2, gather(3, 2 * P, 0, P, inside("zT0", "terms3_0", [P, P], F32, 4 * HALF)[:]))
         terms = over("z_bf0", "terms3b", [P, 4 * P], F32)
         weighed = {(2, 3): weigh(2, HALF, 3, late[2, 3], terms[:, :HALF])}
@@ -462,7 +466,7 @@ def tile_picked_wlapl_gelu_lo_kernel(tc, x_words, x_scales, w1, w2, gate, pos1, 
         for d in (3, 2):
             add_both(2, weighed[2, d], (3,))
         last = inside("zT0", "terms_last", [P, 3, P], F32)
-        add_across(2, 3, gather(2, 3 * P, 1, P, last[:, 2, :]))
+        add_across(2, 3, weigh(2, 3 * P, 1, late[2, 1], last[:, 2, :]))
         add_across(2, 3, terms)
         for d in (3, 2):
             add_both(3, weighed[3, d], (3,))

@@ -106,25 +106,29 @@ def tile_picked_wlapl_gelu_lo_kernel(tc, x_words, x_scales, w1, w2, gate, pos1, 
         load_w1(1, 0)
         load_list(0)
         load_list(3)
-        load_w1(1, 1, 2048, 4096)
+        load_w1(1, 1, 10240, 4096)
         load_list(1)
         load_list(2)
         load_w1(2, 0, 0, 1024)
         load_w1(2, 1, 2048, 4096)
         load_w1(3, 0)
-        load_w1(3, 1, 2048, 5120)
-        w2_raw = [host("w2_raw%d" % s, [P, PACK, H // 2], F32, above=3072) for s in range(2)]
-        for s in range(2):
-            nc.sync.dma_start(out=w2_raw[s][:], in_=w2[:, s * H // 2 : (s + 1) * H // 2].rearrange("(p j) m -> p j m", j=PACK))
+        load_w1(3, 1, 0, 7168)
+        w2_raw = []
+
+        def load_w2(s, raw):
+            nc.sync.dma_start(out=raw[:], in_=w2[:, s * H // 2 : (s + 1) * H // 2].rearrange("(p j) m -> p j m", j=PACK))
+            w2_raw.append(raw)
+
+        load_w2(0, host("w2_raw0", [P, PACK, H // 2], F32, above=1024))
 
         ident = sb("ident", [P, P], F32)
         make_identity(nc, ident[:])
 
         w1_codes = [sb("w1_codes0", [P, PASSES * P], U32)]
         for t in (1, 2):
-            w1_codes.append(place("w1_codes%d" % t, [P, PASSES * P], U32, span["w1_raw%d_1" % (t + 1)][1] + 4 * HALF * (2 * t - 1) - 2 * LAP))
+            w1_codes.append(place("w1_codes%d" % t, [P, PASSES * P], U32, span["w1_raw%d_1" % (t + 1)][1] + 4 * HALF * (3 * t - 2) - 2 * LAP))
         w1_codes.append(host("w1_codes3", [P, PASSES * P], U32, above=4096))
-        w1_sc = [host("w1_sc%d" % t, [P, PASSES * P], U8, 8192 if t == 1 else 0, 2048 if t == 1 else 0) for t in range(TILES)]
+        w1_sc = [host("w1_sc%d" % t, [P, PASSES * P], U8, above=1024 if t == LAST else 0) for t in range(TILES)]
         h = {}
 
         def interleave(copy, rounded, rows):
@@ -350,7 +354,6 @@ def tile_picked_wlapl_gelu_lo_kernel(tc, x_words, x_scales, w1, w2, gate, pos1, 
         sums_in(4, 0, (0, 1, 2, 3))
         add_own(0, 0, T)
         p03 = pick(0, 0, 3, T)
-        p02 = []
         gather_add(0, 0, 0, HALF)
         rounded = interleave(on_vector, over("bias0", "w1_bf1_1", [P, P * PACK], BF16)[:], w1_raw[1, 1])
         terms = gather(0, 0, 1, HALF)
@@ -373,52 +376,53 @@ def tile_picked_wlapl_gelu_lo_kernel(tc, x_words, x_scales, w1, w2, gate, pos1, 
         gather_add(0, P, 2, P, terms[:, P:])
         weigh_add(0, 0, 2, quarter, terms[:, :P])
 
+        p02 = pick(0, HALF, 2, HALF, over("w1_raw2_1", "picked0_2b", [P, HALF], F32)[:])
+        early = {d: pick(1, 0, d, HALF) for d in (1, 2)}
+        make_h(2, u2, sb("h2", [P, T], F32))
         sums_in(5, 1, (0, 1))
         gather_add(1, 0, 0, HALF)
         add_own(1, 0, HALF)
-        w1_bf3 = under("w1_sc1", "w1_bf3", [P, K], BF16)[:]
+        w1_bf3 = under("w1_bf2", "w1_bf3", [P, K], BF16)[:]
         for g in range(PASSES):
-            interleave(on_scalar, w1_bf3[:, g * K // 2 : (g + 1) * K // 2], w1_raw[3, g])
-        p02.append(pick(0, HALF, 2, HALF, inside("w1_raw3_1", "picked0_2b", [P, HALF], F32)[:]))
-        make_h(2, u2, under("w1_raw3_1", "h2", [P, T], F32))
-        gather_add(1, 0, 1, HALF)
+            interleave(on_vector, w1_bf3[:, g * K // 2 : (g + 1) * K // 2], w1_raw[3, g])
+        weigh_add(1, 0, 1, early[1])
         quantise_w1(3, 0, w1_bf3)
         u3 = [bank(1, "u3", [P, T])[:]]
         multiply(3, range(PASSES), u3)
-        p13 = over("w1_raw3_1", "picked1_3", [P, T + HALF], F32)
-        gather_add(1, 0, 2, HALF, p13[:, T:])
-        weigh_add(0, HALF, 2, p02[0])
+        load_w2(1, over("w1_bf3", "w2_raw1", [P, PACK, H // 2], F32))
+        p13 = over("w1_raw3_1", "picked1_3", [P, 4 * HALF], F32)
+        weigh_add(0, HALF, 2, p02, p13[:, HALF:T])
+        weigh_add(1, 0, 2, early[2], p13[:, T : T + HALF])
         pick(1, 0, 3, HALF, p13[:, :HALF])
-        p23 = pick(2, 0, 3, HALF)
-        pick(1, HALF, 3, HALF, p13[:, HALF:T])
+        early = {(2, d): pick(2, 0, d, HALF) for d in (3, 2)}
         make_h(3, u3, sb("h3", [P, T], F32))
+        p13b = pick(1, HALF, 3, HALF, over("w1_sc3", "picked1_3b", [P, HALF], F32)[:])
+        early[3, 3] = pick(3, 0, 3, HALF, host("picked3_3", [P, HALF], F32, above=5120)[:])
+        early[3, 2] = pick(3, 0, 2, HALF)
 
         sums_in(2, 2, (0, 1))
-        gather_add(2, 0, 0, HALF)
+        gather_add(2, 0, 0, HALF, p13[:, 3 * HALF :])
         add_own(2, 0, HALF)
         weigh_add(1, 0, 3, p13[:, :HALF])
         gather_add(2, 0, 1, HALF)
-        gather_add(2, 0, 2, HALF)
-        weigh_add(2, 0, 3, p23)
+        weigh_add(2, 0, 3, early[2, 3])
         w2_bf = over("w1_codes3", "w2_bf", [P, TILES, P, PACK], BF16)
-        round_w2(on_scalar, w2_bf, 0, 32)
-        p33 = pick(3, 0, 3, HALF, host("picked3_3", [P, HALF], F32, above=3072)[:])
+        round_w2(on_vector, w2_bf, 0, 64)
+        weigh_add(2, 0, 2, early[2, 2])
         zT[0] = under("w1_bf3", "zT0", [P, 2, 2, 2 * P], BF16)
         round_z(0, 0, 2)
-        round_w2(on_scalar, w2_bf, 32, 64)
         round_z(1, 0, 2)
         round_z(2, 0, 2)
-        round_w2(on_scalar, w2_bf, 64, 96)
-        round_w2(on_vector, w2_bf, 96, 128)
         sums_in(3, 3, (0, 1))
         gather_add(3, 0, 0, HALF)
         add_own(3, 0, HALF)
-        gather_add(3, 0, 2, HALF)
-        weigh_add(3, 0, 3, p33)
+        gather_add(3, 0, 1, HALF)
+        weigh_add(3, 0, 3, early[3, 3])
         sums_across(1, 3, (3,))
         add_across(3, 3, h[3][:, 3 * P : T])
-        gather_add(3, 0, 1, HALF, host("terms3_1", [P, HALF], F32, 2048, 1024)[:])
+        weigh_add(3, 0, 2, early[3, 2], host("terms3_1", [P, HALF], F32, 2048, 1024)[:])
         zT[1] = under("terms3_1", "zT1", [P, 2, 2, 2 * P], BF16)
+        spare = pick(1, HALF, 2, HALF, over("w2_raw0", "picked1_2b", [P, HALF], F32)[:])
         round_z(3, 0, 2)
 
         sums_across(5, 2, (1, 2))
@@ -430,22 +434,22 @@ def tile_picked_wlapl_gelu_lo_kernel(tc, x_words, x_scales, w1, w2, gate, pos1, 
                 add_across(t, block, terms[:, (block - 2) * P : (block - 1) * P])
 
         late = {(2, 3): pick(2, HALF, 3, HALF, over("terms3_1", "picked2_3b", [P, HALF], F32)[:])}
-        terms = over("picked3_3", "terms1b", [P, 2, HALF], F32)
+        terms = over("picked3_3", "terms1b", [P, 9 * P], F32)
         for t in (1, 2):
             add_both(t, h[t][:, HALF:T])
-        first = gather(1, HALF, 0, HALF, terms[:, 0, :])
+        first = gather(1, HALF, 0, HALF, terms[:, 5 * P : 7 * P])
         backs = [turn_back(0, 6), turn_back(1, 7)]
         add_both(1, first)
         z_bf = host("z_bf0", [P, HALF * PACK], BF16, above=3072)[:]
         for block in range(2):
             fetch_z(backs[block], z_bf[:, block * P * PACK : (block + 1) * P * PACK])
-        add_both(1, gather(1, HALF, 1, HALF, terms[:, 1, :]))
+        round_w2(on_vector, w2_bf, 64, 128)
+        add_both(1, gather(1, HALF, 1, HALF, terms[:, 7 * P :]))
         add_both(3, h[3][:, HALF:T], (2,))
         nc.vector.quantize_mx(out=w2_codes[:].bitcast(FP8X4), scales=w2_sc[:], in_=w2_bf[:].rearrange("p t m j -> p (t m j)"))
-        terms = over("w2_raw1", "terms1c", [P, 5 * P], F32)
-        add_both(1, gather(1, HALF, 2, HALF, terms[:, :HALF]))
-        add_both(1, weigh(1, HALF, 3, p13[:, HALF:T], terms[:, HALF:T]))
-        add_across(2, 2, gather(2, 2 * P, 0, P, terms[:, T:]))
+        add_both(1, weigh(1, HALF, 2, spare, terms[:, :HALF]))
+        add_both(1, weigh(1, HALF, 3, p13b, terms[:, HALF:T]))
+        add_across(2, 2, gather(2, 2 * P, 0, P, terms[:, T : 5 * P]))
         z = quantise_z(0, z_bf)
         accs = second_layer(0, z, (0, 6))
         picks = under("zT0", "picked_late", [P, 2, HALF], F32)

from contextlib import ExitStack

import concourse.mybir as mybir
from concourse.masks import make_identity

K, T, D, H = 1024, 512, 4, 512
P = 128
PACK = 4
PASSES = K // (P * PACK)
TILES = H // P
LAST = TILES - 1
HALF = T // 2
BANK = 2048
LAP = 64
SPARE = 16
RUN = 16
CHUNKS = ((0, 256), (256, 128), (384, 128))

FLOPS = 2 * K * H * T + 2 * H * H * T

F32 = mybir.dt.float32
BF16 = mybir.dt.bfloat16
I32 = mybir.dt.int32
U32 = mybir.dt.uint32
U16 = mybir.dt.uint16
U8 = mybir.dt.uint8
FP8X4 = mybir.dt.float8_e4m3fn_x4
FP4X4 = mybir.dt.float4_e2m1fn_x4
ACT = mybir.ActivationFunctionType
ALU = mybir.AluOpType
BYTES_OF = {F32: 4, BF16: 2, U32: 4, U8: 1}


def tile_picked_wlapl_gelu_lo_kernel(tc, x_words, x_scales, w1, w2, gate, pos1, pos2, pos3, pos4, out_0, out_1, out_2):
    nc = tc.nc
    on_vector, on_scalar = nc.vector.tensor_copy, nc.scalar.copy
    with ExitStack() as ctx:
        keep = ctx.enter_context(tc.tile_pool(name="keep", bufs=1))
        rooms = ctx.enter_context(tc.tile_pool(name="rooms", bufs=1))
        psum = ctx.enter_context(tc.psum_pool(name="psum", bufs=1))
        span = {}

        def sb(name, shape, dtype):
            return keep.tile(shape, dtype, name=name, align_bytes=64)

        def size(shape, dtype):
            count = BYTES_OF[dtype]
            for n in shape[1:]:
                count = count * n
            return count

        def place(name, shape, dtype, at):
            span[name] = (at, at + size(shape, dtype))
            return rooms.tile(shape, dtype, name=name, offset=at, align_bytes=64)

        def host(name, shape, dtype, below=0, above=0):
            at = max([0] + [end for (start, end) in span.values()]) + below
            span[name + "_free"] = (at, at + size(shape, dtype) + above)
            return place(name, shape, dtype, at)

        def under(earlier, name, shape, dtype):
            return place(name, shape, dtype, span[earlier][0] + LAP - size(shape, dtype))

        def over(earlier, name, shape, dtype):
            return place(name, shape, dtype, span[earlier][1] - LAP)

        def inside(earlier, name, shape, dtype, skip=0):
            return place(name, shape, dtype, span[earlier][0] + 2 * LAP + skip)

        def bank(number, name, shape):
            return psum.tile(shape, F32, name=name, offset=number * BANK)

        lists = [keep.tile([P, T // 16], U16, name="list%d" % d) for d in range(D)]
        x_sc = sb("x_sc", [P, PASSES * T], U8)
        nc.gpsimd.memset(x_sc[:].bitcast(I32), 0)
        zero = sb("zero", [P, 1], F32)
        nc.gpsimd.memset(zero[:], 0.0)
        bias0 = host("bias0", [P, 32], F32, above=1024)

        w1_raw = {}

        def load_w1(t, g, below=0, above=0):
            raw = host("w1_raw%d_%d" % (t, g), [P, PACK, P], F32, below, above)
            rows = w1[g * P * PACK : (g + 1) * P * PACK, t * P : (t + 1) * P]
            nc.sync.dma_start(out=raw[:], in_=rows.rearrange("(p j) c -> p j c", j=PACK))
            w1_raw[t, g] = raw[:]

        def load_list(d):
            nc.sync.dma_start(out=lists[d][:], in_=(pos1, pos2, pos3, pos4)[d])

        gate_runs = sb("gate_runs", [P, RUN], F32)
        runs = gate.rearrange("d p (r m) -> (d p r) m", m=RUN)
        nc.sync.dma_start(out=gate_runs[:], in_=runs[0 : runs.shape[0] : P + 1])
        for g in range(PASSES):
            load_w1(0, g)
        x_sc_rows = x_sc[:].bitcast(I32).rearrange("p (g c) -> p g c", g=PASSES)
        for q in range(4):
            nc.sync.dma_start(
                out=x_sc_rows[32 * q : 32 * q + 4],
                in_=x_scales.bitcast(I32)[:, 4 * q : 4 * q + 4, :].rearrange("g r c -> r g c"),
            )
        x_w = [sb("x_w%d" % g, [P, 2 * T], U8) for g in range(PASSES)]
        for g in range(PASSES):
            nc.sync.dma_start(out=x_w[g][:].bitcast(I32), in_=x_words[g].bitcast(I32))
        nc.scalar.activation(out=bias0[:, :1], in_=zero[:], func=ACT.Gelu_apprx_tanh)
        load_w1(1, 0)
        load_list(0)
        load_list(3)
        load_w1(1, 1, 10240, 4096)
        load_list(1)
        load_list(2)
        load_w1(2, 0, 0, 1024)
        load_w1(2, 1, 2048, 4096)
        load_w1(3, 0)
        load_w1(3, 1, 0, 7168)
        w2_raw = []

        def load_w2(s, raw):
            nc.sync.dma_start(out=raw[:], in_=w2[:, s * H // 2 : (s + 1) * H // 2].rearrange("(p j) m -> p j m", j=PACK))
            w2_raw.append(raw)

        load_w2(0, host("w2_raw0", [P, PACK, H // 2], F32, above=1024))

        ident = sb("ident", [P, P], F32)
        make_identity(nc, ident[:])

        w1_codes = [sb("w1_codes0", [P, PASSES * P], U32)]
        for t in (1, 2):
            w1_codes.append(place("w1_codes%d" % t, [P, PASSES * P], U32, span["w1_raw%d_1" % (t + 1)][1] + 4 * HALF * (3 * t - 2) - 2 * LAP))
        w1_codes.append(host("w1_codes3", [P, PASSES * P], U32, above=4096))
        w1_sc = [host("w1_sc%d" % t, [P, PASSES * P], U8, above=1024 if t == LAST else 0) for t in range(TILES)]
        h = {}

        def interleave(copy, rounded, rows):
            copy(
                out=rounded.rearrange("p (c i j) -> p c j i", i=4, j=PACK),
                in_=rows.rearrange("p j (c i) -> p c j i", i=4),
            )
            return rounded

        def quantise_w1(t, first, piece):
            cols = slice(first, first + piece.shape[1] // PACK)
            nc.vector.quantize_mx(out=w1_codes[t][:, cols].bitcast(FP8X4), scales=w1_sc[t][:, cols], in_=piece)

        def parts(us):
            firsts = [sum(u.shape[1] for u in us[:s]) for s in range(len(us))]
            return [(first, u.shape[1], u) for first, u in zip(firsts, us)]

        def multiply(t, passes, us):
            for g in passes:
                for first, n, u in parts(us):
                    nc.tensor.matmul_mx(
                        out=u,
                        lhsT=w1_codes[t][:, g * P : (g + 1) * P].bitcast(FP8X4),
                        lhsT_scale=w1_sc[t][:, g * P : (g + 1) * P],
                        rhs=x_w[g][:, 2 * first : 2 * (first + n)].bitcast(FP4X4),
                        rhs_scale=x_sc[:, g * T + first : g * T + first + n],
                        start=(g == 0),
                        stop=(g == PASSES - 1),
                    )

        def make_h(t, us, tile, bias=0.0):
            h[t] = tile
            for first, n, u in parts(us):
                nc.scalar.activation(out=h[t][:, first : first + n], in_=u, func=ACT.Gelu_apprx_tanh, bias=bias)

        zT = {}
        home = {}
        across = {}
        total = {}
        added = {}

        def add(t, v0, summand):
            for at in range(0, summand.shape[1], P):
                block = (v0 + at) // P
                columns, blocks = home[t, block]
                mine = columns[:, (block - blocks[0]) * P : (block - blocks[0] + 1) * P]
                count = added[t, blocks]
                added[t, blocks] = count + 1
                last = count + 1 == total[t, blocks]
                nc.tensor.matmul(mine, lhsT=summand[:, at : at + P], rhs=ident[:], start=count == 0, stop=last, is_transpose=True)

        def sums_in(number, t, blocks, summands=D + 1):
            columns = bank(number, "sums%d_%d" % (t, blocks[0]), [P, len(blocks) * P])[:]
            added[t, blocks] = 0
            total[t, blocks] = summands * len(blocks)
            for block in blocks:
                home[t, block] = (columns, blocks)

        def sums_across(number, block, tiles, folded=0):
            columns = bank(number, "sums_of_block%d_%d" % (block, tiles[0]), [P, len(tiles) * P])[:]
            added[block, tiles, "across"] = 0
            total[block, tiles, "across"] = (D + 1) * len(tiles) - folded
            for t in tiles:
                across[t, block] = (columns, tiles)

        def add_across(t, block, summand):
            columns, tiles = across[t, block]
            mine = columns[:, (t - tiles[0]) * P : (t - tiles[0] + 1) * P]
            count = added[block, tiles, "across"]
            added[block, tiles, "across"] = count + 1
            last = count + 1 == total[block, tiles, "across"]
            nc.tensor.matmul(mine, lhsT=summand, rhs=ident[:], start=count == 0, stop=last, is_transpose=True)

        def round_across(t, block):
            columns, tiles = across[t, block]
            place_z = zT[block // 2][:, block % 2, :, 64 * tiles[0] : 64 * (tiles[-1] + 1)]
            nc.scalar.copy(
                out=place_z.rearrange("p u (q e) -> p u q e", e=2),
                in_=columns.rearrange("p (q u e) -> p u q e", u=2, e=2),
            )

        def add_own(t, v0, n):
            add(t, v0, h[t][:, v0 : v0 + n])

        def round_z(t, first, count):
            columns, blocks = home[t, first]
            sums = columns[:, (first - blocks[0]) * P : (first - blocks[0] + count) * P]
            place_z = zT[first // 2][:, first % 2 : first % 2 + count, :, 64 * t : 64 * (t + 1)]
            nc.scalar.copy(
                out=place_z.rearrange("p b u (q e) -> p b u q e", e=2),
                in_=sums.rearrange("p (b q u e) -> p b u q e", q=32, u=2, e=2),
            )

        def looked_up(t, v0, d, n):
            return h[t][:].indirect(lists[d][:, v0 // 16 : (v0 + n) // 16])

        def fresh(name, n, dtype=F32):
            return sb(name, [P, n], dtype)[:]

        def gather(t, v0, d, n, terms=None):
            if terms is None:
                terms = fresh("terms%d_%d_%d" % (t, d, v0), n)
            nc.vector.tensor_tensor(out=terms, in0=looked_up(t, v0, d, n), in1=neg_gate[:, d, v0 : v0 + n], op=ALU.mult)
            return terms

        def pick(t, v0, d, n, picked=None):
            if picked is None:
                picked = fresh("picked%d_%d_%d" % (t, d, v0), n)
            nc.scalar.activation(out=picked, in_=looked_up(t, v0, d, n), func=ACT.Copy)
            return picked

        def weigh(t, v0, d, picked, terms=None):
            n = picked.shape[1]
            if terms is None:
                terms = fresh("weighed%d_%d_%d" % (t, d, v0), n)
            nc.vector.tensor_tensor(out=terms, in0=picked, in1=neg_gate[:, d, v0 : v0 + n], op=ALU.mult)
            return terms

        def joined(name, first, second):
            both = fresh(name, first.shape[1])
            nc.vector.tensor_tensor(out=both, in0=first, in1=second, op=ALU.add)
            return both

        def with_own(t, v0, terms):
            return joined("with_own%d_%d" % (t, v0), terms, h[t][:, v0 : v0 + terms.shape[1]])

        def gather_add(t, v0, d, n, terms=None):
            add(t, v0, gather(t, v0, d, n, terms))

        def weigh_add(t, v0, d, picked, terms=None):
            add(t, v0, weigh(t, v0, d, picked, terms))

        def turn_back(block, number):
            words = zT[block // 2][:].bitcast(F32)
            back = bank(number, "back%d" % block, [P, 2, P])
            for u in range(2):
                nc.tensor.transpose(back[:, u, :], words[:, block % 2, u, :], ident[:])
            return back

        def fetch_z(back, z_bf):
            nc.scalar.copy(out=z_bf.bitcast(F32).rearrange("p (v u) -> p v u", u=2), in_=back[:].rearrange("p u v -> p v u"))

        w2_codes = sb("w2_codes", [P, H], U32)
        w2_sc = sb("w2_sc", [P, H], U8)
        y_codes = sb("y_codes", [P, T], U32)
        y_sc = sb("y_sc", [P, T], U8)
        out_rows = out_0.rearrange("(p t) v -> p t v", t=TILES)
        out_words = out_1[0].rearrange("p v r -> p (v r)").bitcast(I32)

        def round_w2(copy, w2_bf, first, end):
            raw = w2_raw[first // (P // 2)][:, :, TILES * first % HALF : TILES * first % HALF + TILES * (end - first)]
            copy(
                out=w2_bf[:, :, first:end, :].rearrange("p t m j -> p m j t"),
                in_=raw.rearrange("p j (m t) -> p m j t", t=TILES),
            )

        def quantise_z(c, z_bf):
            n = CHUNKS[c][1]
            z_codes = sb("z_codes%d" % c, [P, n], U32)
            z_sc = sb("z_sc%d" % c, [P, n], U8)
            nc.vector.quantize_mx(out=z_codes[:].bitcast(FP8X4), scales=z_sc[:], in_=z_bf)
            return z_codes, z_sc

        def second_layer(c, z, numbers):
            n = CHUNKS[c][1]
            accs = [bank(number, "acc%d_%d" % (c, number), [P, 2, n])[:] for number in numbers]
            for t in range(TILES):
                nc.tensor.matmul_mx(
                    out=accs[t // 2][:, t % 2, :],
                    lhsT=w2_codes[:, t * P : (t + 1) * P].bitcast(FP8X4),
                    lhsT_scale=w2_sc[:, t * P : (t + 1) * P],
                    rhs=z[0][:].bitcast(FP8X4),
                    rhs_scale=z[1][:],
                    start=True,
                    stop=True,
                )
            return accs

        y = [sb("y%d" % c, [P, TILES, n], F32) for c, (v0, n) in enumerate(CHUNKS)]

        def fetch_y(c, s, acc, copy, store):
            v0, n = CHUNKS[c]
            copy(out=y[c][:, 2 * s : 2 * s + 2, :], in_=acc)
            if store is not None:
                nc.sync.dma_start(out=out_rows[:, store, v0 : v0 + n], in_=y[c][:, store, :])

        def round_y(c):
            return interleave(on_vector, fresh("y_bf%d" % c, CHUNKS[c][1] * PACK, BF16), y[c][:])

        def quantise_y(c, y_bf):
            v0, n = CHUNKS[c]
            nc.vector.quantize_mx(out=y_codes[:, v0 : v0 + n].bitcast(FP8X4), scales=y_sc[:, v0 : v0 + n], in_=y_bf)

        def store_codes(v0):
            nc.sync.dma_start(out=out_words[:, v0 : v0 + HALF], in_=y_codes[:, v0 : v0 + HALF].bitcast(I32))

        neg_gate = sb("neg_gate", [P, D, T], F32)
        for s in range(RUN // 4):
            spread = bank(s, "spread%d" % s, [P, 4, P])
            for m in range(4):
                nc.tensor.transpose(spread[:, m, :], gate_runs[:, 4 * s + m : 4 * s + m + 1].to_broadcast([P, P]), ident[:])
            nc.scalar.mul(
                neg_gate[:].rearrange("p d (r m) -> p (d r) m", m=RUN)[:, :, 4 * s : 4 * s + 4],
                spread[:].rearrange("p m n -> p n m"),
                -1.0,
            )
        pieces = [fresh("w1_bf0_0", P * PACK, BF16), fresh("w1_bf0_1", P * PACK // 2, BF16), fresh("w1_bf0_2", P * PACK // 2, BF16)]
        interleave(on_vector, pieces[0], w1_raw[0, 0])
        quantise_w1(0, 0, pieces[0])
        for s in range(2):
            interleave(on_vector, pieces[1 + s], w1_raw[0, 1][:, :, s * P // 2 : (s + 1) * P // 2])
        quantise_w1(0, P, pieces[1])
        quantise_w1(0, P + P // 2, pieces[2])
        u0 = [bank(s, "u0_%d" % s, [P, n])[:] for s, n in enumerate((HALF, HALF))]
        multiply(0, range(PASSES), u0)
        h0 = sb("h0", [P, T + SPARE], F32)
        nc.gpsimd.memset(h0[:, T:], 0.0)
        make_h(0, u0, h0, bias0[:, :1])
        u1 = [bank(3, "u1", [P, T])[:]]
        quantise_w1(1, 0, interleave(on_vector, fresh("w1_bf1_0", P * PACK, BF16), w1_raw[1, 0]))
        multiply(1, (0,), u1)

        sums_in(4, 0, (0, 1, 2, 3))
        add_own(0, 0, T)
        p03 = pick(0, 0, 3, T)
        gather_add(0, 0, 0, HALF)
        rounded = interleave(on_vector, over("bias0", "w1_bf1_1", [P, P * PACK], BF16)[:], w1_raw[1, 1])
        terms = gather(0, 0, 1, HALF)
        quantise_w1(1, P, rounded)
        add(0, 0, terms)
        multiply(1, (1,), u1)
        w1_bf2 = under("w1_raw1_1", "w1_bf2", [P, K], BF16)[:]
        for g in range(PASSES):
            interleave(on_scalar, w1_bf2[:, g * K // 2 : (g + 1) * K // 2], w1_raw[2, g])
        quarter = pick(0, 0, 2, P, over("w1_raw2_0", "picked0_2a", [P, P], F32)[:])
        make_h(1, u1, under("w1_raw2_1", "h1", [P, T], F32))
        terms = over("w1_raw1_1", "terms0", [P, 2 * T], F32)
        weigh_add(0, 0, 3, p03, terms[:, :T])
        for d in range(2):
            gather_add(0, HALF, d, HALF, terms[:, T + d * HALF : T + (d + 1) * HALF])
        quantise_w1(2, 0, w1_bf2)
        u2 = [bank(0, "u2", [P, T])[:]]
        multiply(2, range(PASSES), u2)
        terms = inside("w1_raw2_1", "weighed0_2", [P, HALF], F32)
        gather_add(0, P, 2, P, terms[:, P:])
        weigh_add(0, 0, 2, quarter, terms[:, :P])

        p02 = pick(0, HALF, 2, HALF, over("w1_raw2_1", "picked0_2b", [P, HALF], F32)[:])
        early = {d: pick(1, 0, d, HALF) for d in (1, 2)}
        make_h(2, u2, sb("h2", [P, T], F32))
        sums_in(5, 1, (0, 1))
        gather_add(1, 0, 0, HALF)
        add_own(1, 0, HALF)
        w1_bf3 = under("w1_bf2", "w1_bf3", [P, K], BF16)[:]
        for g in range(PASSES):
            interleave(on_vector, w1_bf3[:, g * K // 2 : (g + 1) * K // 2], w1_raw[3, g])
        weigh_add(1, 0, 1, early[1])
        quantise_w1(3, 0, w1_bf3)
        u3 = [bank(1, "u3", [P, T])[:]]
        multiply(3, range(PASSES), u3)
        load_w2(1, over("w1_bf3", "w2_raw1", [P, PACK, H // 2], F32))
        p13 = over("w1_raw3_1", "picked1_3", [P, 4 * HALF], F32)
        weigh_add(0, HALF, 2, p02, p13[:, HALF:T])
        weigh_add(1, 0, 2, early[2], p13[:, T : T + HALF])
        pick(1, 0, 3, HALF, p13[:, :HALF])
        early = {(2, d): pick(2, 0, d, HALF) for d in (3, 2)}
        make_h(3, u3, sb("h3", [P, T], F32))
        p13b = pick(1, HALF, 3, HALF, over("w1_sc3", "picked1_3b", [P, HALF], F32)[:])
        early[3, 3] = pick(3, 0, 3, HALF, host("picked3_3", [P, HALF], F32, above=5120)[:])
        early[3, 2] = pick(3, 0, 2, HALF)

        sums_in(2, 2, (0, 1))
        gather_add(2, 0, 0, HALF, p13[:, 3 * HALF :])
        add_own(2, 0, HALF)
        weigh_add(1, 0, 3, p13[:, :HALF])
        gather_add(2, 0, 1, HALF)
        weigh_add(2, 0, 3, early[2, 3])
        w2_bf = over("w1_codes3", "w2_bf", [P, TILES, P, PACK], BF16)
        round_w2(on_vector, w2_bf, 0, 64)
        weigh_add(2, 0, 2, early[2, 2])
        zT[0] = under("w1_bf3", "zT0", [P, 2, 2, 2 * P], BF16)
        round_z(0, 0, 2)
        round_z(1, 0, 2)
        round_z(2, 0, 2)
        sums_in(3, 3, (0, 1))
        gather_add(3, 0, 0, HALF)
        add_own(3, 0, HALF)
        gather_add(3, 0, 1, HALF)
        weigh_add(3, 0, 3, early[3, 3])
        sums_across(1, 3, (3,))
        add_across(3, 3, h[3][:, 3 * P : T])
        weigh_add(3, 0, 2, early[3, 2], host("terms3_1", [P, HALF], F32, 2048, 1024)[:])
        zT[1] = under("terms3_1", "zT1", [P, 2, 2, 2 * P], BF16)
        spare = pick(1, HALF, 2, HALF, over("w2_raw0", "picked1_2b", [P, HALF], F32)[:])
        round_z(3, 0, 2)

        sums_across(5, 2, (1, 2))
        sums_across(3, 2, (3,))
        sums_across(2, 3, (1, 2))

        def add_both(t, terms, blocks=(2, 3)):
            for block in blocks:
                add_across(t, block, terms[:, (block - 2) * P : (block - 1) * P])

        late = {(2, 3): pick(2, HALF, 3, HALF, over("terms3_1", "picked2_3b", [P, HALF], F32)[:])}
        terms = over("picked3_3", "terms1b", [P, 9 * P], F32)
        for t in (1, 2):
            add_both(t, h[t][:, HALF:T])
        first = gather(1, HALF, 0, HALF, terms[:, 5 * P : 7 * P])
        backs = [turn_back(0, 6), turn_back(1, 7)]
        add_both(1, first)
        z_bf = host("z_bf0", [P, HALF * PACK], BF16, above=3072)[:]
        for block in range(2):
            fetch_z(backs[block], z_bf[:, block * P * PACK : (block + 1) * P * PACK])
        round_w2(on_vector, w2_bf, 64, 128)
        add_both(1, gather(1, HALF, 1, HALF, terms[:, 7 * P :]))
        add_both(3, h[3][:, HALF:T], (2,))
        nc.vector.quantize_mx(out=w2_codes[:].bitcast(FP8X4), scales=w2_sc[:], in_=w2_bf[:].rearrange("p t m j -> p (t m j)"))
        add_both(1, weigh(1, HALF, 2, spare, terms[:, :HALF]))
        add_both(1, weigh(1, HALF, 3, p13b, terms[:, HALF:T]))
        add_across(2, 2, gather(2, 2 * P, 0, P, terms[:, T : 5 * P]))
        z = quantise_z(0, z_bf)
        accs = second_layer(0, z, (0, 6))
        picks = under("zT0", "picked_late", [P, 2, HALF], F32)
        late[2, 2] = pick(2, HALF, 2, HALF, picks[:, 0, :])
        late[3, 3] = pick(3, HALF, 3, HALF, picks[:, 1, :])
        late[3, 2] = pick(3, HALF, 2, HALF, inside("zT0", "picked3_2b", [P, HALF], F32)[:])
        late[2, 1] = pick(2, 3 * P, 1, P, over("zT0", "picked2_1b", [P, P], F32)[:])
        add_across(3, 2, gather(3, 2 * P, 0, P, inside("zT0", "terms3_0", [P, P], F32, 4 * HALF)[:]))
        terms = over("z_bf0", "terms3b", [P, 4 * P], F32)
        weighed = {(2, 3): weigh(2, HALF, 3, late[2, 3], terms[:, :HALF])}
        add_both(2, weighed[2, 3], (2,))
        add_across(3, 2, gather(3, 2 * P, 1, P, terms[:, HALF : 3 * P]))
        add_across(2, 2, gather(2, 2 * P, 1, P, terms[:, 3 * P :]))
        for t, d in ((2, 2), (3, 3), (3, 2)):
            weighed[t, d] = weigh(t, HALF, d, late[t, d])
            add_both(t, weighed[t, d], (2,))
        terms = gather(2, 3 * P, 0, P, under("picked_late", "terms2_0b", [P, P], F32)[:])
        for d in (3, 2):
            add_both(2, weighed[2, d], (3,))
        last = inside("zT0", "terms_last", [P, 3, P], F32)
        add_across(2, 3, weigh(2, 3 * P, 1, late[2, 1], last[:, 2, :]))
        add_across(2, 3, terms)
        for d in (3, 2):
            add_both(3, weighed[3, d], (3,))
        round_z(0, 2, 2)
        for s in range(2):
            fetch_y(0, s, accs[s], on_scalar, slice(2 * s, 2 * s + 2))
        round_across(1, 2)
        round_across(3, 2)
        for d in range(2):
            add_across(3, 3, gather(3, 3 * P, d, P, last[:, d, :]))
        back = turn_back(2, 7)
        z_bf = [fresh("z_bf1", P * PACK, BF16), fresh("z_bf2", P * PACK, BF16)]
        round_across(1, 3)
        round_across(3, 3)
        fetch_z(back, z_bf[0])
        back = turn_back(3, 4)

        quantise_y(0, round_y(0))
        store_codes(0)
        accs = [second_layer(1, quantise_z(1, z_bf[0]), (3, 5))]
        fetch_z(back, z_bf[1])
        for s in range(2):
            fetch_y(1, s, accs[0][s], on_scalar, slice(2 * s, 2 * s + 2))
        accs.append(second_layer(2, quantise_z(2, z_bf[1]), (2, 1)))
        fetch_y(2, 0, accs[1][0], on_vector, None)
        fetch_y(2, 1, accs[1][1], on_scalar, slice(0, 4))
        y_bf = [round_y(1), round_y(2)]
        quantise_y(1, y_bf[0])
        quantise_y(2, y_bf[1])
        store_codes(HALF)
        for q in range(4):
            queue = nc.scalar if q % 2 else nc.sync
            queue.dma_start(
                out=out_2[0, 4 * q : 4 * q + 4, :].bitcast(I32),
                in_=y_sc[32 * q : 32 * q + 4, :].bitcast(I32),
            )
